import numpy as np, ml_dtypes
CORES = [16,17,18,19,32,33,34,35]
N = 8
BF = ml_dtypes.bfloat16
def f(rng, *shape):
    return (rng.standard_normal(shape, dtype=np.float32) * np.exp2(rng.integers(-2, 3, shape[:-1] + (1,)))).astype(BF)
def wide(rng, *shape):
    v = f(rng, *shape).astype(np.float32); k = shape[:-2] + (1, shape[-1])
    return (v * np.exp2(rng.integers(-6, 7, k)) * (rng.random(k) > 0.0625)).astype(BF)
M, K, TR, CAP = 4096, 32, 6, 128
D = 16 * K
def hashes(s, n):
    lo = ((s & 4095) + 1597 * n) & 4095; b = ((s >> 12) + ((lo * lo) >> 6)) & 4095
    return (lo + ((b * b) >> 6)) & 4095, b
def seed_of(a, b, n):
    lo = (a - ((b * b) >> 6)) & 4095
    return ((b - ((lo * lo) >> 6)) & 4095) * 4096 + ((lo - 1597 * n) & 4095)
def owners(t, s):
    a, b = hashes(np.asarray(s, np.int64)[..., None], (TR + 1) * np.arange(K)); w = (a * N) >> 12
    return np.where(b < t[w], w, t[N + w]).astype(np.int64)
def loads(t, s):
    o = owners(t, s); return np.stack([np.sum(o == q, -1) for q in range(N)], -1)
def sixteen(rng, t, keep=()):
    m = 16 - len(keep); kept = np.array(keep, np.int64); base = np.sum(loads(t, kept), 0)
    pool = rng.integers(0, 1 << 24, 1024); c = loads(t, pool); ok = np.flatnonzero(np.all(c * m <= CAP - base, 1)); j = np.arange(m)
    for u in range(m):
        if np.all(np.sum(c[j], 0) + base <= CAP): break
        j[u] = rng.choice(ok)
    return rng.permutation(np.concatenate([pool[j], kept]))
def ranks(rng, least):
    return np.concatenate([rng.integers(least, 4097, N), rng.permutation(N)]).astype(np.int64)
def absent(rng):
    w = rng.permutation(N); t = np.zeros(2 * N, np.int64)
    t[w] = (8192 * np.arange(N) + N - 1) // (2 * (N - 1)); t[N + w] = np.roll(w, -1); return t
def history(rng, dens):
    w = np.zeros((N, 128, M), np.float32)
    for q in range(N):
        for r in range(N):
            w[q] += np.float32(2 ** r) * (rng.random((128, M), dtype=np.float32) < dens[r][:, None])
    return w.astype(BF)
def seeds(rng, rk):
    return np.stack([np.stack([sixteen(rng, rk[g]) for g in range(8)]) for r in range(N)])
def complete(rng, rk, sd, dens=None):
    if dens is None: dens = rng.choice(np.array([0.1, 0.5, 0.9]), (N, 128))
    return {"sd": np.reshape(sd, (N, 128, 1)).astype(np.int32), "rk": np.stack([rk] * N).astype(np.int32), "thr": rng.integers(0, 4097, (N, 8, M)).astype(np.int32),
            "ali": rng.integers(0, M, (N, 8, M)).astype(np.int32), "seen": history(rng, dens), "vec": f(rng, N, 128, M)}
def setup_inputs(rng):
    rk = np.stack([ranks(rng, 2800) for g in range(8)]); return complete(rng, rk, seeds(rng, rk))
def setup_inputs_full(rng):
    o0 = rng.integers(0, N); rk = []
    for g in range(8):
        o = (o0 + g) % N; t = np.concatenate([rng.integers(3604 - 40, 3604 + 41, N), np.full(N, o)]).astype(np.int64); t[o] = 4096; rk.append(t)
    rk = np.stack(rk); sd = seeds(rng, rk); C = CAP // 16
    far = rng.integers(0, N, 8); h = rng.permutation(8); far[h[0]] = 0; far[h[1]] = rng.integers(1, N)
    for g in range(8):
        o = (o0 + g) % N; r = (o + far[g]) % N
        pool = rng.integers(0, 1 << 24, 4096); c = loads(rk[g], pool); fine = np.all(np.delete(c, o, 1) <= C, 1); s = []
        for i in range(8):
            x = rng.integers(-2, 3)
            for v in (C + x, C - x): s.append(pool[rng.choice(np.flatnonzero(fine & (c[:, o] == v)))])
        sd[r, g] = rng.permutation(np.array(s))
    return complete(rng, rk, sd)
def setup_inputs_edges(rng):
    rk, tie = [], []
    for g in range(8):
        t = ranks(rng, 3500); w = rng.permutation(N)[:4]; t[w[0]] = 0; t[N + w[0]] = w[1]; t[w[1]] = 0; t[N + w[1]] = w[0]; t[w[2]] = rng.integers(3500, 4096); t[N + w[2]] = w[0]; t[w[3]] = 4096; rk.append(t)
        tie.append(seed_of(int(w[2]) * (4096 // N) + int(rng.integers(0, 4096 // N)), int(t[w[2]]), (TR + 1) * int(rng.integers(0, K))))
    rk = np.stack(rk); sd = np.stack([np.stack([sixteen(rng, rk[g], (0, (1 << 24) - 1, tie[g])) for g in range(8)]) for r in range(N)])
    d = complete(rng, rk, sd); z = rng.integers(0, 4, (N, 8, M)); thr = np.where(z == 0, 0, np.where(z == 1, 4096, d["thr"])); z = rng.integers(0, 4, (N, 8, M))
    ali = np.where(z == 0, 0, np.where(z == 1, M - 1, np.where(z == 2, np.arange(M), d["ali"])))
    for r in range(N):
        for g in range(8):
            q = owners(rk[g], sd[r, g])[:, ::4]; a, b = hashes(sd[r, g][:, None], ((TR + 1) * np.arange(K) + 1)[None, ::4]); e = (a * M) >> 12
            thr[q, g, e] = b; ali[q, g, e] = M - 1 - e
    d["thr"] = thr.astype(np.int32); d["ali"] = ali.astype(np.int32); return d
def setup_inputs_hot(rng):
    rk = np.stack([ranks(rng, 2800) for g in range(8)]); sd = seeds(rng, rk)
    for g in range(8):
        pool = rng.integers(0, 1 << 24, 1024); sd[rng.integers(0, N), g] = pool[rng.choice(np.flatnonzero(np.all(loads(rk[g], pool) <= CAP // 16, 1)))]
    d = complete(rng, rk, sd); h = rng.integers(0, M, (N, 8, 1)); h[:, 0] = 0; h[:, 7] = M - 1
    d["thr"] = rng.integers(0, 512, (N, 8, M)).astype(np.int32); d["ali"] = (h + np.zeros((1, 1, M), np.int64)).astype(np.int32); return d
def setup_inputs_avid(rng):
    rk = np.stack([absent(rng) for g in range(8)]); dens = rng.choice(np.array([0, 0.97, 1.0]), (N, 128)); dens[rng.integers(0, N)] = 1
    return complete(rng, rk, seeds(rng, rk), dens)
def setup_inputs_spread(rng):
    d = setup_inputs(rng); d["vec"] = wide(rng, N, 128, M); d["thr"] = (4096 >> rng.integers(0, 14, (N, 8, M))).astype(np.int32); return d
def check_inputs(d):
    bad = []
    try:
        sd, rk = d["sd"].astype(np.int64), d["rk"].astype(np.int64); w = d["seen"].astype(np.float32)
        if not ((sd >= 0) & (sd < 1 << 24)).all(): bad.append("seed")
        if not (rk == rk[:1]).all(): bad.append("rk alike on all ranks")
        if not ((rk[..., :N] >= 0) & (rk[..., :N] <= 4096) & (rk[..., N:] >= 0) & (rk[..., N:] < N)).all(): bad.append("rk")
        if not ((d["thr"] >= 0) & (d["thr"] <= 4096)).all(): bad.append("thr")
        if not ((d["ali"] >= 0) & (d["ali"] < M)).all(): bad.append("ali")
        if not ((w >= 0) & (w < 2 ** N) & (w == np.floor(w))).all(): bad.append("seen")
        if not np.isfinite(d["vec"].astype(np.float32)).all(): bad.append("finite")
        if not bad and any((np.sum(loads(rk[r, g], sd[r, 16 * g:16 * g + 16, 0]), 0) > CAP).any() for r in range(N) for g in range(8)): bad.append("cap")
    except Exception:
        bad.append("unreadable")
    return bad
def reference(sd, rk, thr, ali, seen, vec):
    chosen = np.zeros((N, 128, K), np.float32); y = np.zeros((N, 128, D), vec.dtype); n = (TR + 1) * np.arange(K); row = np.arange(16)[:, None]
    for r in range(N):
        for g in range(8):
            s = sd[r, 16 * g:16 * g + 16].astype(np.int64)
            q = owners(rk[r, g].astype(np.int64), s[:, 0])
            x = np.zeros((16, K), np.int64); done = np.zeros((16, K), bool)
            for i in range(1, TR + 1):
                a, b = hashes(s, n + i); e = (a * M) >> 12
                c = np.where(b < thr[q, g, e], e, ali[q, g, e]).astype(np.int64)
                known = (seen[q, 16 * g + row, c].astype(np.float32).astype(np.int64) >> r) & 1
                x = np.where(done, x, c); done = done | (known == 0)
            chosen[r, 16 * g:16 * g + 16] = q * M + x
            y[r, 16 * g:16 * g + 16] = vec[q.T.reshape(-1), 16 * g + row, x.T.reshape(-1)]
    return {"chosen": chosen, "y": y}

@@ -1,0 +1,526 @@
+from concourse.bass import DstId, RemoteDMATransfer
+from concourse.mybir import AluOpType as A_, ActivationFunctionType as AF
+
+N = 8
+TRY = 6
+RW = 144
+BIG = float(1 << 23)
+OPS = {"+": A_.add, "-": A_.subtract, "*": A_.mult, "min": A_.min, "max": A_.max, ">=": A_.is_ge, ">": A_.is_gt, "<": A_.is_lt,
+       "==": A_.is_equal, ">>": A_.arith_shift_right, "&": A_.bitwise_and}
+
+SMALL = {
+    "bufI": ("int32", 8, "ckN 32 pI 8 p16I 8 sdI 8 hI 8 lh 8 ckp 8 ckA 8 rkI 16 oT 32 oL 32 oL2 32 oSq 32 oB0 32 oB 32 oSr 32 oA0 32 oA 32 "
+             "oW 32 oB16 32 oP 32 oM 32 own 32 yI 256 v1 32 v 32 thrI 256 aliI 256 xl 64 xh 64 hT 384 hL 384 "
+             "hb 384 hB 384 ha 384 hA 384 pk 384 xI 384 cI 384 wI 320 sI 320 acc 320 a6 64 aA 64 r 64 wL 64 sL 64 q1 32 "
+             "q16 32 ps 32 mm 32 cq 32 cl 32 bl 32 b8I 32 mb 32"),
+    "bufF": ("float32", 8, "ones 128 p16F 8 n16 8 e8a 128 e8 128 g9a 16 g9 16 w2 8 w5 8 w6 8 wcol 8 c3 8 wS 8 lhF 8 ckF 8 "
+             "ya 8 yc 16 dy 8 dyS 8 sF 8 hF 8 st 256 mqF 256 be 32 beR 32 b8 128 b4 64 "
+             "b2 64 xlF 64 H6 64 hL2 384 ha2 8 nm 8 nm0 8 mT 1024 q4k 32 ch1 32"),
+    "bufB": ("bfloat16", 16, "onesB 128 ones5 512 lta 128 lt 128 selB 144 selT 144 selP 144 selX 128 ckL 128 "
+             "idn 128 up8 128 dn8 128 wI0 128 wI1 128 wU 128 wD 128 iH 64 iL 64 oh8 16 q8 16 "
+             "iotaS 128 ohI 512 ohA 512 oh 512 kE 512 inX 512 rs 256 rsw 256 mq 256 sc 256 "
+             "alH 256 alL 256 thH 256 thL 256 win 1024 mask 1024 m2 512 cm 512 ysb 512"),
+    "bufU": ("uint16", 16, "a16 32 e16 384 c16 320 f16 64 l16 96"),
+}
+SCRATCH = {}
+TILES = {}
+for _buf, (_type, _step, _list) in SMALL.items():
+    _at, _w = 0, _list.split()
+    for _n, _c in zip(_w[0::2], _w[1::2]):
+        TILES[_n] = (_buf, _at, int(_c))
+        _at += -(-int(_c) // _step) * _step
+    SCRATCH[_buf] = ("sbuf", [128, _at], _type)
+for _n, _c, _type in (("seenB", 4096, "bfloat16"), ("vecB", 4096, "bfloat16"), ("tabs", 4096, "bfloat16"),
+                      ("tg", 6144, "bfloat16"), ("sg", 5120, "bfloat16"), ("su", 1024, "bfloat16"), ("rspR", N * RW, "bfloat16")):
+    SCRATCH[_n] = ("sbuf", [128, _c], _type)
+    TILES[_n] = (_n, 0, _c)
+for _j in range(8):
+    SCRATCH["p%d" % _j] = ("psum", [128, 512], "float32")
+    TILES["p%d" % _j] = ("p%d" % _j, 0, 512)
+BLOCKS = {"rsp": RW, "rq": 8, "rr": 8}
+for _n, _c in BLOCKS.items():
+    SCRATCH[_n] = ("sbuf", [128, N, _c], "bfloat16" if _n == "rsp" else "int32")
+SEMAPHORES = ("sv ss sp sg d_sd d_rk d_thr d_ali d_seen d_vec d_tab0 d_tab1 d_tab2 d_tab3 d_y d_ch "
+              "l_be l_rq l_rsp r_be r_rq r_rsp").split()
+
+
+def engine_plan(core, T, topo):
+    off = [c for c in T.cores if topo.chip(c) != topo.chip(core)]
+    on = [c for c in T.cores if topo.chip(c) == topo.chip(core) and c != core]
+    plan = {}
+    pool = topo.engines(core, off[0])
+    rest = [e for e in topo.engines(core, on[0]) if e not in pool]
+    for cores, engines in ((off, pool), (on, rest)):
+        n = 1
+        while 2 * n * len(cores) <= len(engines):
+            n *= 2
+        at = 0
+        for j, c in enumerate(cores):
+            m = n
+            if len(engines) - at - 2 * n >= n * (len(cores) - j - 1):
+                m = 2 * n
+            plan[c] = engines[at:at + m]
+            at += m
+    return plan, off, on
+
+
+def rank_program(g, core, T, topo):
+    me = T.rank_of(core)
+    if me is None:
+        return
+    queues = {"V": (g.vector, "sv"), "S": (g.scalar, "ss"), "P": (g.tensor, "sp"), "G": (g, "sg"), "Y": (g.sync, None)}
+    V, S, P, Y = g.vector, g.scalar, g.tensor, g.sync
+    count, waited, past = {}, {q: {} for q in queues}, {}
+
+    def X(spec):
+        if not isinstance(spec, str):
+            return spec
+        if "@" in spec:
+            w, o = spec.split("@")
+            (wa, wr), (oa, orr) = X(w), X(o)
+            return wa.indirect(oa), wr + orr
+        rows, name = (8, spec[2:]) if spec[:2] == "8|" else (128, spec)
+        f = name.split(":")
+        buf, at, n = TILES[f[0]]
+        a, b, st = (int(f[1]), int(f[2]), int(f[3]) if len(f) > 3 else 1) if len(f) > 1 else (0, n, 1)
+        return T[buf][0:rows, at + a:at + b:st], [(buf, at + a, at + b, st)]
+
+    def meet(p, o, own):
+        if p[0][0] == "p" and not own:
+            return True
+        if p[1] >= o[2] or o[1] >= p[2]:
+            return False
+        return (p[3] == 1 and o[3] == 1) or bool(set(range(p[1], p[2], p[3])) & set(range(o[1], o[2], o[3])))
+
+    def need(q, reads, writes, part=None):
+        tok, mine = {}, queues[q][1]
+        for places, wr in ((reads, False), (writes, True)):
+            for p in places:
+                for o, t, is_w, pt in past.get(p[0], []):
+                    if (is_w or wr or (p[0][0] == "p" and t[0] != mine)) and tok.get(t[0], 0) < t[1] \
+                            and meet(p, o, t[0] == mine) and (pt is None or part is None or pt == part):
+                        tok[t[0]] = t[1]
+        for s in sorted(tok):
+            if waited[q].get(s, 0) < tok[s]:
+                queues[q][0].wait_ge(T.sem[s], tok[s])
+                waited[q][s] = tok[s]
+
+    def note(tok, reads, writes, part=None):
+        for places, w in ((reads, False), (writes, True)):
+            for p in places:
+                past.setdefault(p[0], []).append((p, tok, w, part))
+
+    def run(q, call, out, ins, *more):
+        oa, ow = X(out)
+        reads, args = [], []
+        for i in ins:
+            if isinstance(i, (str, tuple)):
+                a, r = X(i)
+                args.append(a)
+                reads = reads + r
+            else:
+                args.append(i)
+        need(q, reads, ow)
+        s = queues[q][1]
+        count[s] = count.get(s, 0) + 1
+        call(oa, *args, *more).then_inc(T.sem[s], 1)
+        note((s, count[s]), reads, ow)
+
+    def ts(out, a, op, s1, op2=None, s2=None):
+        run("V", V.tensor_scalar, out, [a, s1, s2], *([OPS[op]] if op2 is None else [OPS[op], OPS[op2]]))
+
+    def tt(out, a, op, b):
+        run("V", V.tensor_tensor, out, [a, b], OPS[op])
+
+    def cp(out, a):
+        run("V", V.tensor_copy, out, [a])
+
+    def fill(out, c):
+        run("V", V.memset, out, [], c)
+
+    def scan(out, a, b):
+        run("V", V.tensor_tensor_scan, out, [a, b], 0.0, A_.mult, A_.add)
+
+    idle = []
+
+    def gap(k=1):
+        for _ in range(k):
+            if idle:
+                c = idle.pop(0)
+                c[0](*c[1:])
+
+    def weave(*chains):
+        for j in range(max(len(c) for c in chains)):
+            for c in chains:
+                if j < len(c) and c[j]:
+                    c[j][0](*c[j][1:])
+
+    def act(out, a, bias=0.0, scale=1.0, func=AF.Copy):
+        run("S", lambda o, i: S.activation(o, i, func, bias=bias, scale=scale), out, [a])
+
+    def scaled(out, a, by):
+        run("S", lambda o, i, c: S.activation(o, i, AF.Copy, scale=c), out, [a, by])
+
+    def iota(out, pattern, base, cm, exact=False):
+        run("G", lambda o: g.iota(o, pattern, base, cm) if exact else
+            g.iota(o, pattern, base, cm, allow_small_or_imprecise_dtypes=True), out, [])
+
+    def keep(out, a, pattern, op, base, cm):
+        run("G", lambda o, i: g.affine_select(o, i, pattern, OPS[op], 0.0, base, cm), out, [a])
+
+    def mms(out, pairs):
+        def call(o, *args):
+            for j in range(0, len(args), 2):
+                last = P.matmul(o, args[j], args[j + 1], j == 0, j == len(args) - 2)
+            return last
+        run("P", call, out, [x for p in pairs for x in p])
+
+    def dma(q, out, in_, sem, part=None):
+        (oa, ow), (ia, ir) = X(out), X(in_)
+        need(q, ir, ow, part)
+        queues[q][0].dma_start(oa, ia).then_inc(T.sem[sem], 16)
+        count[sem] = count.get(sem, 0) + 16
+        note((sem, count[sem]), ir, ow, part)
+
+    plan, off, on = engine_plan(core, T, topo)
+
+    def send(sem, src, dst, local, cores=None):
+        tr = []
+        for c in cores or off + on:
+            rid, pnc, _s = topo.addr(c)
+            a, r = X(src(T.rank_of(c)))
+            need("G", r, [])
+            m = 0
+            for e in plan[c]:
+                m |= 1 << e
+            tr.append(RemoteDMATransfer(dst_ids=[DstId(rid=rid, pnc=pnc)], dma_engine_mask=m, remote_sem=T.sem[sem],
+                                        srcs=[a], dsts=[X(dst)[0]], alu_op=0))
+            count[local] = count.get(local, 0) + len(plan[c])
+        g.remote_dma_fused(tr, local_sem=T.sem[local])
+
+    def block(name, r, a=0, b=None):
+        w = BLOCKS[name]
+        b = w if b is None else b
+        return T[name][:, r, a:b], [(name, w * r + a, w * r + b, 1)]
+
+    def parts(name, a, b):
+        w = BLOCKS[name]
+        return T[name][:, :, a:b], [(name, w * r + a, w * r + b, 1) for r in range(N)]
+
+    def landing(piece, sem):
+        count[sem] = sum(len(engine_plan(c, T, topo)[0][core]) for c in T.cores if c != core)
+        for r in range(N):
+            if r != me:
+                note((sem, count[sem]), [], X(piece(r))[1])
+
+    def ext(t):
+        return (t[:], [])
+
+    def at(name, w, i):
+        return "%s:%d:%d" % (name, w * i, w * i + w)
+
+    landing(lambda r: at("beR", 4, r), "r_be")
+    landing(lambda r: block("rr", r), "r_rq")
+    landing(lambda r: at("rspR", RW, r), "r_rsp")
+
+    dma("Y", "sdI:0:1", ext(T.sd), "d_sd")
+    dma("S", "8|rkI", ext(T.rk), "d_rk")
+    dma("Y", "thrI", ext(T.thr), "d_thr")
+    dma("Y", "aliI", ext(T.ali), "d_ali")
+    dma("Y", "seenB", ext(T.seen), "d_seen")
+
+    for name, c in (("ones", 1.0), ("win", 0.0), ("onesB", 1.0), ("ones5", 1.0), ("selB", 0.0), ("selX", 0.0), ("ckL", 0.0),
+                    ("yc", 0.0), ("be", 0.0), ("rs", 1.0)):
+        fill(name, c)
+    step = 1597 * (TRY + 1)
+    iota("ckN", [[step, 32]], -int(BIG), 0, True)
+    iota("pI:0:1", [[0, 1]], 0, 1, True)
+    iota("ckp:0:1", [[0, 1]], 0, step, True)
+    iota("q8:0:8", [[1, 8]], 0, 0)
+    keep("8|e8a", "8|ones", [[1, 128]], ">=", 0, -16)
+    keep("8|e8", "8|e8a", [[-1, 128]], ">=", 15, 16)
+    keep("g9a:0:9", "ones:0:9", [[-16, 9]], ">=", 0, 1)
+    keep("g9:0:9", "g9a:0:9", [[16, 9]], ">=", 15, -1)
+    iota("ohI", [[0, 32], [1, 16]], 0, 0)
+    keep("lta", "onesB", [[16, 8], [1, 16]], ">", 0, -1)
+    keep("lt", "lta", [[-16, 8], [0, 16]], ">=", 0, 1)
+    keep("kE", "ones5", [[1, 32], [0, 16]], "==", 0, -1)
+    iota("iotaS", [[1, 128]], 0, 0)
+    ts("p16I:0:1", "pI:0:1", "&", 15)
+    fill("rs:0:256:32", 0.0)
+    cp("p16F:0:1", "p16I:0:1")
+    ts("n16:0:1", "p16F:0:1", "*", -1.0)
+    act("tabs:0:1024", "win")
+    act("tabs:1024:2048", "win")
+
+    idle += [(fill, "rsw", 1.0), (ts, "ckA:0:1", "ckp:0:1", "&", 3840), (ts, "ckA:1:2", "ckp:0:1", "&", 255), (fill, "rsw:0:256:8", 0.0),
+             (cp, "ckF:0:2", "ckA:0:2"), (ts, "c3:0:1", "p16F:0:1", ">=", 4.0, "*", 8192.0),
+             (ts, "ckL:2:128:16", "onesB:0:8", "*", "ckF:0:1"), (ts, "ckL:3:128:16", "onesB:0:8", "*", "ckF:1:2"),
+             (ts, "w2:0:1", "p16F:0:1", ">=", 2.0, "*", 8192.0),
+             (ts, "wS:0:1", "c3:0:1", "max", 1.0), (ts, "wcol:0:1", "w2:0:1", "max", 1.0),
+             (ts, "w6:0:1", "p16F:0:1", "<", 8.0), (ts, "w5:0:1", "p16F:0:1", ">=", 8.0),
+             (tt, "oh8:0:8", "oh:0:8", "+", "oh:8:16")]
+    cp("sF:0:1", "sdI:0:1")
+    ts("hI:0:1", "sdI:0:1", ">>", 12)
+    ts("8|ya", "8|rkI:0:8", "*", 16.0)
+    ts("oT", "ckN", "+", "sF:0:1")
+    ts("hF:0:1", "hI:0:1", "*", 64.0, "+", -BIG)
+    tt("8|yc:1:9", "8|ya", "+", "8|rkI:8:16")
+    ts("oL", "oT", "&", 4095)
+    ts("lh:0:1", "sdI:0:1", "&", 3840)
+    tt("8|dy", "8|yc:1:9", "-", "8|yc:0:8")
+    tt("oSq", "oL", "*", "oL")
+    ts("lh:1:2", "sdI:0:1", "&", 255)
+    ts("oL2", "oL", "*", 64.0, "+", -BIG)
+    ts("oB0", "oSq", "+", "hF:0:1")
+    mms("p3:0:8", [("8|e8", "8|dy")])
+    act("dyS", "p3:0:8")
+    ts("lh:2:3", "hI:0:1", "&", 255)
+    ts("lh:3:4", "hI:0:1", "&", 3840)
+    ts("oB", "oB0", ">>", 6, "&", 4095)
+    cp("lhF:0:3", "lh:0:3")
+    run("S", lambda o, i, b: S.activation(o, i, AF.Abs, bias=b), "ohA", ["ohI", "n16:0:1"])
+    act("oh", "ohA", 1.0, -1.0, AF.Relu)
+    act("selB:15:144:16", "g9:0:9")
+    tt("oSr", "oB", "*", "oB")
+    ts("lhF:3:4", "lh:3:4", "+", -2048.0)
+    for j, c in ((0, "lhF:0:1"), (1, "lhF:1:2"), (4, "lhF:3:4"), (5, "lhF:2:3")):
+        scaled("selX:%d:128:16" % j, "g9:0:8", c)
+    tt("oA0", "oSr", "+", "oL2")
+    ts("oB16", "oB", "*", 16.0, "+", 8.0)
+    gap()
+    ts("oA", "oA0", ">>", 6, "&", 4095)
+    gap(2)
+    for w in range(N):
+        ts("st:%d:256:8" % w, "oA", ">=", 512.0 * w, "*", at("dyS", 1, w))
+    ts("oW", "oA", ">>", 9)
+    gap()
+    scan("yI", "rsw", "st")
+    tt("oP", "oB16", "+", "oW")
+    gap()
+    tt("oM", "yI:7:256:8", "min", "oP")
+    gap(2)
+    ts("own", "oM", "&", 7)
+    gap(2)
+    for q in range(N):
+        ts(at("mq", 32, q), "own", "==", float(q))
+    gap(2)
+    scan("sc", "rs", "mq")
+    mms("p2:0:8", [("onesB", "q8:0:8"), ("lt", "sc:31:256:32")])
+    mms("p7", [("selX", "oh"), ("ckL", "kE")])
+    act("be:1:32:4", "sc:31:256:32")
+    cp("mqF", "mq")
+    gap()
+    tt("mqF:0:256:32", "mq:0:256:32", "+", "p2:0:8")
+    act("be:0:32:4", "p2:0:8")
+    act("inX", "p7")
+    gap()
+    scan("p1:0:256", "rs", "mqF")
+    gap()
+    tt("p0:0:128", "p1:0:128", "*", "mq:0:128")
+    tt("b8", "p1:128:256", "*", "mq:128:256")
+    gap()
+    tt("p0:128:192", "p0:0:64", "+", "b8:0:64")
+    tt("b4", "p0:64:128", "+", "b8:64:128")
+    gap()
+    tt("b2", "p0:128:192", "+", "b4")
+    gap()
+    tt("v1", "b2:0:32", "+", "b2:32:64")
+    gap()
+    ts("a16", "v1", "-", 1.0)
+    send("r_be", lambda q: at("be", 4, q), at("beR", 4, me), "l_be")
+    scaled("selP", "selB", "wS:0:1")
+    act("tabs:2048:4096", "tabs:0:2048")
+    cp("win@a16", "inX")
+    mms("p4:0:64", [("selP:%d:%d" % (15 - b, 143 - b), "win:%d:1024:16" % b) for b in range(16)])
+
+    cp("p5:0:256", "aliI")
+    act("alH", "p5:0:256", -8.0, 1.0, AF.Relu)
+    ts("p6:0:256", "thrI", "+", -2048.0)
+    act("thH", "p6:0:256", -4.0)
+    cp(at("beR", 4, me), at("be", 4, me))
+    cp(parts("rq", 0, 8), "p4:0:64")
+    send("r_rq", lambda q: block("rq", q), block("rr", me), "l_rq")
+    tt("alL", "p5:0:256", "-", "alH")
+    tt("thL", "p6:0:256", "-", "thH")
+    for j, name in ((1, "alH"), (3, "thH"), (0, "alL"), (2, "thL")):
+        dma("Y", (T.tabs[j:128:16, :], X("tabs")[1]), name, "d_tab%d" % j, j)
+    Y.wait_ge(T.sem["l_rq"], count["l_rq"])
+    dma("Y", "vecB", ext(T.vec), "d_vec")
+
+    ts("nm0", "beR:1:32:4", "*", -0.5, "+", 0.5 + float(128 * me))
+    ts("ha2", "beR:1:32:4", "*", 0.5, "+", -0.25)
+    tt("nm", "nm0", "-", "beR:0:32:4")
+    for r in range(N):
+        run("S", lambda o, i, b: S.activation(o, i, AF.Abs, bias=b), at("mT", 128, r), ["iotaS", at("nm", 1, r)])
+    gap(len(idle))
+    scaled("selT", "selB", "wcol:0:1")
+    cp(block("rr", me), block("rq", me))
+    for r in range(N):
+        ts(at("mask", 128, r), at("mT", 128, r), "<", at("ha2", 1, r), "*", float(2 ** (15 - r)))
+    keep("idn", "onesB", [[-1, 128]], "==", 0, 1)
+    keep("up8", "onesB", [[-1, 128]], "==", 8, 1)
+    keep("dn8", "onesB", [[-1, 128]], "==", -8, 1)
+
+    def R(name, i, n=1):
+        return "%s:%d:%d" % (name, 64 * i, 64 * i + 64 * n)
+
+    def counter(i):
+        return float(1597 * (i + 1) % 4096)
+
+    def hashes(i0, n):
+        def r(tile):
+            return R(tile, i0, n)
+        each = range(i0, i0 + n)
+        return ([(ts, R("hT", i), "xl", "+", counter(i)) for i in each] +
+                [(ts, r("hL"), r("hT"), "&", 4095), (tt, r("p0"), r("hL"), "*", r("hL"))] +
+                [(tt, R("hb", i), R("p0", i), "+", "H6") for i in each] +
+                [(ts, r("hB"), r("hb"), ">>", 6, "&", 4095), (tt, r("p1"), r("hB"), "*", r("hB")),
+                 (tt, r("ha"), r("p1"), "+", r("hL2")), (ts, r("hA"), r("ha"), ">>", 6, "&", 4095), (cp, r("e16"), r("hA")),
+                 (ts, r("p0"), r("hB"), "*", 8192.0, "+", 4096.0 - 16777216.0), (tt, r("pk"), r("p0"), "+", r("hA"))])
+
+    def wrap(out, sel, src, a, n):
+        mms(out + ":0:%d" % (n // 16), [("%s:%d:%d" % (sel, 15 - b, 143 - b), "%s:%d:%d:16" % (src, a + b, a + n)) for b in range(16)])
+
+    def bank(i):
+        return ("p2", "p5")[i % 2]
+
+    def sbank(i):
+        return ("p3", "p4")[i % 2]
+
+    def table(i):
+        wrap(bank(i), "selT", "tg", 1024 * i, 1024)
+
+    def look(i):
+        act(at("tg", 1024, i), "tabs@" + R("e16", i))
+
+    def seen(i):
+        tt(at("sg", 1024, i), "seenB@" + R("c16", i), "*", "mask")
+        wrap(sbank(i), "selB", "sg", 1024 * i, 1024)
+
+    def item(i):
+        ops = [(tt, R("xI", i), bank(i) + ":0:64", "min", R("pk", i)), (ts, R("cI", i), R("xI", i), "&", 4095)]
+        if i < TRY - 1:
+            ops.append((cp, R("c16", i), R("cI", i)))
+            ops.append((ts, R("p1", i), R("cI", i), "+", 4096.0 * (TRY - 1 - i)))
+        return ops
+
+    def known(j):
+        return [(cp, R("wI", j), sbank(j) + ":0:64"), (ts, R("sI", j), R("wI", j), "&", 1 << 15)]
+
+    def go(j):
+        if j == 0:
+            return [(tt, R("acc", 0), R("p1", 0), "-", R("sI", 0))]
+        return [(tt, R("p0", j), R("p1", j), "-", R("sI", j)), (tt, R("acc", j), R("p0", j), "max", R("acc", j - 1))]
+
+    x = parts("rr", 0, 8)
+    ts("xl", x, "&", 8191)
+    ts("xh", x, ">>", 13)
+    cp("xlF", "xl")
+    first = hashes(0, 1)
+    second = hashes(1, 1)
+    for i in range(TRY):
+        act(R("hL2", i), "xlF", 64.0 * counter(i) - BIG, 64.0)
+    weave(first[:1], second[:1], [(ts, "H6", "xh", "*", 64.0, "+", 131072.0 - BIG)])
+    weave(first[1:], second[1:])
+    look(0)
+    table(0)
+    look(1)
+    table(1)
+    for h in range(2):
+        mms(("p6", "p7")[h], [("idn", "mask:%d:%d" % (512 * h, 512 * h + 512))])
+    third, fourth = hashes(2, 2), hashes(4, 2)
+    weave(third, fourth[:-3], [None] * 8 + item(0))
+    for i in (2, 3):
+        look(i)
+    table(2)
+    seen(0)
+    weave(item(1), fourth[-3:])
+    for i in (4, 5):
+        look(i)
+    for out, a, c in (("wI0", "idn", "w6"), ("wU", "up8", "w6"), ("wI1", "idn", "w5"), ("wD", "dn8", "w5")):
+        scaled(out, a, c + ":0:1")
+    for i in range(1, TRY - 2):
+        if i + 2 < TRY:
+            table(i + 2)
+        weave(item(i + 1), known(i - 2) if i > 1 else [], go(i - 3) if i > 2 else [])
+        if i == TRY - 3:
+            act("su", "seenB@" + R("c16", i + 1))
+        seen(i)
+    far = T.rank_of(off[0]) // 4
+    halves = (far, 1 - far)
+    weave(known(2), item(5), go(1))
+    for h in halves:
+        tt("sg:%d:%d" % (4096 + 512 * h, 4608 + 512 * h), "su:%d:%d" % (512 * h, 512 * h + 512), "*", ("p6", "p7")[h])
+    for h in halves:
+        wrap(("p3", "p2")[h], "selB", "sg", 4096 + 512 * h, 512)
+
+    def H(name, h):
+        return "%s:%d:%d" % (name, 32 * h, 32 * h + 32)
+
+    def final(h):
+        return [(cp, H("wL", h), ("p3", "p2")[h] + ":0:32"), (ts, H("sL", h), H("wL", h), "&", 1 << 15),
+                (tt, H("p0", h), "p1:%d:%d" % (256 + 32 * h, 288 + 32 * h), "-", H("sL", h)), (tt, H("aA", h), H("p0", h), "max", H("a6", h)),
+                (ts, H("r", h), H("aA", h), "&", 4095), (cp, H("f16", h), H("r", h)),
+                (cp, H("iH", h), H("r", h)), (tt, H("iL", h), H("r", h), "-", H("iH", h))]
+
+    def features(q, r):
+        out = "rspR:%d:%d" % (RW * me, RW * me + 128) if r == me else block("rsp", r, 0, 128)
+        (act if q == "S" else cp)(out, "vecB@" + at("f16", 8, r))
+
+    def items(h):
+        b = ("p3", "p2")[h]
+        mms(b + ":64:96", [("wU", H("iH", h)), ("wI0", H("iL", h))])
+        mms(b + ":96:128", [("wD", H("iH", h)), ("wI1", H("iL", h))])
+
+    def itemcols(h):
+        for j in range(2):
+            cp((T["rsp"][:, 4 * h:4 * h + 4, 128 + 8 * j:136 + 8 * j], parts("rsp", 128 + 8 * j, 136 + 8 * j)[1][4 * h:4 * h + 4]),
+               ("p3", "p2")[h] + ":%d:%d" % (64 + 32 * j, 96 + 32 * j))
+
+    order = [T.rank_of(c) for c in off + on] + [me]
+    early, late = final(halves[0]), final(halves[1])
+    weave(known(3) + go(3) + [(tt, "a6", R("acc", 3), "max", R("cI", 5))], go(2), [None, None] + early[:3])
+    weave(early[3:6])
+    for r in order[:4]:
+        features("S", r)
+    weave(early[6:], late[:2])
+    items(halves[0])
+    weave(late[2:5])
+    itemcols(halves[0])
+    weave(late[5:])
+    items(halves[1])
+    send("r_rsp", lambda q: block("rsp", q), at("rspR", RW, me), "l_rsp", off)
+    features("V", order[4])
+    features("S", order[5])
+    features("V", order[6])
+    itemcols(halves[1])
+    send("r_rsp", lambda q: block("rsp", q), at("rspR", RW, me), "l_rsp", on)
+    features("V", order[7])
+    cp("rspR:%d:%d" % (RW * me + 128, RW * me + RW), block("rsp", me, 128, RW))
+
+    cp("v", "a16")
+    ts("q1", "v", ">>", 7)
+    ts("mm", "v", ">>", 4, "&", 7)
+    ts("bl", "v", "&", 7)
+    ts("b8I", "v", "&", 8)
+    ts("q16", "q1", "*", float(RW - 128))
+    ts("cq", "q1", "*", float(RW), "+", 128.0)
+    ts("q4k", "q1", "*", 4096.0)
+    tt("mb", "mm", "+", "b8I")
+    tt("ps", "v", "+", "q16")
+    cp("l16:64:96", "bl")
+    tt("cl", "cq", "+", "mb")
+    cp("l16:0:32", "ps")
+    cp("l16:32:64", "cl")
+    cp("m2", "oh8:0:8@l16:64:96")
+
+    act("ysb", "rspR@l16:0:32")
+    dma("Y", ext(T.y), "ysb", "d_y")
+    tt("cm", "rspR@l16:32:64", "*", "m2")
+    mms("p7:0:32", [("selB:%d:%d" % (15 - u, 143 - u), "cm:%d:512:16" % u) for u in range(16)])
+    tt("ch1", "p7:0:32", "+", "q4k")
+    dma("S", ext(T.chosen), "ch1", "d_ch")
+    for s in SEMAPHORES:
+        if count.get(s, 0) > waited["G"].get(s, 0):
+            g.wait_ge(T.sem[s], count[s])

@@ -8,19 +8,21 @@ BIG = float(1 << 23)
 OPS = {"+": A_.add, "-": A_.subtract, "*": A_.mult, "min": A_.min, "max": A_.max, ">=": A_.is_ge, ">": A_.is_gt, "<": A_.is_lt,
        "==": A_.is_equal, ">>": A_.arith_shift_right, "&": A_.bitwise_and}
 
+PLAN = "Hf02 Hf22 Hf44 Hn04 Tf02 Tf22 Tf42 Mf00 Sf02 Tn42 Sf23 Tn22 Af00SSSS Tn02 Sn2334 Sn021 An00SVS"
+
 SMALL = {
     "bufI": ("int32", 8, "ckN 32 pI 8 p16I 8 sdI 8 hI 8 lh 8 ckp 8 ckA 8 rkI 16 oT 32 oL 32 oL2 32 oSq 32 oB0 32 oB 32 oSr 32 oA0 32 oA 32 "
-             "oW 32 oB16 32 oP 32 oM 32 own 32 yI 256 v1 32 v 32 thrI 256 aliI 256 xl 64 xh 64 hT 384 hL 384 "
-             "hb 384 hB 384 ha 384 hA 384 pk 384 xI 384 cI 384 wI 320 sI 320 acc 320 a6 64 aA 64 r 64 wL 64 sL 64 q1 32 "
+             "oW 32 oB16 32 oP 32 oM 32 own 32 yI 256 v1 32 v 32 thrI 256 aliI 256 xl 64 xh 64 hL 384 "
+             "hb 384 hB 384 ha 384 hA 384 pk 384 xI 384 cI 384 wI 384 sI 384 val 384 acc 384 r 64 rq4 64 q1 32 "
              "q16 32 ps 32 mm 32 cq 32 cl 32 bl 32 b8I 32 mb 32"),
     "bufF": ("float32", 8, "ones 128 p16F 8 n16 8 e8a 128 e8 128 g9a 16 g9 16 w2 8 w5 8 w6 8 wcol 8 c3 8 wS 8 lhF 8 ckF 8 "
              "ya 8 yc 16 dy 8 dyS 8 sF 8 hF 8 st 256 mqF 256 be 32 beR 32 b8 128 b4 64 "
-             "b2 64 xlF 64 H6 64 hL2 384 ha2 8 nm 8 nm0 8 mT 1024 q4k 32 ch1 32"),
+             "b2 64 xlF 64 ha2 8 nm 8 nm0 8 rank 384 ch1 128"),
     "bufB": ("bfloat16", 16, "onesB 128 ones5 512 lta 128 lt 128 selB 144 selT 144 selP 144 selX 128 ckL 128 "
              "idn 128 up8 128 dn8 128 wI0 128 wI1 128 wU 128 wD 128 iH 64 iL 64 oh8 16 q8 16 "
              "iotaS 128 ohI 512 ohA 512 oh 512 kE 512 inX 512 rs 256 rsw 256 mq 256 sc 256 "
-             "alH 256 alL 256 thH 256 thL 256 win 1024 mask 1024 m2 512 cm 512 ysb 512"),
-    "bufU": ("uint16", 16, "a16 32 e16 384 c16 320 f16 64 l16 96"),
+             "alH 256 alL 256 thH 256 thL 256 win 1024 mT 1024 mask 1024 m2 512 cm 512 ysb 512 selC 48"),
+    "bufU": ("uint16", 16, "a16 32 e16 384 c16 384 f16 64 l16 96"),
 }
 SCRATCH = {}
 TILES = {}
@@ -31,7 +33,7 @@ for _buf, (_type, _step, _list) in SMALL.items():
         _at += -(-int(_c) // _step) * _step
     SCRATCH[_buf] = ("sbuf", [128, _at], _type)
 for _n, _c, _type in (("seenB", 4096, "bfloat16"), ("vecB", 4096, "bfloat16"), ("tabs", 4096, "bfloat16"),
-                      ("tg", 6144, "bfloat16"), ("sg", 5120, "bfloat16"), ("su", 1024, "bfloat16"), ("rspR", N * RW, "bfloat16")):
+                      ("tg", 6144, "bfloat16"), ("sg", 6144, "bfloat16"), ("su", 6144, "bfloat16"), ("rspR", N * RW, "bfloat16")):
     SCRATCH[_n] = ("sbuf", [128, _c], _type)
     TILES[_n] = (_n, 0, _c)
 for _j in range(8):
@@ -40,16 +42,26 @@ for _j in range(8):
 BLOCKS = {"rsp": RW, "rq": 8, "rr": 8}
 for _n, _c in BLOCKS.items():
     SCRATCH[_n] = ("sbuf", [128, N, _c], "bfloat16" if _n == "rsp" else "int32")
+UNITS = {"hT": (12, "int32"), "hL2": (12, "float32"), "H6": (4, "float32")}
+for _n, (_c, _type) in UNITS.items():
+    SCRATCH[_n] = ("sbuf", [128, _c, 32], _type)
 SEMAPHORES = ("sv ss sp sg d_sd d_rk d_thr d_ali d_seen d_vec d_tab0 d_tab1 d_tab2 d_tab3 d_y d_ch "
-              "l_be l_rq l_rsp r_be r_rq r_rsp").split()
+              "l_be l_rq l_far l_near r_be r_rq r_far r_near").split()
+
+COSTS = [dict(zip("cycle pe gather scatter call pick act pool own other dma MB issue be rq far near".split(), _row)) for _row in (
+    (0.00083, 0.00083, 0.00125, 0.0025, 0.04, 0.06, 0.2, 0.15, 0.06, 0.10, 1.1, 3.6, 0.3, 4.0, 2.5, 3.2, 2.0),
+    (0.00083, 0.00042, 0.00125, 0.0025, 0.0, 0.06, 0.2, 0.15, 0.20, 0.20, 1.1, 3.6, 0.3, 3.0, 2.0, 2.5, 1.7),
+    (0.00083, 0.00042, 0.00125, 0.0025, 0.0, 0.06, 0.2, 0.15, 0.06, 0.10, 1.6, 5.0, 0.3, 6.0, 5.0, 6.0, 3.5))]
+ROUNDS, HEAT, REACH, SEED = 40000, 0.05, 12, 1
+KNOWN = []
 
 
-def engine_plan(core, T, topo):
+def engine_plan(core, T, topo, alone=False):
     off = [c for c in T.cores if topo.chip(c) != topo.chip(core)]
     on = [c for c in T.cores if topo.chip(c) == topo.chip(core) and c != core]
     plan = {}
     pool = topo.engines(core, off[0])
-    rest = [e for e in topo.engines(core, on[0]) if e not in pool]
+    rest = [e for e in topo.engines(core, on[0]) if alone or e not in pool]
     for cores, engines in ((off, pool), (on, rest)):
         n = 1
         while 2 * n * len(cores) <= len(engines):
@@ -64,13 +76,95 @@ def engine_plan(core, T, topo):
     return plan, off, on
 
 
+def arrange(calls):
+    n = len(calls)
+    qs = [c["q"] for c in calls]
+    above, near = [], []
+    for c in calls:
+        bits, keep = 0, set()
+        for a in sorted({a["n"] for a in c["after"] + c["behind"]}, reverse=True):
+            if not bits >> a & 1 or calls[a]["late"]:
+                keep.add(a)
+            bits |= above[a] | 1 << a
+        above.append(bits)
+        near.append(keep)
+    for order, _end in KNOWN:
+        at = {i: j for j, i in enumerate(order)}
+        if len(order) == n and all(at[a] < at[i] for i in range(n) for a in near[i]):
+            return [calls[i] for i in order]
+    sets = []
+    for cost in COSTS:
+        time = [sum(cost[k] * v for k, v in c["time"].items()) for c in calls]
+        late = [sum(cost[k] * v for k, v in c["late"].items()) for c in calls]
+        edges = [[(a["n"], time[a["n"]] + (late[a["n"]] or cost["own" if a["q"] == b["q"] else "other"])) for a in b["after"]
+                  if a["n"] in near[b["n"]]] + [(a["n"], 1e-6) for a in b["behind"]] for b in calls]
+        sets.append((time, [time[i] + late[i] for i in range(n)], edges))
+
+    def length(order):
+        total = 0.0
+        for time, full, edges in sets:
+            free, start, end = dict.fromkeys(qs, 0.0), [0.0] * n, 0.0
+            for i in order:
+                q = qs[i]
+                t = free[q]
+                for a, d in edges[i]:
+                    if start[a] + d > t:
+                        t = start[a] + d
+                start[i] = t
+                if q:
+                    free[q] = t + time[i]
+                if t + full[i] > end:
+                    end = t + full[i]
+            total += end
+        return total / len(sets), start
+
+    time, full, edges = sets[0]
+    busy, start = {}, [0.0] * n
+    for i in range(n):
+        t = max([start[a] + d for a, d in edges[i]] + [0.0])
+        if qs[i]:
+            for a, b in busy.setdefault(qs[i], []):
+                if t + time[i] <= a:
+                    break
+                t = max(t, b)
+            busy[qs[i]] = sorted(busy[qs[i]] + [(t, t + time[i])])
+        start[i] = t
+    order = sorted(range(n), key=lambda i: (start[i], i))
+    now = length(order)[0]
+    best, x = (now, order), SEED
+    for r in range(ROUNDS):
+        x = (x * 6364136223846793005 + 1442695040888963407) % (1 << 64)
+        p, hops, step = (x >> 48) * n >> 16, 1 + int((x >> 32 & 65535) ** 3 * REACH >> 48), (x >> 31 & 1) * 2 - 1
+        group, j = [order[p]], p
+        while hops and 0 <= j + step < n:
+            j += step
+            o = order[j]
+            if any((above[o] >> i & 1) if step > 0 else (above[i] >> o & 1) for i in group):
+                group.append(o)
+            elif qs[o] == qs[group[0]]:
+                hops -= 1
+        if hops or len(group) > 6 or not qs[group[0]]:
+            continue
+        if step > 0:
+            new = order[:p] + [o for o in order[p:j + 1] if o not in group] + group + order[j + 1:]
+        else:
+            new = order[:j] + group[::-1] + [o for o in order[j:p + 1] if o not in group] + order[p + 1:]
+        got, start = length(new)
+        if got <= now + HEAT * (1 - r / ROUNDS) * ((x >> 16 & 32767) / 32768) ** 2:
+            now, order = got, sorted(new, key=lambda i: start[i])
+            if now < best[0]:
+                best = now, order
+    KNOWN.append((best[1], best[0]))
+    return [calls[i] for i in best[1]]
+
+
 def rank_program(g, core, T, topo):
     me = T.rank_of(core)
     if me is None:
         return
     queues = {"V": (g.vector, "sv"), "S": (g.scalar, "ss"), "P": (g.tensor, "sp"), "G": (g, "sg"), "Y": (g.sync, None)}
-    V, S, P, Y = g.vector, g.scalar, g.tensor, g.sync
-    count, waited, past = {}, {q: {} for q in queues}, {}
+    V, S, P = g.vector, g.scalar, g.tensor
+    calls, past, named = [], {}, {}
 
     def X(spec):
         if not isinstance(spec, str):
@@ -79,11 +173,14 @@ def rank_program(g, core, T, topo):
             w, o = spec.split("@")
             (wa, wr), (oa, orr) = X(w), X(o)
             return wa.indirect(oa), wr + orr
-        rows, name = (8, spec[2:]) if spec[:2] == "8|" else (128, spec)
+        rows, name = (int(spec.split("|")[0]), spec.split("|")[1]) if "|" in spec else (128, spec)
         f = name.split(":")
         buf, at, n = TILES[f[0]]
         a, b, st = (int(f[1]), int(f[2]), int(f[3]) if len(f) > 3 else 1) if len(f) > 1 else (0, n, 1)
         return T[buf][0:rows, at + a:at + b:st], [(buf, at + a, at + b, st)]
+
+    def width(places):
+        return sum(len(range(*p[1:])) for p in places)
 
     def meet(p, o, own):
         if p[0][0] == "p" and not own:
@@ -92,27 +189,26 @@ def rank_program(g, core, T, topo):
             return False
         return (p[3] == 1 and o[3] == 1) or bool(set(range(p[1], p[2], p[3])) & set(range(o[1], o[2], o[3])))
 
-    def need(q, reads, writes, part=None):
-        tok, mine = {}, queues[q][1]
+    def add(q, emit, reads, writes, time, late=None, sem=None, inc=1, part=None, after=(), behind=()):
+        c = {"n": len(calls), "q": q, "emit": emit, "time": time, "late": late or {}, "sem": sem or queues[q][1], "inc": inc,
+             "behind": list(behind)}
+        dep = {a["n"]: a for a in after}
         for places, wr in ((reads, False), (writes, True)):
             for p in places:
-                for o, t, is_w, pt in past.get(p[0], []):
-                    if (is_w or wr or (p[0][0] == "p" and t[0] != mine)) and tok.get(t[0], 0) < t[1] \
-                            and meet(p, o, t[0] == mine) and (pt is None or part is None or pt == part):
-                        tok[t[0]] = t[1]
-        for s in sorted(tok):
-            if waited[q].get(s, 0) < tok[s]:
-                queues[q][0].wait_ge(T.sem[s], tok[s])
-                waited[q][s] = tok[s]
-
-    def note(tok, reads, writes, part=None):
+                for o, a, is_w, pt in past.get(p[0], []):
+                    if (is_w or wr or (p[0][0] == "p" and a["q"] != q)) and a["n"] not in dep \
+                            and meet(p, o, a["q"] == q) and (pt is None or part is None or pt == part):
+                        dep[a["n"]] = a
+        c["after"] = list(dep.values())
         for places, w in ((reads, False), (writes, True)):
             for p in places:
-                past.setdefault(p[0], []).append((p, tok, w, part))
+                past.setdefault(p[0], []).append((p, c, w, part))
+        calls.append(c)
+        return c
 
-    def run(q, call, out, ins, *more):
+    def run(q, call, out, ins, *more, rate=1.0, time=None):
         oa, ow = X(out)
-        reads, args = [], []
+        reads, args, n = [], [], width(ow)
         for i in ins:
             if isinstance(i, (str, tuple)):
                 a, r = X(i)
@@ -120,46 +216,40 @@ def rank_program(g, core, T, topo):
                 reads = reads + r
             else:
                 args.append(i)
-        need(q, reads, ow)
-        s = queues[q][1]
-        count[s] = count.get(s, 0) + 1
-        call(oa, *args, *more).then_inc(T.sem[s], 1)
-        note((s, count[s]), reads, ow)
+        if isinstance(out, str) and "@" in out:
+            n, rate, reads, ow = 16 * width(ow[1:]), "scatter", reads + ow[1:], ow[:1]
+        elif ins and isinstance(ins[0], str) and "@" in ins[0]:
+            rate = "gather"
+        elif rate == 0.5 and not all(SCRATCH[p[0]][2] in ("bfloat16", "uint16") for p in ow + X(ins[0] if ins else out)[1]):
+            rate = 1.0
+        if time is None:
+            time = {rate: n, "pick": 1} if isinstance(rate, str) else \
+                {"V": {"cycle": max(64, n * rate), "call": 1}, "S": {"cycle": n, "act": 1}, "G": {"cycle": 2 * n, "pool": 1}}[q]
+        return add(q, lambda: call(oa, *args, *more), reads, ow, time)
 
     def ts(out, a, op, s1, op2=None, s2=None):
-        run("V", V.tensor_scalar, out, [a, s1, s2], *([OPS[op]] if op2 is None else [OPS[op], OPS[op2]]))
+        run("V", V.tensor_scalar, out, [a, s1, s2], *([OPS[op]] if op2 is None else [OPS[op], OPS[op2]]), rate=0.5)
 
     def tt(out, a, op, b):
-        run("V", V.tensor_tensor, out, [a, b], OPS[op])
+        run("V", V.tensor_tensor, out, [a, b], OPS[op], rate=1.0 if "p" in (X(a)[1][0][0][0], X(b)[1][0][0][0]) else 2.0)
 
     def cp(out, a):
-        run("V", V.tensor_copy, out, [a])
+        run("V", V.tensor_copy, out, [a], rate=0.5)
 
     def fill(out, c):
-        run("V", V.memset, out, [], c)
+        run("V", V.memset, out, [], c, rate=0.5)
 
-    def scan(out, a, b):
-        run("V", V.tensor_tensor_scan, out, [a, b], 0.0, A_.mult, A_.add)
-
-    idle = []
-
-    def gap(k=1):
-        for _ in range(k):
-            if idle:
-                c = idle.pop(0)
-                c[0](*c[1:])
-
-    def weave(*chains):
-        for j in range(max(len(c) for c in chains)):
-            for c in chains:
-                if j < len(c) and c[j]:
-                    c[j][0](*c[j][1:])
+    def scan(out, a, b, op0=A_.mult, op1=A_.add):
+        run("V", V.tensor_tensor_scan, out, [a, b], 0.0, op0, op1, rate=0.5)
 
     def act(out, a, bias=0.0, scale=1.0, func=AF.Copy):
         run("S", lambda o, i: S.activation(o, i, func, bias=bias, scale=scale), out, [a])
 
     def scaled(out, a, by):
         run("S", lambda o, i, c: S.activation(o, i, AF.Copy, scale=c), out, [a, by])
+
+    def away(out, a, by):
+        run("S", lambda o, i, b: S.activation(o, i, AF.Abs, bias=b), out, [a, by])
 
     def iota(out, pattern, base, cm, exact=False):
         run("G", lambda o: g.iota(o, pattern, base, cm) if exact else
@@ -168,35 +258,40 @@ def rank_program(g, core, T, topo):
     def keep(out, a, pattern, op, base, cm):
         run("G", lambda o, i: g.affine_select(o, i, pattern, OPS[op], 0.0, base, cm), out, [a])
 
-    def mms(out, pairs):
+    def mms(out, pairs, four=False):
         def call(o, *args):
             for j in range(0, len(args), 2):
                 last = P.matmul(o, args[j], args[j + 1], j == 0, j == len(args) - 2)
             return last
-        run("P", call, out, [x for p in pairs for x in p])
+        n = sum(max(min(64, width(X(a)[1])), width(X(b)[1])) for a, b in pairs)
+        run("P", call, out, [x for p in pairs for x in p], time={"pe": n * (4 if four else 1), "pick": 1})
 
-    def dma(q, out, in_, sem, part=None):
+    def dma(q, out, in_, sem, mb, part=None, after=()):
         (oa, ow), (ia, ir) = X(out), X(in_)
-        need(q, ir, ow, part)
-        queues[q][0].dma_start(oa, ia).then_inc(T.sem[sem], 16)
-        count[sem] = count.get(sem, 0) + 16
-        note((sem, count[sem]), ir, ow, part)
+        last = named.get(q)
+        named[q] = add(q, lambda: queues[q][0].dma_start(oa, ia), ir, ow, {"pick": 1}, {"dma": 1, "MB": mb}, sem, 16, part, after,
+                       [last] if last else [])
 
-    plan, off, on = engine_plan(core, T, topo)
+    off, on = engine_plan(core, T, topo)[1:]
 
-    def send(sem, src, dst, local, cores=None):
-        tr = []
+    def send(name, src, dst, cores=None):
+        tr, reads = [], []
+        plan = engine_plan(core, T, topo, cores == on)[0]
         for c in cores or off + on:
             rid, pnc, _s = topo.addr(c)
             a, r = X(src(T.rank_of(c)))
-            need("G", r, [])
+            reads += r
             m = 0
             for e in plan[c]:
                 m |= 1 << e
-            tr.append(RemoteDMATransfer(dst_ids=[DstId(rid=rid, pnc=pnc)], dma_engine_mask=m, remote_sem=T.sem[sem],
-                                        srcs=[a], dsts=[X(dst)[0]], alu_op=0))
-            count[local] = count.get(local, 0) + len(plan[c])
-        g.remote_dma_fused(tr, local_sem=T.sem[local])
+            tr.append(RemoteDMATransfer(dst_ids=[DstId(rid=rid, pnc=pnc)], dma_engine_mask=m, remote_sem=T.sem["r_" + name],
+                                        srcs=[a], dsts=[X(dst(me))[0]], alu_op=0))
+
+        def emit():
+            g.remote_dma_fused(tr, local_sem=T.sem["l_" + name])
+        named[name] = add("G", emit, reads, [], {"issue": 1}, {name: 1}, "l_" + name, sum(len(plan[c]) for c in cores or off + on))
+        add(None, None, [], [p for c in cores or off + on for p in X(dst(T.rank_of(c)))[1]], {}, {"issue": 1, name: 1},
+            "r_" + name, sum(len(engine_plan(c, T, topo, cores == on)[0][core]) for c in cores or off + on), behind=[named[name]])
 
     def block(name, r, a=0, b=None):
         w = BLOCKS[name]
@@ -207,298 +302,274 @@ def rank_program(g, core, T, topo):
         w = BLOCKS[name]
         return T[name][:, :, a:b], [(name, w * r + a, w * r + b, 1) for r in range(N)]
 
-    def landing(piece, sem):
-        count[sem] = sum(len(engine_plan(c, T, topo)[0][core]) for c in T.cores if c != core)
-        for r in range(N):
-            if r != me:
-                note((sem, count[sem]), [], X(piece(r))[1])
-
     def ext(t):
         return (t[:], [])
 
     def at(name, w, i):
         return "%s:%d:%d" % (name, w * i, w * i + w)
 
-    landing(lambda r: at("beR", 4, r), "r_be")
-    landing(lambda r: block("rr", r), "r_rq")
-    landing(lambda r: at("rspR", RW, r), "r_rsp")
+    dma("Y", "sdI:0:1", ext(T.sd), "d_sd", 0.03)
+    dma("S", "8|rkI", ext(T.rk), "d_rk", 0.0)
+    dma("Y", "thrI", ext(T.thr), "d_thr", 0.15)
+    dma("Y", "aliI", ext(T.ali), "d_ali", 0.3)
+    dma("Y", "seenB", ext(T.seen), "d_seen", 1.2)
 
-    dma("Y", "sdI:0:1", ext(T.sd), "d_sd")
-    dma("S", "8|rkI", ext(T.rk), "d_rk")
-    dma("Y", "thrI", ext(T.thr), "d_thr")
-    dma("Y", "aliI", ext(T.ali), "d_ali")
-    dma("Y", "seenB", ext(T.seen), "d_seen")
-
-    for name, c in (("ones", 1.0), ("win", 0.0), ("onesB", 1.0), ("ones5", 1.0), ("selB", 0.0), ("selX", 0.0), ("ckL", 0.0),
-                    ("yc", 0.0), ("be", 0.0), ("rs", 1.0)):
+    for name, c in (("ones", 1.0), ("win", 0.0), ("onesB", 1.0), ("ones5", 1.0), ("yc", 0.0), ("rsw", 1.0)):
         fill(name, c)
     step = 1597 * (TRY + 1)
     iota("ckN", [[step, 32]], -int(BIG), 0, True)
     iota("pI:0:1", [[0, 1]], 0, 1, True)
-    iota("ckp:0:1", [[0, 1]], 0, step, True)
-    iota("q8:0:8", [[1, 8]], 0, 0)
     keep("8|e8a", "8|ones", [[1, 128]], ">=", 0, -16)
     keep("8|e8", "8|e8a", [[-1, 128]], ">=", 15, 16)
     keep("g9a:0:9", "ones:0:9", [[-16, 9]], ">=", 0, 1)
     keep("g9:0:9", "g9a:0:9", [[16, 9]], ">=", 15, -1)
     iota("ohI", [[0, 32], [1, 16]], 0, 0)
+    iota("ckp:0:1", [[0, 1]], 0, step, True)
+    iota("q8:0:8", [[1, 8]], 0, 0)
     keep("lta", "onesB", [[16, 8], [1, 16]], ">", 0, -1)
     keep("lt", "lta", [[-16, 8], [0, 16]], ">=", 0, 1)
     keep("kE", "ones5", [[1, 32], [0, 16]], "==", 0, -1)
-    iota("iotaS", [[1, 128]], 0, 0)
-    ts("p16I:0:1", "pI:0:1", "&", 15)
-    fill("rs:0:256:32", 0.0)
-    cp("p16F:0:1", "p16I:0:1")
-    ts("n16:0:1", "p16F:0:1", "*", -1.0)
-    act("tabs:0:1024", "win")
-    act("tabs:1024:2048", "win")
+    for j in range(2):
+        act(at("tabs", 1024, j), "win")
 
-    idle += [(fill, "rsw", 1.0), (ts, "ckA:0:1", "ckp:0:1", "&", 3840), (ts, "ckA:1:2", "ckp:0:1", "&", 255), (fill, "rsw:0:256:8", 0.0),
-             (cp, "ckF:0:2", "ckA:0:2"), (ts, "c3:0:1", "p16F:0:1", ">=", 4.0, "*", 8192.0),
-             (ts, "ckL:2:128:16", "onesB:0:8", "*", "ckF:0:1"), (ts, "ckL:3:128:16", "onesB:0:8", "*", "ckF:1:2"),
-             (ts, "w2:0:1", "p16F:0:1", ">=", 2.0, "*", 8192.0),
-             (ts, "wS:0:1", "c3:0:1", "max", 1.0), (ts, "wcol:0:1", "w2:0:1", "max", 1.0),
-             (ts, "w6:0:1", "p16F:0:1", "<", 8.0), (ts, "w5:0:1", "p16F:0:1", ">=", 8.0),
-             (tt, "oh8:0:8", "oh:0:8", "+", "oh:8:16")]
     cp("sF:0:1", "sdI:0:1")
     ts("hI:0:1", "sdI:0:1", ">>", 12)
-    ts("8|ya", "8|rkI:0:8", "*", 16.0)
     ts("oT", "ckN", "+", "sF:0:1")
     ts("hF:0:1", "hI:0:1", "*", 64.0, "+", -BIG)
-    tt("8|yc:1:9", "8|ya", "+", "8|rkI:8:16")
     ts("oL", "oT", "&", 4095)
-    ts("lh:0:1", "sdI:0:1", "&", 3840)
-    tt("8|dy", "8|yc:1:9", "-", "8|yc:0:8")
     tt("oSq", "oL", "*", "oL")
-    ts("lh:1:2", "sdI:0:1", "&", 255)
+    ts("8|ya", "8|rkI:0:8", "*", 16.0)
+    tt("8|yc:1:9", "8|ya", "+", "8|rkI:8:16")
+    tt("8|dy", "8|yc:1:9", "-", "8|yc:0:8")
+    mms("p3:0:8", [("8|e8", "8|dy")], True)
+    act("dyS", "p3:0:8")
     ts("oL2", "oL", "*", 64.0, "+", -BIG)
     ts("oB0", "oSq", "+", "hF:0:1")
-    mms("p3:0:8", [("8|e8", "8|dy")])
-    act("dyS", "p3:0:8")
+    ts("oB", "oB0", ">>", 6, "&", 4095)
+    tt("oSr", "oB", "*", "oB")
+    tt("oA0", "oSr", "+", "oL2")
+    ts("oA", "oA0", ">>", 6, "&", 4095)
+    for w in range(N):
+        ts("st:%d:256:8" % w, "oA", ">=", 512.0 * w, "*", at("dyS", 1, w))
+    fill("rsw:0:256:8", 0.0)
+    scan("yI", "rsw", "st")
+    ts("oB16", "oB", "*", 16.0, "+", 8.0)
+    ts("oW", "oA", ">>", 9)
+    tt("oP", "oB16", "+", "oW")
+    tt("oM", "yI:7:256:8", "min", "oP")
+    ts("own", "oM", "&", 7)
+
+    for q in range(N):
+        ts(at("mq", 32, q), "own", "==", float(q))
+    fill("rs", 1.0)
+    fill("rs:0:256:32", 0.0)
+    scan("sc", "rs", "mq")
+    mms("p2:0:8", [("onesB", "q8:0:8"), ("lt", "sc:31:256:32")])
+    cp("mqF", "mq")
+    tt("mqF:0:256:32", "mq:0:256:32", "+", "p2:0:8")
+    scan("p1:0:256", "rs", "mqF")
+    tt("p0:0:128", "p1:0:128", "*", "mq:0:128")
+    tt("b8", "p1:128:256", "*", "mq:128:256")
+    tt("p0:128:192", "p0:0:64", "+", "b8:0:64")
+    tt("b4", "p0:64:128", "+", "b8:64:128")
+    tt("b2", "p0:128:192", "+", "b4")
+    tt("v1", "b2:0:32", "+", "b2:32:64")
+    ts("a16", "v1", "-", 1.0)
+
+    ts("p16I:0:1", "pI:0:1", "&", 15)
+    cp("p16F:0:1", "p16I:0:1")
+    ts("n16:0:1", "p16F:0:1", "*", -1.0)
+    away("ohA", "ohI", "n16:0:1")
+    act("oh", "ohA", 1.0, -1.0, AF.Relu)
+    for name in ("selX", "ckL", "selB", "be"):
+        fill(name, 0.0)
+    ts("lh:0:1", "sdI:0:1", "&", 3840)
+    ts("lh:1:2", "sdI:0:1", "&", 255)
     ts("lh:2:3", "hI:0:1", "&", 255)
     ts("lh:3:4", "hI:0:1", "&", 3840)
-    ts("oB", "oB0", ">>", 6, "&", 4095)
     cp("lhF:0:3", "lh:0:3")
-    run("S", lambda o, i, b: S.activation(o, i, AF.Abs, bias=b), "ohA", ["ohI", "n16:0:1"])
-    act("oh", "ohA", 1.0, -1.0, AF.Relu)
-    act("selB:15:144:16", "g9:0:9")
-    tt("oSr", "oB", "*", "oB")
     ts("lhF:3:4", "lh:3:4", "+", -2048.0)
     for j, c in ((0, "lhF:0:1"), (1, "lhF:1:2"), (4, "lhF:3:4"), (5, "lhF:2:3")):
         scaled("selX:%d:128:16" % j, "g9:0:8", c)
-    tt("oA0", "oSr", "+", "oL2")
-    ts("oB16", "oB", "*", 16.0, "+", 8.0)
-    gap()
-    ts("oA", "oA0", ">>", 6, "&", 4095)
-    gap(2)
-    for w in range(N):
-        ts("st:%d:256:8" % w, "oA", ">=", 512.0 * w, "*", at("dyS", 1, w))
-    ts("oW", "oA", ">>", 9)
-    gap()
-    scan("yI", "rsw", "st")
-    tt("oP", "oB16", "+", "oW")
-    gap()
-    tt("oM", "yI:7:256:8", "min", "oP")
-    gap(2)
-    ts("own", "oM", "&", 7)
-    gap(2)
-    for q in range(N):
-        ts(at("mq", 32, q), "own", "==", float(q))
-    gap(2)
-    scan("sc", "rs", "mq")
-    mms("p2:0:8", [("onesB", "q8:0:8"), ("lt", "sc:31:256:32")])
+    ts("ckA:0:1", "ckp:0:1", "&", 3840)
+    ts("ckA:1:2", "ckp:0:1", "&", 255)
+    cp("ckF:0:2", "ckA:0:2")
+    ts("ckL:2:128:16", "onesB:0:8", "*", "ckF:0:1")
+    ts("ckL:3:128:16", "onesB:0:8", "*", "ckF:1:2")
     mms("p7", [("selX", "oh"), ("ckL", "kE")])
-    act("be:1:32:4", "sc:31:256:32")
-    cp("mqF", "mq")
-    gap()
-    tt("mqF:0:256:32", "mq:0:256:32", "+", "p2:0:8")
-    act("be:0:32:4", "p2:0:8")
     act("inX", "p7")
-    gap()
-    scan("p1:0:256", "rs", "mqF")
-    gap()
-    tt("p0:0:128", "p1:0:128", "*", "mq:0:128")
-    tt("b8", "p1:128:256", "*", "mq:128:256")
-    gap()
-    tt("p0:128:192", "p0:0:64", "+", "b8:0:64")
-    tt("b4", "p0:64:128", "+", "b8:64:128")
-    gap()
-    tt("b2", "p0:128:192", "+", "b4")
-    gap()
-    tt("v1", "b2:0:32", "+", "b2:32:64")
-    gap()
-    ts("a16", "v1", "-", 1.0)
-    send("r_be", lambda q: at("be", 4, q), at("beR", 4, me), "l_be")
-    scaled("selP", "selB", "wS:0:1")
-    act("tabs:2048:4096", "tabs:0:2048")
+    act("be:1:32:4", "sc:31:256:32")
+    act("be:0:32:4", "p2:0:8")
+    send("be", lambda q: at("be", 4, q), lambda r: at("beR", 4, r))
     cp("win@a16", "inX")
+    act("selB:15:144:16", "g9:0:9")
+    ts("c3:0:1", "p16F:0:1", ">=", 4.0, "*", 8192.0)
+    ts("wS:0:1", "c3:0:1", "max", 1.0)
+    scaled("selP", "selB", "wS:0:1")
     mms("p4:0:64", [("selP:%d:%d" % (15 - b, 143 - b), "win:%d:1024:16" % b) for b in range(16)])
+    cp(parts("rq", 0, 8), "p4:0:64")
+    send("rq", lambda q: block("rq", q), lambda r: block("rr", r))
+    cp(block("rr", me), block("rq", me))
+    cp(at("beR", 4, me), at("be", 4, me))
 
     cp("p5:0:256", "aliI")
     act("alH", "p5:0:256", -8.0, 1.0, AF.Relu)
     ts("p6:0:256", "thrI", "+", -2048.0)
     act("thH", "p6:0:256", -4.0)
-    cp(at("beR", 4, me), at("be", 4, me))
-    cp(parts("rq", 0, 8), "p4:0:64")
-    send("r_rq", lambda q: block("rq", q), block("rr", me), "l_rq")
     tt("alL", "p5:0:256", "-", "alH")
     tt("thL", "p6:0:256", "-", "thH")
+    for j in range(2):
+        act(at("tabs", 1024, 2 + j), at("tabs", 1024, j))
     for j, name in ((1, "alH"), (3, "thH"), (0, "alL"), (2, "thL")):
-        dma("Y", (T.tabs[j:128:16, :], X("tabs")[1]), name, "d_tab%d" % j, j)
-    Y.wait_ge(T.sem["l_rq"], count["l_rq"])
-    dma("Y", "vecB", ext(T.vec), "d_vec")
-
-    ts("nm0", "beR:1:32:4", "*", -0.5, "+", 0.5 + float(128 * me))
-    ts("ha2", "beR:1:32:4", "*", 0.5, "+", -0.25)
-    tt("nm", "nm0", "-", "beR:0:32:4")
-    for r in range(N):
-        run("S", lambda o, i, b: S.activation(o, i, AF.Abs, bias=b), at("mT", 128, r), ["iotaS", at("nm", 1, r)])
-    gap(len(idle))
+        dma("Y", (T.tabs[j:128:16, :], X("tabs")[1]), name, "d_tab%d" % j, 0.3, j)
+    dma("Y", "vecB", ext(T.vec), "d_vec", 1.0, after=[named["rq"]])
+    ts("w2:0:1", "p16F:0:1", ">=", 2.0, "*", 8192.0)
+    ts("wcol:0:1", "w2:0:1", "max", 1.0)
     scaled("selT", "selB", "wcol:0:1")
-    cp(block("rr", me), block("rq", me))
-    for r in range(N):
-        ts(at("mask", 128, r), at("mT", 128, r), "<", at("ha2", 1, r), "*", float(2 ** (15 - r)))
-    keep("idn", "onesB", [[-1, 128]], "==", 0, 1)
-    keep("up8", "onesB", [[-1, 128]], "==", 8, 1)
-    keep("dn8", "onesB", [[-1, 128]], "==", -8, 1)
 
-    def R(name, i, n=1):
-        return "%s:%d:%d" % (name, 64 * i, 64 * i + 64 * n)
+    near = me // 4
+    far = 1 - near
+    order = [T.rank_of(c) for c in off + on] + [me]
+
+    def masks(ranks):
+        for r in ranks:
+            away(at("mT", 128, r), "iotaS", at("nm", 1, r))
+            ts(at("mask", 128, r), at("mT", 128, r), "<", at("ha2", 1, r), "*", -float(2 ** (15 - r)))
+
+    def shifts():
+        ts("w6:0:1", "p16F:0:1", "<", 8.0)
+        ts("w5:0:1", "p16F:0:1", ">=", 8.0)
+        keep("idn", "onesB", [[-1, 128]], "==", 0, 1)
+        keep("up8", "onesB", [[-1, 128]], "==", 8, 1)
+        keep("dn8", "onesB", [[-1, 128]], "==", -8, 1)
+        for out, a, c in (("wI0", "idn", "w6"), ("wU", "up8", "w6"), ("wI1", "idn", "w5"), ("wD", "dn8", "w5")):
+            scaled(out, a, c + ":0:1")
+
+    def span(h, i, n=1):
+        return (i if h == 0 else 2 * TRY - i - n, n)
+
+    def R(name, s, w=32):
+        return "%s:%d:%d" % (name, w * s[0], w * (s[0] + s[1]))
+
+    def units(name, a, b, step=1):
+        return T[name][:, a:b:step, :], [(name, 32 * j, 32 * j + 32, 1) for j in range(a, b, step)]
+
+    def both(name, i):
+        return units(name, i, 2 * TRY - i, 2 * TRY - 1 - 2 * i)
 
     def counter(i):
         return float(1597 * (i + 1) % 4096)
 
-    def hashes(i0, n):
+    def hashes(s):
         def r(tile):
-            return R(tile, i0, n)
-        each = range(i0, i0 + n)
-        return ([(ts, R("hT", i), "xl", "+", counter(i)) for i in each] +
-                [(ts, r("hL"), r("hT"), "&", 4095), (tt, r("p0"), r("hL"), "*", r("hL"))] +
-                [(tt, R("hb", i), R("p0", i), "+", "H6") for i in each] +
-                [(ts, r("hB"), r("hb"), ">>", 6, "&", 4095), (tt, r("p1"), r("hB"), "*", r("hB")),
-                 (tt, r("ha"), r("p1"), "+", r("hL2")), (ts, r("hA"), r("ha"), ">>", 6, "&", 4095), (cp, r("e16"), r("hA")),
-                 (ts, r("p0"), r("hB"), "*", 8192.0, "+", 4096.0 - 16777216.0), (tt, r("pk"), r("p0"), "+", r("hA"))])
+            return R(tile, s)
+        a, b = s[0], s[0] + s[1]
+        ts(r("hL"), units("hT", a, b), "&", 4095)
+        tt(r("p0"), r("hL"), "*", r("hL"))
+        for j in range(a, b, 2):
+            tt(R("hb", (j, 2)), R("p0", (j, 2)), "+", units("H6", j // TRY * 2, j // TRY * 2 + 2))
+        ts(r("hB"), r("hb"), ">>", 6, "&", 4095)
+        tt(r("p1"), r("hB"), "*", r("hB"))
+        tt(r("ha"), r("p1"), "+", units("hL2", a, b))
+        ts(r("hA"), r("ha"), ">>", 6, "&", 4095)
+        cp(r("e16"), r("hA"))
+        ts(r("p0"), r("hB"), "*", 8192.0, "+", 4096.0 - 16777216.0)
+        tt(r("pk"), r("p0"), "+", r("hA"))
 
-    def wrap(out, sel, src, a, n):
-        mms(out + ":0:%d" % (n // 16), [("%s:%d:%d" % (sel, 15 - b, 143 - b), "%s:%d:%d:16" % (src, a + b, a + n)) for b in range(16)])
+    def wrap(bank, sel, src, s):
+        a, b = 512 * s[0], 512 * (s[0] + s[1])
+        mms(R(bank, (0, s[1])), [("%s:%d:%d" % (sel, 15 - j, 143 - j), "%s:%d:%d:16" % (src, a + j, b)) for j in range(16)])
 
-    def bank(i):
-        return ("p2", "p5")[i % 2]
+    def candidates(s, bank):
+        act(R("tg", s, 512), "tabs@" + R("e16", s))
+        wrap(bank, "selT", "tg", s)
+        tt(R("xI", s), R(bank, (0, s[1])), "min", R("pk", s))
+        ts(R("cI", s), R("xI", s), "&", 4095)
+        cp(R("c16", s), R("cI", s))
+        tt(R("p1", s), R("cI", s), "+", R("p6", s))
 
-    def sbank(i):
-        return ("p3", "p4")[i % 2]
+    best = {}
 
-    def table(i):
-        wrap(bank(i), "selT", "tg", 1024 * i, 1024)
+    def rival(h, i, tile):
+        if h in best:
+            tt(R("acc", span(h, i)), R(tile, span(h, i)), "max", best[h])
+            tile = "acc"
+        best[h] = R(tile, span(h, i))
 
-    def look(i):
-        act(at("tg", 1024, i), "tabs@" + R("e16", i))
+    def unseen(h, i, n, bank, scalar=()):
+        for j in range(i, i + n):
+            s = span(h, j)
+            if j in scalar:
+                act(R("su", s, 512), "seenB@" + R("c16", s))
+                scan(R("sg", s, 512), R("su", s, 512), at("mask", 512, h), A_.max, A_.mult)
+            else:
+                tt(R("sg", s, 512), "seenB@" + R("c16", s), "*", at("mask", 512, h))
+        s = span(h, i, n)
+        wrap(bank, "selB", "sg", s)
+        ts(R("wI", s), R(bank, (0, n)), "*", -1.0)
+        ts(R("sI", s), R("wI", s), "&", 1 << 15)
+        tt(R("val", s), R("p1", s), "-", R("sI", s))
+        for j in range(i, i + n):
+            rival(h, j, "val")
 
-    def seen(i):
-        tt(at("sg", 1024, i), "seenB@" + R("c16", i), "*", "mask")
-        wrap(sbank(i), "selB", "sg", 1024 * i, 1024)
-
-    def item(i):
-        ops = [(tt, R("xI", i), bank(i) + ":0:64", "min", R("pk", i)), (ts, R("cI", i), R("xI", i), "&", 4095)]
-        if i < TRY - 1:
-            ops.append((cp, R("c16", i), R("cI", i)))
-            ops.append((ts, R("p1", i), R("cI", i), "+", 4096.0 * (TRY - 1 - i)))
-        return ops
-
-    def known(j):
-        return [(cp, R("wI", j), sbank(j) + ":0:64"), (ts, R("sI", j), R("wI", j), "&", 1 << 15)]
-
-    def go(j):
-        if j == 0:
-            return [(tt, R("acc", 0), R("p1", 0), "-", R("sI", 0))]
-        return [(tt, R("p0", j), R("p1", j), "-", R("sI", j)), (tt, R("acc", j), R("p0", j), "max", R("acc", j - 1))]
+    def answer(h, name, cores, engines):
+        def H(tile):
+            return at(tile, 32, h)
+        ts(H("r"), best[h], "&", 4095)
+        cp(H("f16"), H("r"))
+        ts(H("iH"), H("r"), "+", 4096.0 * me)
+        ts(H("rq4"), H("r"), "+", 4096.0 * me)
+        tt(H("iL"), H("rq4"), "-", H("iH"))
+        mms("p7:0:32", [("wU", H("iH")), ("wI0", H("iL"))])
+        mms("p7:32:64", [("wD", H("iH")), ("wI1", H("iL"))])
+        for j in range(2):
+            cp((T["rsp"][:, 4 * h:4 * h + 4, 128 + 8 * j:136 + 8 * j], parts("rsp", 128 + 8 * j, 136 + 8 * j)[1][4 * h:4 * h + 4]),
+               at("p7", 32, j))
+        for c, q in zip(cores, engines):
+            (act if q == "S" else cp)(block("rsp", T.rank_of(c), 0, 128), "vecB@" + at("f16", 8, T.rank_of(c)))
+        send(name, lambda q: block("rsp", q), lambda r: at("rspR", RW, r), cores)
 
     x = parts("rr", 0, 8)
     ts("xl", x, "&", 8191)
     ts("xh", x, ">>", 13)
     cp("xlF", "xl")
-    first = hashes(0, 1)
-    second = hashes(1, 1)
     for i in range(TRY):
-        act(R("hL2", i), "xlF", 64.0 * counter(i) - BIG, 64.0)
-    weave(first[:1], second[:1], [(ts, "H6", "xh", "*", 64.0, "+", 131072.0 - BIG)])
-    weave(first[1:], second[1:])
-    look(0)
-    table(0)
-    look(1)
-    table(1)
-    for h in range(2):
-        mms(("p6", "p7")[h], [("idn", "mask:%d:%d" % (512 * h, 512 * h + 512))])
-    third, fourth = hashes(2, 2), hashes(4, 2)
-    weave(third, fourth[:-3], [None] * 8 + item(0))
-    for i in (2, 3):
-        look(i)
-    table(2)
-    seen(0)
-    weave(item(1), fourth[-3:])
-    for i in (4, 5):
-        look(i)
-    for out, a, c in (("wI0", "idn", "w6"), ("wU", "up8", "w6"), ("wI1", "idn", "w5"), ("wD", "dn8", "w5")):
-        scaled(out, a, c + ":0:1")
-    for i in range(1, TRY - 2):
-        if i + 2 < TRY:
-            table(i + 2)
-        weave(item(i + 1), known(i - 2) if i > 1 else [], go(i - 3) if i > 2 else [])
-        if i == TRY - 3:
-            act("su", "seenB@" + R("c16", i + 1))
-        seen(i)
-    far = T.rank_of(off[0]) // 4
-    halves = (far, 1 - far)
-    weave(known(2), item(5), go(1))
-    for h in halves:
-        tt("sg:%d:%d" % (4096 + 512 * h, 4608 + 512 * h), "su:%d:%d" % (512 * h, 512 * h + 512), "*", ("p6", "p7")[h])
-    for h in halves:
-        wrap(("p3", "p2")[h], "selB", "sg", 4096 + 512 * h, 512)
-
-    def H(name, h):
-        return "%s:%d:%d" % (name, 32 * h, 32 * h + 32)
-
-    def final(h):
-        return [(cp, H("wL", h), ("p3", "p2")[h] + ":0:32"), (ts, H("sL", h), H("wL", h), "&", 1 << 15),
-                (tt, H("p0", h), "p1:%d:%d" % (256 + 32 * h, 288 + 32 * h), "-", H("sL", h)), (tt, H("aA", h), H("p0", h), "max", H("a6", h)),
-                (ts, H("r", h), H("aA", h), "&", 4095), (cp, H("f16", h), H("r", h)),
-                (cp, H("iH", h), H("r", h)), (tt, H("iL", h), H("r", h), "-", H("iH", h))]
-
-    def features(q, r):
-        out = "rspR:%d:%d" % (RW * me, RW * me + 128) if r == me else block("rsp", r, 0, 128)
-        (act if q == "S" else cp)(out, "vecB@" + at("f16", 8, r))
-
-    def items(h):
-        b = ("p3", "p2")[h]
-        mms(b + ":64:96", [("wU", H("iH", h)), ("wI0", H("iL", h))])
-        mms(b + ":96:128", [("wD", H("iH", h)), ("wI1", H("iL", h))])
-
-    def itemcols(h):
-        for j in range(2):
-            cp((T["rsp"][:, 4 * h:4 * h + 4, 128 + 8 * j:136 + 8 * j], parts("rsp", 128 + 8 * j, 136 + 8 * j)[1][4 * h:4 * h + 4]),
-               ("p3", "p2")[h] + ":%d:%d" % (64 + 32 * j, 96 + 32 * j))
-
-    order = [T.rank_of(c) for c in off + on] + [me]
-    early, late = final(halves[0]), final(halves[1])
-    weave(known(3) + go(3) + [(tt, "a6", R("acc", 3), "max", R("cI", 5))], go(2), [None, None] + early[:3])
-    weave(early[3:6])
-    for r in order[:4]:
-        features("S", r)
-    weave(early[6:], late[:2])
-    items(halves[0])
-    weave(late[2:5])
-    itemcols(halves[0])
-    weave(late[5:])
-    items(halves[1])
-    send("r_rsp", lambda q: block("rsp", q), at("rspR", RW, me), "l_rsp", off)
-    features("V", order[4])
-    features("S", order[5])
-    features("V", order[6])
-    itemcols(halves[1])
-    send("r_rsp", lambda q: block("rsp", q), at("rspR", RW, me), "l_rsp", on)
-    features("V", order[7])
+        ts(both("hT", i), "xl", "+", counter(i))
+        act(both("hL2", i), "xlF", 64.0 * counter(i) - BIG, 64.0)
+    for j in range(2):
+        ts(units("H6", j, 4, 2), "xh", "*", 64.0, "+", 131072.0 - BIG)
+    iota("iotaS", [[1, 128]], 0, 0)
+    ts("nm0", "beR:1:32:4", "*", -0.5, "+", 0.5 + float(128 * me))
+    ts("ha2", "beR:1:32:4", "*", 0.5, "+", -0.25)
+    tt("nm", "nm0", "-", "beR:0:32:4")
+    masks(order[:4])
+    iota("rank:0:192", [[-4096, TRY], [0, 32]], 4096 * (TRY - 1), 0)
+    iota("rank:192:384", [[4096, TRY], [0, 32]], 0, 0)
+    act("p6:0:384", "rank")
+    banks = {"T": ["p2", "p5"], "S": ["p3", "p4"]}
+    for s in PLAN.split():
+        h, i, n = {"f": far, "n": near}[s[1]], int(s[2]), int(s[3])
+        if s[0] == "H":
+            hashes(span(h, i, n))
+        elif s[0] == "T":
+            candidates(span(h, i, n), banks["T"][0])
+            banks["T"].reverse()
+            for hh in (h, 1 - h)[:max(0, i + n - TRY + 1)]:
+                rival(hh, TRY - 1, "cI")
+        elif s[0] == "S":
+            unseen(h, i, n, banks["S"][0], [int(j) for j in s[4:]])
+            banks["S"].reverse()
+        elif s[0] == "A":
+            answer(h, "far" if h == far else "near", off if h == far else on, s[4:])
+        else:
+            masks(order[4:])
+            shifts()
+    act("rspR:%d:%d" % (RW * me, RW * me + 128), "vecB@" + at("f16", 8, me))
     cp("rspR:%d:%d" % (RW * me + 128, RW * me + RW), block("rsp", me, 128, RW))
 
+    fill("selC", 0.0)
+    act("selC:3:35:4", "g9:0:8")
+    tt("oh8:0:8", "oh:0:8", "+", "oh:8:16")
     cp("v", "a16")
     ts("q1", "v", ">>", 7)
     ts("mm", "v", ">>", 4, "&", 7)
@@ -506,7 +577,6 @@ def rank_program(g, core, T, topo):
     ts("b8I", "v", "&", 8)
     ts("q16", "q1", "*", float(RW - 128))
     ts("cq", "q1", "*", float(RW), "+", 128.0)
-    ts("q4k", "q1", "*", 4096.0)
     tt("mb", "mm", "+", "b8I")
     tt("ps", "v", "+", "q16")
     cp("l16:64:96", "bl")
@@ -516,11 +586,27 @@ def rank_program(g, core, T, topo):
     cp("m2", "oh8:0:8@l16:64:96")
 
     act("ysb", "rspR@l16:0:32")
-    dma("Y", ext(T.y), "ysb", "d_y")
+    dma("Y", ext(T.y), "ysb", "d_y", 0.1)
     tt("cm", "rspR@l16:32:64", "*", "m2")
-    mms("p7:0:32", [("selB:%d:%d" % (15 - u, 143 - u), "cm:%d:512:16" % u) for u in range(16)])
-    tt("ch1", "p7:0:32", "+", "q4k")
-    dma("S", ext(T.chosen), "ch1", "d_ch")
+    for c in range(4):
+        mms("32|" + at("p7", 32, c), [("selC:%d:%d" % (3 - a, 35 - a), "cm:%d:512:16" % (4 * a + c)) for a in range(4)])
+    cp("32|ch1", "32|p7:0:128")
+    dma("S", ext(T.chosen), "32|ch1", "d_ch", 0.0)
+
+    count, waited = {}, {q: {} for q in queues}
+    for c in arrange(calls):
+        if c["q"] is not None:
+            need = {}
+            for a in c["after"]:
+                need[a["sem"]] = max(need.get(a["sem"], 0), a["count"])
+            for s in sorted(need):
+                if waited[c["q"]].get(s, 0) < need[s]:
+                    queues[c["q"]][0].wait_ge(T.sem[s], need[s])
+                    waited[c["q"]][s] = need[s]
+            done = c["emit"]()
+            if done is not None:
+                done.then_inc(T.sem[c["sem"]], c["inc"])
+        c["count"] = count[c["sem"]] = count.get(c["sem"], 0) + c["inc"]
     for s in SEMAPHORES:
         if count.get(s, 0) > waited["G"].get(s, 0):
             g.wait_ge(T.sem[s], count[s])

@@ -8,19 +8,17 @@ BIG = float(1 << 23)
 OPS = {"+": A_.add, "-": A_.subtract, "*": A_.mult, "min": A_.min, "max": A_.max, ">=": A_.is_ge, ">": A_.is_gt, "<": A_.is_lt,
        "==": A_.is_equal, ">>": A_.arith_shift_right, "&": A_.bitwise_and}
 
-PLAN = "Hf02 Hf22 Hf44 Hn04 Tf02 Tf22 Tf42 Mf00 Sf02 Tn42 Sf23 Tn22 Af00SSSS Tn02 Sn2334 Sn021 An00SVS"
+PLAN = "Tb01 Tf12 Tf32 Mf00 Sf03 Tn12 Sf32 Tn32 Tf51 Tn51 Af00SSSS Sn0312 Sn324 An00SVS"
 
 SMALL = {
-    "bufI": ("int32", 8, "ckN 32 pI 8 p16I 8 sdI 8 hI 8 lh 8 ckp 8 ckA 8 rkI 16 oT 32 oL 32 oL2 32 oSq 32 oB0 32 oB 32 oSr 32 oA0 32 oA 32 "
-             "oW 32 oB16 32 oP 32 oM 32 own 32 yI 256 v1 32 v 32 thrI 256 aliI 256 xl 64 xh 64 hL 384 "
-             "hb 384 hB 384 ha 384 hA 384 pk 384 xI 384 cI 384 wI 384 sI 384 val 384 acc 384 r 64 rq4 64 q1 32 "
-             "q16 32 ps 32 mm 32 cq 32 cl 32 bl 32 b8I 32 mb 32"),
+    "bufI": ("int32", 8, "pI 8 p16I 8 sdI 128 hI 8 h64 32 lh 8 ckp 8 ckA 8 rkI 16 oT 32 oB0 64 oA0 64 oA 32 "
+             "oW 32 oB16 32 own 32 yI 256 v 32 thrI 256 aliI 256 xl 64 hT 384 hb 768 ha 768 oz 128 oy 128 lz 384 ly 384 bz 384 by 768 "
+             "xI 384 cI 384 wI 384 d0 384 d1 384 res 384 q1 32 q16 32 ps 32 mm 32 cq 32 cl 32 bl 32 b8I 32 mb 32"),
     "bufF": ("float32", 8, "ones 128 p16F 8 n16 8 e8a 128 e8 128 g9a 16 g9 16 w2 8 w5 8 w6 8 wcol 8 c3 8 wS 8 lhF 8 ckF 8 "
-             "ya 8 yc 16 dy 8 dyS 8 sF 8 hF 8 st 256 mqF 256 be 32 beR 32 b8 128 b4 64 "
-             "b2 64 xlF 64 ha2 8 nm 8 nm0 8 rank 384 ch1 128"),
+             "ya 8 yc 16 dy 8 dyS 8 st 256 top 256 be 32 beR 32 ha2 8 nm 8 nm0 8 ch1 128"),
     "bufB": ("bfloat16", 16, "onesB 128 ones5 512 lta 128 lt 128 selB 144 selT 144 selP 144 selX 128 ckL 128 "
-             "idn 128 up8 128 dn8 128 wI0 128 wI1 128 wU 128 wD 128 iH 64 iL 64 oh8 16 q8 16 "
-             "iotaS 128 ohI 512 ohA 512 oh 512 kE 512 inX 512 rs 256 rsw 256 mq 256 sc 256 "
+             "idn 128 up8 128 dn8 128 wI0 128 wI1 128 wU 128 wD 128 iH 64 iL 64 oh8 16 o128 32 "
+             "iotaS 128 ohI 512 ohA 512 oh 512 kE 512 inX 512 rs 256 mq 256 sc 256 mine 256 sb 256 "
              "alH 256 alL 256 thH 256 thL 256 win 1024 mT 1024 mask 1024 m2 512 cm 512 ysb 512 selC 48"),
     "bufU": ("uint16", 16, "a16 32 e16 384 c16 384 f16 64 l16 96"),
 }
@@ -42,17 +40,15 @@ for _j in range(8):
 BLOCKS = {"rsp": RW, "rq": 8, "rr": 8}
 for _n, _c in BLOCKS.items():
     SCRATCH[_n] = ("sbuf", [128, N, _c], "bfloat16" if _n == "rsp" else "int32")
-UNITS = {"hT": (12, "int32"), "hL2": (12, "float32"), "H6": (4, "float32")}
-for _n, (_c, _type) in UNITS.items():
-    SCRATCH[_n] = ("sbuf", [128, _c, 32], _type)
+for _n in ("hA", "kp"):
+    SCRATCH[_n] = ("sbuf", [128, 2 * TRY, 32], "int32")
 SEMAPHORES = ("sv ss sp sg d_sd d_rk d_thr d_ali d_seen d_vec d_tab0 d_tab1 d_tab2 d_tab3 d_y d_ch "
               "l_be l_rq l_far l_near r_be r_rq r_far r_near").split()
 
 COSTS = [dict(zip("cycle pe gather scatter call pick act pool own other dma MB issue be rq far near".split(), _row)) for _row in (
-    (0.00083, 0.00083, 0.00125, 0.0025, 0.04, 0.06, 0.2, 0.15, 0.06, 0.10, 1.1, 3.6, 0.3, 4.0, 2.5, 3.2, 2.0),
-    (0.00083, 0.00042, 0.00125, 0.0025, 0.0, 0.06, 0.2, 0.15, 0.20, 0.20, 1.1, 3.6, 0.3, 3.0, 2.0, 2.5, 1.7),
-    (0.00083, 0.00042, 0.00125, 0.0025, 0.0, 0.06, 0.2, 0.15, 0.06, 0.10, 1.6, 5.0, 0.3, 6.0, 5.0, 6.0, 3.5))]
-ROUNDS, HEAT, REACH, SEED = 40000, 0.05, 12, 1
+    (0.00083, 0.00042, 0.00125, 0.0025, 0.0, 0.06, 0.2, 0.15, 0.20, 0.20, 1.3, 3.6, 0.3, 3.5, 2.3, 4.0, 2.0),
+    (0.00110, 0.00060, 0.00200, 0.0045, 0.0, 0.06, 0.25, 0.15, 0.25, 0.25, 1.6, 5.0, 0.5, 5.0, 3.5, 5.5, 3.0))]
+ROUNDS, HEAT, REACH, SEED = 80000, 0.4, 12, 1
 KNOWN = []
 
 
@@ -101,7 +97,7 @@ def arrange(calls):
         sets.append((time, [time[i] + late[i] for i in range(n)], edges))
 
     def length(order):
-        total = 0.0
+        total, starts = 0.0, []
         for time, full, edges in sets:
             free, start, end = dict.fromkeys(qs, 0.0), [0.0] * n, 0.0
             for i in order:
@@ -116,7 +112,21 @@ def arrange(calls):
                 if t + full[i] > end:
                     end = t + full[i]
             total += end
-        return total / len(sets), start
+            starts.append(start)
+        return total / len(sets), starts
+
+    def holds(order, starts):
+        before, last, pairs = {}, {}, []
+        for i in order:
+            before[i], last[qs[i]] = last.get(qs[i]), i
+        for (time, full, edges), start in zip(sets, starts):
+            i = max(range(n), key=lambda i: start[i] + full[i])
+            while start[i] > 0.0:
+                a = [a for a, d in edges[i] if start[a] + d >= start[i]]
+                if not a:
+                    pairs.append((i, before[i]))
+                i = a[0] if a else before[i]
+        return pairs
 
     time, full, edges = sets[0]
     busy, start = {}, [0.0] * n
@@ -131,10 +141,12 @@ def arrange(calls):
         start[i] = t
     order = sorted(range(n), key=lambda i: (start[i], i))
     now = length(order)[0]
-    best, x = (now, order), SEED
+    best, x, held = (now, order), SEED, []
     for r in range(ROUNDS):
         x = (x * 6364136223846793005 + 1442695040888963407) % (1 << 64)
         p, hops, step = (x >> 48) * n >> 16, 1 + int((x >> 32 & 65535) ** 3 * REACH >> 48), (x >> 31 & 1) * 2 - 1
+        if x >> 8 & 3 and held:
+            p = order.index(held[(x >> 48) * len(held) >> 16][step > 0])
         group, j = [order[p]], p
         while hops and 0 <= j + step < n:
             j += step
@@ -149,9 +161,9 @@ def arrange(calls):
             new = order[:p] + [o for o in order[p:j + 1] if o not in group] + group + order[j + 1:]
         else:
             new = order[:j] + group[::-1] + [o for o in order[j:p + 1] if o not in group] + order[p + 1:]
-        got, start = length(new)
+        got, starts = length(new)
         if got <= now + HEAT * (1 - r / ROUNDS) * ((x >> 16 & 32767) / 32768) ** 2:
-            now, order = got, sorted(new, key=lambda i: start[i])
+            now, order, held = got, sorted(new, key=lambda i: starts[0][i]), holds(new, starts)
             if now < best[0]:
                 best = now, order
     KNOWN.append((best[1], best[0]))
@@ -239,8 +251,16 @@ def rank_program(g, core, T, topo):
     def fill(out, c):
         run("V", V.memset, out, [], c, rate=0.5)
 
-    def scan(out, a, b, op0=A_.mult, op1=A_.add):
-        run("V", V.tensor_tensor_scan, out, [a, b], 0.0, op0, op1, rate=0.5)
+    def scan(out, a, b, op0=A_.mult, op1=A_.add, first=0.0):
+        run("V", V.tensor_tensor_scan, out, [a, b], first, op0, op1, rate=0.5)
+
+    def half(name, w, i, j):
+        return "%s:%d:%d:2" % (name, w * i + j, w * i + w)
+
+    def square(out, z, y, a, *ops):
+        ts(half(*z, 1), a, *ops)
+        ts(half(*y, 0), a, *ops)
+        scan(at(*out), at(*z), at(*y))
 
     def act(out, a, bias=0.0, scale=1.0, func=AF.Copy):
         run("S", lambda o, i: S.activation(o, i, func, bias=bias, scale=scale), out, [a])
@@ -258,13 +278,17 @@ def rank_program(g, core, T, topo):
     def keep(out, a, pattern, op, base, cm):
         run("G", lambda o, i: g.affine_select(o, i, pattern, OPS[op], 0.0, base, cm), out, [a])
 
-    def mms(out, pairs, four=False):
+    def mms(out, pairs, four=False, stop=True, begun=None):
         def call(o, *args):
             for j in range(0, len(args), 2):
-                last = P.matmul(o, args[j], args[j + 1], j == 0, j == len(args) - 2)
+                last = P.matmul(o, args[j], args[j + 1], j == 0 and not begun, j == len(args) - 2 and stop)
             return last
         n = sum(max(min(64, width(X(a)[1])), width(X(b)[1])) for a, b in pairs)
-        run("P", call, out, [x for p in pairs for x in p], time={"pe": n * (4 if four else 1), "pick": 1})
+        c = run("P", call, out, [x for p in pairs for x in p], time={"pe": n * (4 if four else 1), "pick": 1})
+        if begun:
+            c["after"].remove(begun)
+            c["behind"].append(begun)
+        return c
 
     def dma(q, out, in_, sem, mb, part=None, after=()):
         (oa, ow), (ia, ir) = X(out), X(in_)
@@ -314,67 +338,59 @@ def rank_program(g, core, T, topo):
     dma("Y", "aliI", ext(T.ali), "d_ali", 0.3)
     dma("Y", "seenB", ext(T.seen), "d_seen", 1.2)
 
-    for name, c in (("ones", 1.0), ("win", 0.0), ("onesB", 1.0), ("ones5", 1.0), ("yc", 0.0), ("rsw", 1.0)):
-        fill(name, c)
     step = 1597 * (TRY + 1)
-    iota("ckN", [[step, 32]], -int(BIG), 0, True)
+    for name, c in (("ones", 1.0), ("sdI:4:128", step), ("h64", 0), ("oz:0:128:2", 0), ("win", 0.0), ("onesB", 1.0),
+                    ("ones5", 1.0), ("yc", 0.0), ("top", BIG), ("st:0:256:8", BIG), ("lz:0:384:2", 0), ("bz:0:384:2", 0),
+                    ("d0:0:384:6", 0)):
+        fill(name, c)
     iota("pI:0:1", [[0, 1]], 0, 1, True)
     keep("8|e8a", "8|ones", [[1, 128]], ">=", 0, -16)
     keep("8|e8", "8|e8a", [[-1, 128]], ">=", 15, 16)
     keep("g9a:0:9", "ones:0:9", [[-16, 9]], ">=", 0, 1)
     keep("g9:0:9", "g9a:0:9", [[16, 9]], ">=", 15, -1)
     iota("ohI", [[0, 32], [1, 16]], 0, 0)
-    iota("ckp:0:1", [[0, 1]], 0, step, True)
-    iota("q8:0:8", [[1, 8]], 0, 0)
+    iota("ckp:0:1", [[0, 1]], 1597, step, True)
     keep("lta", "onesB", [[16, 8], [1, 16]], ">", 0, -1)
     keep("lt", "lta", [[-16, 8], [0, 16]], ">=", 0, 1)
     keep("kE", "ones5", [[1, 32], [0, 16]], "==", 0, -1)
     for j in range(2):
         act(at("tabs", 1024, j), "win")
 
-    cp("sF:0:1", "sdI:0:1")
-    ts("hI:0:1", "sdI:0:1", ">>", 12)
-    ts("oT", "ckN", "+", "sF:0:1")
-    ts("hF:0:1", "hI:0:1", "*", 64.0, "+", -BIG)
-    ts("oL", "oT", "&", 4095)
-    tt("oSq", "oL", "*", "oL")
+    scan("oT", "ones:0:32", "sdI:0:128:4", first=-BIG)
+    ts("h64:0:1", "sdI:0:1", ">>", 6, "&", 4095 << 6)
+    scan("oy:1:64:2", "ones:0:32", "h64")
+    square(("oB0", 64, 0), ("oz", 64, 0), ("oy", 64, 0), "oT", "&", 4095)
+    ts("oy:65:128:2", "oy:0:64:2", "*", 64.0)
+    square(("oA0", 64, 0), ("oz", 64, 1), ("oy", 64, 1), "oB0:1:64:2", ">>", 6, "&", 4095)
+    ts("oA", "oA0:1:64:2", ">>", 6, "&", 4095)
     ts("8|ya", "8|rkI:0:8", "*", 16.0)
     tt("8|yc:1:9", "8|ya", "+", "8|rkI:8:16")
     tt("8|dy", "8|yc:1:9", "-", "8|yc:0:8")
     mms("p3:0:8", [("8|e8", "8|dy")], True)
     act("dyS", "p3:0:8")
-    ts("oL2", "oL", "*", 64.0, "+", -BIG)
-    ts("oB0", "oSq", "+", "hF:0:1")
-    ts("oB", "oB0", ">>", 6, "&", 4095)
-    tt("oSr", "oB", "*", "oB")
-    tt("oA0", "oSr", "+", "oL2")
-    ts("oA", "oA0", ">>", 6, "&", 4095)
-    for w in range(N):
+    scaled("top:0:256:8", "ones:0:32", "dyS:0:1")
+    for w in range(1, N):
         ts("st:%d:256:8" % w, "oA", ">=", 512.0 * w, "*", at("dyS", 1, w))
-    fill("rsw:0:256:8", 0.0)
-    scan("yI", "rsw", "st")
-    ts("oB16", "oB", "*", 16.0, "+", 8.0)
     ts("oW", "oA", ">>", 9)
-    tt("oP", "oB16", "+", "oW")
-    tt("oM", "yI:7:256:8", "min", "oP")
-    ts("own", "oM", "&", 7)
+    ts("oB16", "oy:64:128:2", "*", 16.0, "+", 8.0)
+    tt("top:7:256:8", "oB16", "+", "oW")
+    scan("yI", "st", "top", A_.add, A_.min)
+    ts("own", "yI:7:256:8", "&", 7)
 
     for q in range(N):
-        ts(at("mq", 32, q), "own", "==", float(q))
+        ts(at("mq", 32, q), "own", "==", float(q), "*", -1.0)
+    ts("o128", "own", "*", 128.0)
     fill("rs", 1.0)
     fill("rs:0:256:32", 0.0)
     scan("sc", "rs", "mq")
-    mms("p2:0:8", [("onesB", "q8:0:8"), ("lt", "sc:31:256:32")])
-    cp("mqF", "mq")
-    tt("mqF:0:256:32", "mq:0:256:32", "+", "p2:0:8")
-    scan("p1:0:256", "rs", "mqF")
-    tt("p0:0:128", "p1:0:128", "*", "mq:0:128")
-    tt("b8", "p1:128:256", "*", "mq:128:256")
-    tt("p0:128:192", "p0:0:64", "+", "b8:0:64")
-    tt("b4", "p0:64:128", "+", "b8:64:128")
-    tt("b2", "p0:128:192", "+", "b4")
-    tt("v1", "b2:0:32", "+", "b2:32:64")
-    ts("a16", "v1", "-", 1.0)
+    mms("p2:0:8", [("lt", "sc:31:256:32")])
+    scan("mine", "sc", "mq", A_.min, A_.mult)
+    keep("idn", "onesB", [[-1, 128]], "==", 0, 1)
+    begun = mms("p1:0:32", [("idn", "o128")] + [("idn", at("mine", 32, q)) for q in range(N)], stop=False)
+    for q in range(N):
+        ts(at("sb", 32, q), at("mq", 32, q), "*", at("p2", 1, q))
+    mms("p1:0:32", [("idn", at("sb", 32, q)) for q in range(N)], begun=begun)
+    ts("a16", "p1:0:32", "-", 1.0)
 
     ts("p16I:0:1", "pI:0:1", "&", 15)
     cp("p16F:0:1", "p16I:0:1")
@@ -385,8 +401,10 @@ def rank_program(g, core, T, topo):
         fill(name, 0.0)
     ts("lh:0:1", "sdI:0:1", "&", 3840)
     ts("lh:1:2", "sdI:0:1", "&", 255)
-    ts("lh:2:3", "hI:0:1", "&", 255)
-    ts("lh:3:4", "hI:0:1", "&", 3840)
+    ts("lh:2:3", "sdI:0:1", ">>", 12, "&", 255)
+    ts("hI:0:1", "sdI:0:1", ">>", 12)
+    ts("hI:1:2", "hI:0:1", "+", 2048.0)
+    ts("lh:3:4", "hI:1:2", "&", 3840)
     cp("lhF:0:3", "lh:0:3")
     ts("lhF:3:4", "lh:3:4", "+", -2048.0)
     for j, c in ((0, "lhF:0:1"), (1, "lhF:1:2"), (4, "lhF:3:4"), (5, "lhF:2:3")):
@@ -399,7 +417,7 @@ def rank_program(g, core, T, topo):
     mms("p7", [("selX", "oh"), ("ckL", "kE")])
     act("inX", "p7")
     act("be:1:32:4", "sc:31:256:32")
-    act("be:0:32:4", "p2:0:8")
+    cp("be:0:32:4", "p2:0:8")
     send("be", lambda q: at("be", 4, q), lambda r: at("beR", 4, r))
     cp("win@a16", "inX")
     act("selB:15:144:16", "g9:0:9")
@@ -439,14 +457,13 @@ def rank_program(g, core, T, topo):
     def shifts():
         ts("w6:0:1", "p16F:0:1", "<", 8.0)
         ts("w5:0:1", "p16F:0:1", ">=", 8.0)
-        keep("idn", "onesB", [[-1, 128]], "==", 0, 1)
         keep("up8", "onesB", [[-1, 128]], "==", 8, 1)
         keep("dn8", "onesB", [[-1, 128]], "==", -8, 1)
         for out, a, c in (("wI0", "idn", "w6"), ("wU", "up8", "w6"), ("wI1", "idn", "w5"), ("wD", "dn8", "w5")):
             scaled(out, a, c + ":0:1")
 
     def span(h, i, n=1):
-        return (i if h == 0 else 2 * TRY - i - n, n)
+        return (TRY - i - n if h == 0 else TRY + i, n)
 
     def R(name, s, w=32):
         return "%s:%d:%d" % (name, w * s[0], w * (s[0] + s[1]))
@@ -455,46 +472,34 @@ def rank_program(g, core, T, topo):
         return T[name][:, a:b:step, :], [(name, 32 * j, 32 * j + 32, 1) for j in range(a, b, step)]
 
     def both(name, i):
-        return units(name, i, 2 * TRY - i, 2 * TRY - 1 - 2 * i)
+        return units(name, TRY - 1 - i, TRY + 1 + i, 2 * i + 1)
 
-    def counter(i):
-        return float(1597 * (i + 1) % 4096)
-
-    def hashes(s):
-        def r(tile):
-            return R(tile, s)
-        a, b = s[0], s[0] + s[1]
-        ts(r("hL"), units("hT", a, b), "&", 4095)
-        tt(r("p0"), r("hL"), "*", r("hL"))
-        for j in range(a, b, 2):
-            tt(R("hb", (j, 2)), R("p0", (j, 2)), "+", units("H6", j // TRY * 2, j // TRY * 2 + 2))
-        ts(r("hB"), r("hb"), ">>", 6, "&", 4095)
-        tt(r("p1"), r("hB"), "*", r("hB"))
-        tt(r("ha"), r("p1"), "+", units("hL2", a, b))
-        ts(r("hA"), r("ha"), ">>", 6, "&", 4095)
-        cp(r("e16"), r("hA"))
-        ts(r("p0"), r("hB"), "*", 8192.0, "+", 4096.0 - 16777216.0)
-        tt(r("pk"), r("p0"), "+", r("hA"))
+    def hashes(i):
+        if i:
+            ts(at("hT", 64, i), "xl", "+", float(1597 * i % 4096))
+        if i < 3:
+            ts(half("ly", 128, i, 1), parts("rr", 0, 8), ">>", 7, "&", 4095 << 6)
+        square(("hb", 128, i), ("lz", 128, i % 3), ("ly", 128, i % 3), at("hT", 64, i) if i else parts("rr", 0, 8), "&", 4095)
+        ts(half("by", 128, i, 1), at("hT", 64, i) if i else half("ly", 128, 0, 0), "*", 64.0)
+        square(("ha", 128, i), ("bz", 128, i % 3), ("by", 128, i), half("hb", 128, i, 1), ">>", 6, "&", 4095)
+        ts(both("hA", i), half("ha", 128, i, 1), ">>", 6, "&", 4095)
+        ts(at("p0", 64, i), half("by", 128, i, 0), "*", 8192.0, "+", 4096.0 - 16777216.0)
+        tt(both("kp", i), at("p0", 64, i), "+", both("hA", i))
 
     def wrap(bank, sel, src, s):
         a, b = 512 * s[0], 512 * (s[0] + s[1])
         mms(R(bank, (0, s[1])), [("%s:%d:%d" % (sel, 15 - j, 143 - j), "%s:%d:%d:16" % (src, a + j, b)) for j in range(16)])
 
     def candidates(s, bank):
+        cp(R("e16", s), units("hA", s[0], s[0] + s[1]))
         act(R("tg", s, 512), "tabs@" + R("e16", s))
         wrap(bank, "selT", "tg", s)
-        tt(R("xI", s), R(bank, (0, s[1])), "min", R("pk", s))
+        tt(R("xI", s), R(bank, (0, s[1])), "min", units("kp", s[0], s[0] + s[1]))
         ts(R("cI", s), R("xI", s), "&", 4095)
         cp(R("c16", s), R("cI", s))
-        tt(R("p1", s), R("cI", s), "+", R("p6", s))
 
-    best = {}
-
-    def rival(h, i, tile):
-        if h in best:
-            tt(R("acc", span(h, i)), R(tile, span(h, i)), "max", best[h])
-            tile = "acc"
-        best[h] = R(tile, span(h, i))
+    def sixth(name, h, i):
+        return "%s:%d:%d:6" % (name, 192 * h + TRY - 1 - i, 192 * h + 192)
 
     def unseen(h, i, n, bank, scalar=()):
         for j in range(i, i + n):
@@ -507,19 +512,19 @@ def rank_program(g, core, T, topo):
         s = span(h, i, n)
         wrap(bank, "selB", "sg", s)
         ts(R("wI", s), R(bank, (0, n)), "*", -1.0)
-        ts(R("sI", s), R("wI", s), "&", 1 << 15)
-        tt(R("val", s), R("p1", s), "-", R("sI", s))
         for j in range(i, i + n):
-            rival(h, j, "val")
+            ts(sixth("d0", h, j), R("wI", span(h, j)), ">>", 15, "&", 1)
 
     def answer(h, name, cores, engines):
         def H(tile):
             return at(tile, 32, h)
-        ts(H("r"), best[h], "&", 4095)
-        cp(H("f16"), H("r"))
-        ts(H("iH"), H("r"), "+", 4096.0 * me)
-        ts(H("rq4"), H("r"), "+", 4096.0 * me)
-        tt(H("iL"), H("rq4"), "-", H("iH"))
+        ts(sixth("d1", h, 0), R("cI", span(h, 0)), "+", 4096.0 * me)
+        for i in range(1, TRY):
+            tt(sixth("d1", h, i), R("cI", span(h, i)), "-", R("cI", span(h, i - 1)))
+        scan(at("res", 192, h), at("d0", 192, h), at("d1", 192, h))
+        ts(H("f16"), sixth("res", h, 0), "-", 4096.0 * me)
+        cp(H("iH"), sixth("res", h, 0))
+        tt(H("iL"), sixth("res", h, 0), "-", H("iH"))
         mms("p7:0:32", [("wU", H("iH")), ("wI0", H("iL"))])
         mms("p7:32:64", [("wD", H("iH")), ("wI1", H("iL"))])
         for j in range(2):
@@ -529,36 +534,23 @@ def rank_program(g, core, T, topo):
             (act if q == "S" else cp)(block("rsp", T.rank_of(c), 0, 128), "vecB@" + at("f16", 8, T.rank_of(c)))
         send(name, lambda q: block("rsp", q), lambda r: at("rspR", RW, r), cores)
 
-    x = parts("rr", 0, 8)
-    ts("xl", x, "&", 8191)
-    ts("xh", x, ">>", 13)
-    cp("xlF", "xl")
+    ts("xl", parts("rr", 0, 8), "&", 8191)
     for i in range(TRY):
-        ts(both("hT", i), "xl", "+", counter(i))
-        act(both("hL2", i), "xlF", 64.0 * counter(i) - BIG, 64.0)
-    for j in range(2):
-        ts(units("H6", j, 4, 2), "xh", "*", 64.0, "+", 131072.0 - BIG)
+        hashes(i)
     iota("iotaS", [[1, 128]], 0, 0)
-    ts("nm0", "beR:1:32:4", "*", -0.5, "+", 0.5 + float(128 * me))
-    ts("ha2", "beR:1:32:4", "*", 0.5, "+", -0.25)
-    tt("nm", "nm0", "-", "beR:0:32:4")
+    ts("nm0", "beR:1:32:4", "*", 0.5, "+", 0.5)
+    ts("ha2", "beR:1:32:4", "*", -0.5, "+", -0.25)
+    tt("nm", "nm0", "+", "beR:0:32:4")
     masks(order[:4])
-    iota("rank:0:192", [[-4096, TRY], [0, 32]], 4096 * (TRY - 1), 0)
-    iota("rank:192:384", [[4096, TRY], [0, 32]], 0, 0)
-    act("p6:0:384", "rank")
-    banks = {"T": ["p2", "p5"], "S": ["p3", "p4"]}
+    banks = {"T": ["p2", "p5", "p6"], "S": ["p3", "p4", "p1"]}
     for s in PLAN.split():
-        h, i, n = {"f": far, "n": near}[s[1]], int(s[2]), int(s[3])
-        if s[0] == "H":
-            hashes(span(h, i, n))
-        elif s[0] == "T":
-            candidates(span(h, i, n), banks["T"][0])
-            banks["T"].reverse()
-            for hh in (h, 1 - h)[:max(0, i + n - TRY + 1)]:
-                rival(hh, TRY - 1, "cI")
+        h, i, n = {"f": far, "n": near, "b": 0}[s[1]], int(s[2]), int(s[3])
+        if s[0] == "T":
+            candidates((TRY - 1, 2) if s[1] == "b" else span(h, i, n), banks["T"][0])
+            banks["T"].append(banks["T"].pop(0))
         elif s[0] == "S":
             unseen(h, i, n, banks["S"][0], [int(j) for j in s[4:]])
-            banks["S"].reverse()
+            banks["S"].append(banks["S"].pop(0))
         elif s[0] == "A":
             answer(h, "far" if h == far else "near", off if h == far else on, s[4:])
         else:

@@ -8,16 +8,19 @@ BIG = float(1 << 23)
 OPS = {"+": A_.add, "-": A_.subtract, "*": A_.mult, "min": A_.min, "max": A_.max, ">=": A_.is_ge, ">": A_.is_gt, "<": A_.is_lt,
        "==": A_.is_equal, ">>": A_.arith_shift_right, "&": A_.bitwise_and}
 
-PLAN = "Tb01 Tf12 Tf32 Mf00 Sf03 Tn12 Sf32 Tn32 Tf51 Tn51 Af00SSSS Sn0312 Sn324 An00SVS"
+PLAN = "Tb01 Tf12 Tf31 Tf41 Tf51 Mf00 Sf03 Sf31 Sf41 Af00 Tn41 Tn12 Tn31 Tn51 Sn41 Sn02 Sn22 An00"
+RELAYED = ("ah", "far")
+APART = 4
+HERE = 4
 
 SMALL = {
     "bufI": ("int32", 8, "pI 8 p16I 8 sdI 128 hI 8 h64 32 lh 8 ckp 8 ckA 8 rkI 16 oT 32 oB0 64 oA0 64 oA 32 "
-             "oW 32 oB16 32 own 32 yI 256 v 32 thrI 256 aliI 256 xl 64 hT 384 hb 768 ha 768 oz 128 oy 128 lz 384 ly 384 bz 384 by 768 "
-             "xI 384 cI 384 wI 384 d0 384 d1 384 res 384 q1 32 q16 32 ps 32 mm 32 cq 32 cl 32 bl 32 b8I 32 mb 32"),
+             "oW 32 oB16 32 own 32 yI 256 v 32 thrI 256 aliI 256 xl 64 xq 64 hT 384 hb 768 ha 768 oz 128 oy 128 lz 384 ly 384 bz 384 by 768 "
+             "xI 384 cI 384 wI 384 d0 384 d1 384 res 384 q16 32 mm 32 cq 32 lI 96"),
     "bufF": ("float32", 8, "ones 128 p16F 8 n16 8 e8a 128 e8 128 g9a 16 g9 16 w2 8 w5 8 w6 8 wcol 8 c3 8 wS 8 lhF 8 ckF 8 "
-             "ya 8 yc 16 dy 8 dyS 8 st 256 top 256 be 32 beR 32 ha2 8 nm 8 nm0 8 ch1 128"),
+             "ya 8 yc 16 dy 8 dyS 8 st 256 top 256 ha2 8 nm 8 nm0 8 ch1 128"),
     "bufB": ("bfloat16", 16, "onesB 128 ones5 512 lta 128 lt 128 selB 144 selT 144 selP 144 selX 128 ckL 128 "
-             "idn 128 up8 128 dn8 128 wI0 128 wI1 128 wU 128 wD 128 iH 64 iL 64 oh8 16 o128 32 "
+             "idn 128 up8 128 dn8 128 wI0 128 wI1 128 wU 128 wD 128 iH 64 iL 64 oh8 16 o128 32 beR 64 "
              "iotaS 128 ohI 512 ohA 512 oh 512 kE 512 inX 512 rs 256 mq 256 sc 256 mine 256 sb 256 "
              "alH 256 alL 256 thH 256 thL 256 win 1024 mT 1024 mask 1024 m2 512 cm 512 ysb 512 selC 48"),
     "bufU": ("uint16", 16, "a16 32 e16 384 c16 384 f16 64 l16 96"),
@@ -37,44 +40,66 @@ for _n, _c, _type in (("seenB", 4096, "bfloat16"), ("vecB", 4096, "bfloat16"), (
 for _j in range(8):
     SCRATCH["p%d" % _j] = ("psum", [128, 512], "float32")
     TILES["p%d" % _j] = ("p%d" % _j, 0, 512)
-BLOCKS = {"rsp": RW, "rq": 8, "rr": 8}
+BLOCKS = {"rsp": RW, "rq": 8, "rr": 8, "ah": 16 * (TRY - HERE) or 8, "ar": 16 * (TRY - HERE) or 8}
 for _n, _c in BLOCKS.items():
     SCRATCH[_n] = ("sbuf", [128, N, _c], "bfloat16" if _n == "rsp" else "int32")
 for _n in ("hA", "kp"):
     SCRATCH[_n] = ("sbuf", [128, 2 * TRY, 32], "int32")
-SEMAPHORES = ("sv ss sp sg d_sd d_rk d_thr d_ali d_seen d_vec d_tab0 d_tab1 d_tab2 d_tab3 d_y d_ch "
-              "l_be l_rq l_far l_near r_be r_rq r_far r_near").split()
+SEMAPHORES = ("sv ss sp sg d_sd d_rk d_thr d_ali d_seen0 d_seen1 d_pad1 d_pad2 d_pad3 d_vec d_tab0 d_tab1 d_tab2 d_tab3 d_y d_ch "
+              "l_be l_rq l_ah l_far l_near r_be r_rq r_ah r_far r_near").split()
 
-COSTS = [dict(zip("cycle pe gather scatter call pick act pool own other dma MB issue be rq far near".split(), _row)) for _row in (
-    (0.00083, 0.00042, 0.00125, 0.0025, 0.0, 0.06, 0.2, 0.15, 0.20, 0.20, 1.3, 3.6, 0.3, 3.5, 2.3, 4.0, 2.0),
-    (0.00110, 0.00060, 0.00200, 0.0045, 0.0, 0.06, 0.25, 0.15, 0.25, 0.25, 1.6, 5.0, 0.5, 5.0, 3.5, 5.5, 3.0))]
-ROUNDS, HEAT, REACH, SEED = 80000, 0.4, 12, 1
+COSTS = [dict(zip("cycle pe gather scatter pick act pool wait dma MB issue first be rq ah far near".split(), _row)) for _row in (
+    (0.00083, 0.00042, 0.00125, 0.0025, 0.06, 0.25, 0.15, 0.20, 1.3, 3.6, 0.4, 1.0, 4.0, 2.0, 5.2, 4.5, 1.8),
+    (0.00105, 0.00053, 0.00190, 0.0047, 0.06, 0.31, 0.15, 0.25, 1.6, 5.0, 0.6, 2.5, 6.0, 3.5, 7.5, 6.5, 3.0))]
+ROUNDS, REACH, SHARE, TURN, GAIN, BAR, BACK, SEED = 20000, 8, 5, 4, 0.2, 50, 2500, 2
 KNOWN = []
 
 
-def engine_plan(core, T, topo, alone=False):
-    off = [c for c in T.cores if topo.chip(c) != topo.chip(core)]
-    on = [c for c in T.cores if topo.chip(c) == topo.chip(core) and c != core]
-    plan = {}
+def routes(core, name, T, topo):
+    here = [c for c in T.cores if topo.chip(c) == topo.chip(core)]
+    off, on = [c for c in T.cores if c not in here], [c for c in here if c != core]
     pool = topo.engines(core, off[0])
-    rest = [e for e in topo.engines(core, on[0]) if alone or e not in pool]
-    for cores, engines in ((off, pool), (on, rest)):
+    rest = [e for e in topo.engines(core, on[0]) if name == "near" or e not in pool]
+    off, on, via = ([] if name == "near" else off), ([] if name == "far" else on), {}
+    if name in RELAYED:
+        idle = [c for c in topo.cores_of(core) if topo.die(c) != topo.die(core) and c not in T.cores]
+        via[off[here.index(core)]] = idle[here.index(core)]
+    plan = {}
+    for cores, engines in (([c for c in off if c not in via], pool), (on + list(via), rest)):
         n = 1
-        while 2 * n * len(cores) <= len(engines):
+        while 2 * n * len(cores) <= len(engines) and cores:
             n *= 2
         at = 0
         for j, c in enumerate(cores):
             m = n
             if len(engines) - at - 2 * n >= n * (len(cores) - j - 1):
                 m = 2 * n
-            plan[c] = engines[at:at + m]
+            plan[c] = via.get(c, c), engines[at:at + m], len(topo.engines(via[c], c)) if c in via else m
             at += m
-    return plan, off, on
+    return {c: plan[c] for c in off + on}
+
+
+def transfer(to, engines, name, src, dst, T, topo):
+    rid, pnc, _s = topo.addr(to)
+    return RemoteDMATransfer(dst_ids=[DstId(rid=rid, pnc=pnc)], dma_engine_mask=sum(1 << e for e in engines),
+                             remote_sem=T.sem["r_" + name], srcs=[src], dsts=[dst], alu_op=0)
+
+
+def relay_program(g, core, T, topo):
+    for name in RELAYED:
+        for c in T.cores:
+            for to, (via, engines, n) in routes(c, name, T, topo).items():
+                if via == core:
+                    r = T.rank_of(c)
+                    piece = T.ar[:, r, :] if name == "ah" else T.rspR[:, RW * r:RW * r + RW]
+                    g.wait_ge(T.sem["r_" + name], len(engines))
+                    g.remote_dma_fused([transfer(to, topo.engines(core, to), name, piece, piece, T, topo)], local_sem=T.sem["l_" + name])
+                    g.wait_ge(T.sem["l_" + name], n)
 
 
 def arrange(calls):
     n = len(calls)
-    qs = [c["q"] for c in calls]
+    qs = [None] * n
     above, near = [], []
     for c in calls:
         bits, keep = 0, set()
@@ -84,54 +109,88 @@ def arrange(calls):
             bits |= above[a] | 1 << a
         above.append(bits)
         near.append(keep)
-    for order, _end in KNOWN:
+    for order, way, _end in KNOWN:
         at = {i: j for j, i in enumerate(order)}
         if len(order) == n and all(at[a] < at[i] for i in range(n) for a in near[i]):
-            return [calls[i] for i in order]
-    sets = []
-    for cost in COSTS:
-        time = [sum(cost[k] * v for k, v in c["time"].items()) for c in calls]
-        late = [sum(cost[k] * v for k, v in c["late"].items()) for c in calls]
-        edges = [[(a["n"], time[a["n"]] + (late[a["n"]] or cost["own" if a["q"] == b["q"] else "other"])) for a in b["after"]
-                  if a["n"] in near[b["n"]]] + [(a["n"], 1e-6) for a in b["behind"]] for b in calls]
-        sets.append((time, [time[i] + late[i] for i in range(n)], edges))
+            return [(calls[i], way[i]) for i in order]
+    edges = [[n + a["n"] for a in c["after"] if a["n"] in near[c["n"]]] + [a["n"] for a in c["behind"]] for c in calls]
+    way, sets = [0] * n, [([0.0] * n, [0.0] * n) for _ in COSTS]
+    users = [[] for _ in calls]
+    for i in range(n):
+        for a in edges[i]:
+            users[a % n].append((i, a >= n))
 
-    def length(order):
-        total, starts = 0.0, []
-        for time, full, edges in sets:
-            free, start, end = dict.fromkeys(qs, 0.0), [0.0] * n, 0.0
-            for i in order:
-                q = qs[i]
-                t = free[q]
-                for a, d in edges[i]:
-                    if start[a] + d > t:
-                        t = start[a] + d
-                start[i] = t
-                if q:
-                    free[q] = t + time[i]
-                if t + full[i] > end:
-                    end = t + full[i]
-            total += end
-            starts.append(start)
-        return total / len(sets), starts
+    def take(i, w):
+        way[i], qs[i] = w, calls[i]["ways"][w][0]
+        for cost, (time, full) in zip(COSTS, sets):
+            time[i] = sum(cost[k] * v for k, v in calls[i]["ways"][w][2].items()) + 1e-6
+            full[i] = time[i] + (sum(cost[k] * v for k, v in calls[i]["late"].items()) or (cost["wait"] if qs[i] else 0.0))
 
-    def holds(order, starts):
-        before, last, pairs = {}, {}, []
+    def turn(i):
+        for c in calls[i:i + 2]:
+            if c["n"] == i or c["lead"] is calls[i]:
+                take(c["n"], 1 - way[c["n"]])
+
+    def heads(order, time, full):
+        free, at, can = dict.fromkeys("VSPGY", 0.0), [0.0] * (2 * n), [0.0] * n
         for i in order:
-            before[i], last[qs[i]] = last.get(qs[i]), i
-        for (time, full, edges), start in zip(sets, starts):
-            i = max(range(n), key=lambda i: start[i] + full[i])
-            while start[i] > 0.0:
-                a = [a for a, d in edges[i] if start[a] + d >= start[i]]
-                if not a:
-                    pairs.append((i, before[i]))
-                i = a[0] if a else before[i]
-        return pairs
+            t = 0.0
+            for a in edges[i]:
+                if at[a] > t:
+                    t = at[a]
+            can[i] = t
+            q = qs[i]
+            if q:
+                if free[q] > t:
+                    t = free[q]
+                free[q] = t + time[i]
+            at[i] = t
+            at[n + i] = t + full[i]
+        return at, can
 
-    time, full, edges = sets[0]
+    def tails(order, time, full):
+        rest, left, own = dict.fromkeys("VSPGY", 0.0), [0.0] * n, [0.0] * n
+        for i in reversed(order):
+            f = t = full[i]
+            for u, after in users[i]:
+                d = left[u] + f if after else left[u]
+                if d > t:
+                    t = d
+            own[i] = t
+            q = qs[i]
+            if q:
+                if rest[q] + time[i] > t:
+                    t = rest[q] + time[i]
+                rest[q] = t
+            left[i] = t
+        return left, own
+
+    def guess(row, a, b, seq):
+        total = 0.0
+        for (at, can, left, own, time, full), end in zip(state, ends):
+            t = at[row[a - 1]] + time[row[a - 1]] if a else 0.0
+            new = []
+            for i in seq:
+                if can[i] > t:
+                    t = can[i]
+                new.append(t)
+                t += time[i]
+            t, worst = left[row[b]] if b < len(row) else 0.0, end - GAIN
+            for i, h in zip(reversed(seq), reversed(new)):
+                t += time[i]
+                if own[i] > t:
+                    t = own[i]
+                if h + t > worst:
+                    worst = h + t
+            total += worst
+        return total
+
+    for i in range(n):
+        take(i, 0)
+    time, full = sets[0]
     busy, start = {}, [0.0] * n
     for i in range(n):
-        t = max([start[a] + d for a, d in edges[i]] + [0.0])
+        t = max([start[a % n] + (full[a % n] if a >= n else 1e-6) for a in edges[i]] + [0.0])
         if qs[i]:
             for a, b in busy.setdefault(qs[i], []):
                 if t + time[i] <= a:
@@ -140,39 +199,68 @@ def arrange(calls):
             busy[qs[i]] = sorted(busy[qs[i]] + [(t, t + time[i])])
         start[i] = t
     order = sorted(range(n), key=lambda i: (start[i], i))
-    now = length(order)[0]
-    best, x, held = (now, order), SEED, []
+    best, x, barred, since = None, SEED, {}, 0
     for r in range(ROUNDS):
-        x = (x * 6364136223846793005 + 1442695040888963407) % (1 << 64)
-        p, hops, step = (x >> 48) * n >> 16, 1 + int((x >> 32 & 65535) ** 3 * REACH >> 48), (x >> 31 & 1) * 2 - 1
-        if x >> 8 & 3 and held:
-            p = order.index(held[(x >> 48) * len(held) >> 16][step > 0])
-        group, j = [order[p]], p
-        while hops and 0 <= j + step < n:
-            j += step
-            o = order[j]
-            if any((above[o] >> i & 1) if step > 0 else (above[i] >> o & 1) for i in group):
-                group.append(o)
-            elif qs[o] == qs[group[0]]:
-                hops -= 1
-        if hops or len(group) > 6 or not qs[group[0]]:
+        state = [heads(order, *s) for s in sets]
+        at0 = state[0][0]
+        order.sort(key=lambda i: at0[i])
+        ends = [max(at) for at, _can in state]
+        if best is None or sum(ends) < best[2] * len(sets) - 1e-9:
+            best, since = (list(order), list(way), sum(ends) / len(sets)), r
+        elif r - since > BACK:
+            order, since, barred = list(best[0]), r, {}
+            for i in range(n):
+                take(i, best[1][i])
             continue
-        if step > 0:
-            new = order[:p] + [o for o in order[p:j + 1] if o not in group] + group + order[j + 1:]
-        else:
-            new = order[:j] + group[::-1] + [o for o in order[j:p + 1] if o not in group] + order[p + 1:]
-        got, starts = length(new)
-        if got <= now + HEAT * (1 - r / ROUNDS) * ((x >> 16 & 32767) / 32768) ** 2:
-            now, order, held = got, sorted(new, key=lambda i: starts[0][i]), holds(new, starts)
-            if now < best[0]:
-                best = now, order
-    KNOWN.append((best[1], best[0]))
-    return [calls[i] for i in best[1]]
+        state = [h + tails(order, *s) + s for h, s in zip(state, sets)]
+        rows = {q: [i for i in order if qs[i] == q] for q in "VSPG"}
+        x = (x * 6364136223846793005 + 1442695040888963407) % (1 << 64)
+        at, can, left = state[(x >> 40) % len(sets)][:3]
+        end, moves = ends[(x >> 40) % len(sets)], []
+        for row in rows.values():
+            for j, i in enumerate(row):
+                if j and at[i] + left[i] > end - 1e-6 and can[i] < at[i] - 1e-6:
+                    x = (x * 6364136223846793005 + 1442695040888963407) % (1 << 64)
+                    if (x >> 40) % 100 >= SHARE:
+                        continue
+                    first = max([at0[a % n] for a in edges[i]] + [-1.0])
+                    for k in range(j - 1, max(-1, j - 1 - REACH), -1):
+                        if at0[row[k]] <= first:
+                            break
+                        moves.append((guess(row, k, j + 1, [i] + row[k:j]) + (barred.get((i, row[k]), 0) > r) * 99 +
+                                      (x >> k % 30 & 255) * 1e-6, i, row[k], 0))
+                    u = row[j - 1]
+                    last = min([at0[o] for o, _after in users[u]] + [1e9])
+                    for k in range(j, min(len(row), j + REACH)):
+                        if at0[row[k]] >= last:
+                            break
+                        moves.append((guess(row, j - 1, k + 1, row[j:k + 1] + [u]) + (barred.get((row[k], u), 0) > r) * 99 +
+                                      (x >> k % 30 & 255) * 1e-6, u, row[k], 1))
+                    for o in (i, u):
+                        o = calls[o]["lead"]["n"] if calls[o]["lead"] else o
+                        if len(calls[o]["ways"]) > 1 and barred.get(o, 0) <= r and not (x >> 20) % TURN:
+                            turn(o)
+                            moves.append((sum(max(heads(order, *s)[0]) for s in sets), o, o, 2))
+                            turn(o)
+        if moves:
+            _end, i, o, kind = min(moves)
+            if kind == 2:
+                turn(i)
+                barred[i] = r + 3 * BAR
+                continue
+            row = rows[qs[i]]
+            for p in (row[row.index(o):row.index(i)] if kind == 0 else row[row.index(i) + 1:row.index(o) + 1]):
+                barred[(p, i) if kind == 0 else (i, p)] = r + BAR + (x >> 30) % BAR
+            order.remove(i)
+            order.insert(order.index(o) + kind, i)
+    KNOWN.append(best)
+    return [(calls[i], best[1][i]) for i in best[0]]
 
 
 def rank_program(g, core, T, topo):
     me = T.rank_of(core)
     if me is None:
+        relay_program(g, core, T, topo)
         return
     queues = {"V": (g.vector, "sv"), "S": (g.scalar, "ss"), "P": (g.tensor, "sp"), "G": (g, "sg"), "Y": (g.sync, None)}
     V, S, P = g.vector, g.scalar, g.tensor
@@ -201,9 +289,9 @@ def rank_program(g, core, T, topo):
             return False
         return (p[3] == 1 and o[3] == 1) or bool(set(range(p[1], p[2], p[3])) & set(range(o[1], o[2], o[3])))
 
-    def add(q, emit, reads, writes, time, late=None, sem=None, inc=1, part=None, after=(), behind=()):
-        c = {"n": len(calls), "q": q, "emit": emit, "time": time, "late": late or {}, "sem": sem or queues[q][1], "inc": inc,
-             "behind": list(behind)}
+    def add(q, emit, reads, writes, time, late=None, sem=None, inc=1, part=None, after=(), behind=(), ways=None, lead=None):
+        c = {"n": len(calls), "q": q, "ways": ways or [(q, emit, time)], "late": late or {}, "sem": sem, "inc": inc,
+             "behind": list(behind), "lead": lead}
         dep = {a["n"]: a for a in after}
         for places, wr in ((reads, False), (writes, True)):
             for p in places:
@@ -236,8 +324,25 @@ def rank_program(g, core, T, topo):
             rate = 1.0
         if time is None:
             time = {rate: n, "pick": 1} if isinstance(rate, str) else \
-                {"V": {"cycle": max(64, n * rate), "call": 1}, "S": {"cycle": n, "act": 1}, "G": {"cycle": 2 * n, "pool": 1}}[q]
+                {"V": {"cycle": max(64, n * rate)}, "S": {"cycle": n, "act": 1}, "G": {"cycle": 2 * n, "pool": 1}}[q]
+        if offers:
+            offers.append((q, lambda: call(oa, *args, *more), time, reads, ow))
+            return None
         return add(q, lambda: call(oa, *args, *more), reads, ow, time)
+
+    offers = []
+
+    def either(*two, lead=None):
+        offers.append(None)
+        for c in two:
+            if c:
+                c[0](*c[1:])
+            else:
+                offers.append((None, None, {}, [], []))
+        ways = offers[1:]
+        del offers[:]
+        return add("?%d" % len(calls), None, sum((w[3] for w in ways), []), sum((w[4] for w in ways), []), None,
+                   ways=[w[:3] for w in ways], lead=lead)
 
     def ts(out, a, op, s1, op2=None, s2=None):
         run("V", V.tensor_scalar, out, [a, s1, s2], *([OPS[op]] if op2 is None else [OPS[op], OPS[op2]]), rate=0.5)
@@ -265,8 +370,14 @@ def rank_program(g, core, T, topo):
     def act(out, a, bias=0.0, scale=1.0, func=AF.Copy):
         run("S", lambda o, i: S.activation(o, i, func, bias=bias, scale=scale), out, [a])
 
-    def scaled(out, a, by):
+    def times(out, a, by):
         run("S", lambda o, i, c: S.activation(o, i, AF.Copy, scale=c), out, [a, by])
+
+    def scaled(out, a, by):
+        either((times, out, a, by), (ts, out, a, "*", by))
+
+    def move(out, a):
+        either((act, out, a), (cp, out, a))
 
     def away(out, a, by):
         run("S", lambda o, i, b: S.activation(o, i, AF.Abs, bias=b), out, [a, by])
@@ -296,26 +407,18 @@ def rank_program(g, core, T, topo):
         named[q] = add(q, lambda: queues[q][0].dma_start(oa, ia), ir, ow, {"pick": 1}, {"dma": 1, "MB": mb}, sem, 16, part, after,
                        [last] if last else [])
 
-    off, on = engine_plan(core, T, topo)[1:]
+    off, on = list(routes(core, "far", T, topo)), list(routes(core, "near", T, topo))
 
-    def send(name, src, dst, cores=None):
-        tr, reads = [], []
-        plan = engine_plan(core, T, topo, cores == on)[0]
-        for c in cores or off + on:
-            rid, pnc, _s = topo.addr(c)
-            a, r = X(src(T.rank_of(c)))
-            reads += r
-            m = 0
-            for e in plan[c]:
-                m |= 1 << e
-            tr.append(RemoteDMATransfer(dst_ids=[DstId(rid=rid, pnc=pnc)], dma_engine_mask=m, remote_sem=T.sem["r_" + name],
-                                        srcs=[a], dsts=[X(dst(me))[0]], alu_op=0))
+    def send(name, src, dst):
+        plan = routes(core, name, T, topo)
+        tr = [transfer(via, engines, name, X(src(T.rank_of(c)))[0], X(dst(me))[0], T, topo) for c, (via, engines, _n) in plan.items()]
 
         def emit():
             g.remote_dma_fused(tr, local_sem=T.sem["l_" + name])
-        named[name] = add("G", emit, reads, [], {"issue": 1}, {name: 1}, "l_" + name, sum(len(plan[c]) for c in cores or off + on))
-        add(None, None, [], [p for c in cores or off + on for p in X(dst(T.rank_of(c)))[1]], {}, {"issue": 1, name: 1},
-            "r_" + name, sum(len(engine_plan(c, T, topo, cores == on)[0][core]) for c in cores or off + on), behind=[named[name]])
+        named[name] = add("G", emit, [p for c in plan for p in X(src(T.rank_of(c)))[1]], [], {"issue": 1, "first": name == "be"},
+                          {name: 1}, "l_" + name, sum(len(engines) for _via, engines, _n in plan.values()))
+        add(None, None, [], [p for c in plan for p in X(dst(T.rank_of(c)))[1]], {}, {"issue": 1, name: 1},
+            "r_" + name, sum(routes(c, name, T, topo)[core][2] for c in plan), behind=[named[name]])
 
     def block(name, r, a=0, b=None):
         w = BLOCKS[name]
@@ -336,13 +439,14 @@ def rank_program(g, core, T, topo):
     dma("S", "8|rkI", ext(T.rk), "d_rk", 0.0)
     dma("Y", "thrI", ext(T.thr), "d_thr", 0.15)
     dma("Y", "aliI", ext(T.ali), "d_ali", 0.3)
-    dma("Y", "seenB", ext(T.seen), "d_seen", 1.2)
+    dma("Y", "seenB", ext(T.seen), "d_seen0", 1.3)
 
     step = 1597 * (TRY + 1)
     for name, c in (("ones", 1.0), ("sdI:4:128", step), ("h64", 0), ("oz:0:128:2", 0), ("win", 0.0), ("onesB", 1.0),
-                    ("ones5", 1.0), ("yc", 0.0), ("top", BIG), ("st:0:256:8", BIG), ("lz:0:384:2", 0), ("bz:0:384:2", 0),
-                    ("d0:0:384:6", 0)):
+                    ("ones5", 1.0), ("yc", 0.0), ("top", BIG), ("st:0:256:8", BIG)):
         fill(name, c)
+    for name, n in (("lz:0:384:2", 192), ("bz:0:384:2", 192), ("d0:0:384:6", 64)):
+        either((iota, name, [[0, n]], 0, 0, True), (fill, name, 0))
     iota("pI:0:1", [[0, 1]], 0, 1, True)
     keep("8|e8a", "8|ones", [[1, 128]], ">=", 0, -16)
     keep("8|e8", "8|e8a", [[-1, 128]], ">=", 15, 16)
@@ -353,8 +457,6 @@ def rank_program(g, core, T, topo):
     keep("lta", "onesB", [[16, 8], [1, 16]], ">", 0, -1)
     keep("lt", "lta", [[-16, 8], [0, 16]], ">=", 0, 1)
     keep("kE", "ones5", [[1, 32], [0, 16]], "==", 0, -1)
-    for j in range(2):
-        act(at("tabs", 1024, j), "win")
 
     scan("oT", "ones:0:32", "sdI:0:128:4", first=-BIG)
     ts("h64:0:1", "sdI:0:1", ">>", 6, "&", 4095 << 6)
@@ -367,7 +469,7 @@ def rank_program(g, core, T, topo):
     tt("8|yc:1:9", "8|ya", "+", "8|rkI:8:16")
     tt("8|dy", "8|yc:1:9", "-", "8|yc:0:8")
     mms("p3:0:8", [("8|e8", "8|dy")], True)
-    act("dyS", "p3:0:8")
+    move("dyS", "p3:0:8")
     scaled("top:0:256:8", "ones:0:32", "dyS:0:1")
     for w in range(1, N):
         ts("st:%d:256:8" % w, "oA", ">=", 512.0 * w, "*", at("dyS", 1, w))
@@ -383,6 +485,7 @@ def rank_program(g, core, T, topo):
     fill("rs", 1.0)
     fill("rs:0:256:32", 0.0)
     scan("sc", "rs", "mq")
+    send("be", lambda q: "sc:%d:%d" % (32 * q + 24, 32 * q + 32), lambda r: at("beR", 8, r))
     mms("p2:0:8", [("lt", "sc:31:256:32")])
     scan("mine", "sc", "mq", A_.min, A_.mult)
     keep("idn", "onesB", [[-1, 128]], "==", 0, 1)
@@ -395,9 +498,9 @@ def rank_program(g, core, T, topo):
     ts("p16I:0:1", "pI:0:1", "&", 15)
     cp("p16F:0:1", "p16I:0:1")
     ts("n16:0:1", "p16F:0:1", "*", -1.0)
-    away("ohA", "ohI", "n16:0:1")
-    act("oh", "ohA", 1.0, -1.0, AF.Relu)
-    for name in ("selX", "ckL", "selB", "be"):
+    either((act, "oh", "ohA", 1.0, -1.0, AF.Relu), None,
+           lead=either((away, "ohA", "ohI", "n16:0:1"), (ts, "oh", "ohI", "==", "p16F:0:1")))
+    for name in ("selX", "ckL", "selB"):
         fill(name, 0.0)
     ts("lh:0:1", "sdI:0:1", "&", 3840)
     ts("lh:1:2", "sdI:0:1", "&", 255)
@@ -415,12 +518,9 @@ def rank_program(g, core, T, topo):
     ts("ckL:2:128:16", "onesB:0:8", "*", "ckF:0:1")
     ts("ckL:3:128:16", "onesB:0:8", "*", "ckF:1:2")
     mms("p7", [("selX", "oh"), ("ckL", "kE")])
-    act("inX", "p7")
-    act("be:1:32:4", "sc:31:256:32")
-    cp("be:0:32:4", "p2:0:8")
-    send("be", lambda q: at("be", 4, q), lambda r: at("beR", 4, r))
+    move("inX", "p7")
     cp("win@a16", "inX")
-    act("selB:15:144:16", "g9:0:9")
+    move("selB:15:144:16", "g9:0:9")
     ts("c3:0:1", "p16F:0:1", ">=", 4.0, "*", 8192.0)
     ts("wS:0:1", "c3:0:1", "max", 1.0)
     scaled("selP", "selB", "wS:0:1")
@@ -428,21 +528,22 @@ def rank_program(g, core, T, topo):
     cp(parts("rq", 0, 8), "p4:0:64")
     send("rq", lambda q: block("rq", q), lambda r: block("rr", r))
     cp(block("rr", me), block("rq", me))
-    cp(at("beR", 4, me), at("be", 4, me))
+    move(at("beR", 8, me), "sc:%d:%d" % (32 * me + 24, 32 * me + 32))
 
     cp("p5:0:256", "aliI")
-    act("alH", "p5:0:256", -8.0, 1.0, AF.Relu)
+    either((act, "alH", "p5:0:256", -8.0, 1.0, AF.Relu), (ts, "alH", "p5:0:256", "-", 8.0, "max", 0.0))
     ts("p6:0:256", "thrI", "+", -2048.0)
-    act("thH", "p6:0:256", -4.0)
+    either((act, "thH", "p6:0:256", -4.0), (ts, "thH", "p6:0:256", "-", 4.0))
     tt("alL", "p5:0:256", "-", "alH")
     tt("thL", "p6:0:256", "-", "thH")
-    for j in range(2):
-        act(at("tabs", 1024, 2 + j), at("tabs", 1024, j))
+    for j in range(8):
+        either((act, at("tabs", 512, j), "ones5"), (fill, at("tabs", 512, j), 0.0) if j % 2 else (iota, at("tabs", 512, j), [[0, 512]], 0, 0))
     for j, name in ((1, "alH"), (3, "thH"), (0, "alL"), (2, "thL")):
-        dma("Y", (T.tabs[j:128:16, :], X("tabs")[1]), name, "d_tab%d" % j, 0.3, j)
-    dma("Y", "vecB", ext(T.vec), "d_vec", 1.0, after=[named["rq"]])
-    ts("w2:0:1", "p16F:0:1", ">=", 2.0, "*", 8192.0)
-    ts("wcol:0:1", "w2:0:1", "max", 1.0)
+        dma("Y", (T.tabs[4 * j:128:16, :], X("tabs")[1]), name, "d_tab%d" % j, 0.3, j)
+    ts("p16I:1:2", "pI:0:1", "&", 3)
+    ts("w2:0:1", "p16F:0:1", ">=", 8.0, "*", 8191.0)
+    ts("w2:1:2", "w2:0:1", "+", 1.0)
+    ts("wcol:0:1", "p16I:1:2", "==", 0.0, "*", "w2:1:2")
     scaled("selT", "selB", "wcol:0:1")
 
     near = me // 4
@@ -463,7 +564,9 @@ def rank_program(g, core, T, topo):
             scaled(out, a, c + ":0:1")
 
     def span(h, i, n=1):
-        return (TRY - i - n if h == 0 else TRY + i, n)
+        if i >= APART:
+            return (2 * i, 2 * n) if h == 2 else (2 * i + h, 1)
+        return (APART - 1, 2) if h == 2 else (APART - i - n if h == 0 else APART + i, n)
 
     def R(name, s, w=32):
         return "%s:%d:%d" % (name, w * s[0], w * (s[0] + s[1]))
@@ -472,110 +575,118 @@ def rank_program(g, core, T, topo):
         return T[name][:, a:b:step, :], [(name, 32 * j, 32 * j + 32, 1) for j in range(a, b, step)]
 
     def both(name, i):
-        return units(name, TRY - 1 - i, TRY + 1 + i, 2 * i + 1)
+        return units(name, APART - 1 - i, APART + 1 + i, 2 * i + 1) if i < APART else units(name, 2 * i, 2 * i + 2)
+
+    def ahead(name, i, j, h=2):
+        a, lo, hi = 16 * (i - HERE) + 8 * j, 4 * (h % 2), 4 * min(h, 1) + 4
+        return T[name][:, lo:hi, a:a + 8], parts(name, a, a + 8)[1][lo:hi]
 
     def hashes(i):
+        x, low = (parts("rr", 0, 8), "xl") if i < HERE else (parts("rq", 0, 8), "xq")
+        a, k = (both("hA", i), both("kp", i)) if i < HERE else (ahead("ah", i, 0), ahead("ah", i, 1))
         if i:
-            ts(at("hT", 64, i), "xl", "+", float(1597 * i % 4096))
-        if i < 3:
-            ts(half("ly", 128, i, 1), parts("rr", 0, 8), ">>", 7, "&", 4095 << 6)
-        square(("hb", 128, i), ("lz", 128, i % 3), ("ly", 128, i % 3), at("hT", 64, i) if i else parts("rr", 0, 8), "&", 4095)
+            ts(at("hT", 64, i), low, "+", float(1597 * i % 4096))
+        if i < 3 or i >= HERE:
+            ts(half("ly", 128, i % 3, 1), x, ">>", 7, "&", 4095 << 6)
+        square(("hb", 128, i), ("lz", 128, i % 3), ("ly", 128, i % 3), at("hT", 64, i) if i else x, "&", 4095)
         ts(half("by", 128, i, 1), at("hT", 64, i) if i else half("ly", 128, 0, 0), "*", 64.0)
         square(("ha", 128, i), ("bz", 128, i % 3), ("by", 128, i), half("hb", 128, i, 1), ">>", 6, "&", 4095)
-        ts(both("hA", i), half("ha", 128, i, 1), ">>", 6, "&", 4095)
+        ts(a, half("ha", 128, i, 1), ">>", 6, "&", 4095)
         ts(at("p0", 64, i), half("by", 128, i, 0), "*", 8192.0, "+", 4096.0 - 16777216.0)
-        tt(both("kp", i), at("p0", 64, i), "+", both("hA", i))
+        tt(k, at("p0", 64, i), "+", a)
 
     def wrap(bank, sel, src, s):
         a, b = 512 * s[0], 512 * (s[0] + s[1])
         mms(R(bank, (0, s[1])), [("%s:%d:%d" % (sel, 15 - j, 143 - j), "%s:%d:%d:16" % (src, a + j, b)) for j in range(16)])
 
-    def candidates(s, bank):
-        cp(R("e16", s), units("hA", s[0], s[0] + s[1]))
-        act(R("tg", s, 512), "tabs@" + R("e16", s))
+    def candidates(h, i, n, bank):
+        s = span(h, i, n)
+        cp(R("e16", s), units("hA", s[0], s[0] + s[1]) if i < HERE else ahead("ar", i, 0, h))
+        move(R("tg", s, 512), "tabs@" + R("e16", s))
         wrap(bank, "selT", "tg", s)
-        tt(R("xI", s), R(bank, (0, s[1])), "min", units("kp", s[0], s[0] + s[1]))
+        tt(R("xI", s), R(bank, (0, s[1])), "min", units("kp", s[0], s[0] + s[1]) if i < HERE else ahead("ar", i, 1, h))
         ts(R("cI", s), R("xI", s), "&", 4095)
-        cp(R("c16", s), R("cI", s))
+        if i < TRY - 1:
+            cp(R("c16", s), R("cI", s))
 
     def sixth(name, h, i):
-        return "%s:%d:%d:6" % (name, 192 * h + TRY - 1 - i, 192 * h + 192)
+        return "%s:%d:%d:6" % (name, 192 * (h % 2) + TRY - 1 - i, 192 * min(h, 1) + 192)
 
-    def unseen(h, i, n, bank, scalar=()):
-        for j in range(i, i + n):
-            s = span(h, j)
-            if j in scalar:
-                act(R("su", s, 512), "seenB@" + R("c16", s))
-                scan(R("sg", s, 512), R("su", s, 512), at("mask", 512, h), A_.max, A_.mult)
-            else:
-                tt(R("sg", s, 512), "seenB@" + R("c16", s), "*", at("mask", 512, h))
+    def unseen(h, i, n, bank):
+        for j, k in [(j, h) for j in range(i, i + n)] if h < 2 else [(i, far), (i, near)]:
+            s = span(k, j)
+            either(None, (scan, R("sg", s, 512), R("su", s, 512), at("mask", 512, k), A_.max, A_.mult),
+                   lead=either((tt, R("sg", s, 512), "seenB@" + R("c16", s), "*", at("mask", 512, k)),
+                               (act, R("su", s, 512), "seenB@" + R("c16", s))))
         s = span(h, i, n)
         wrap(bank, "selB", "sg", s)
-        ts(R("wI", s), R(bank, (0, n)), "*", -1.0)
+        ts(R("wI", s), R(bank, (0, s[1])), "*", -1.0)
         for j in range(i, i + n):
             ts(sixth("d0", h, j), R("wI", span(h, j)), ">>", 15, "&", 1)
 
-    def answer(h, name, cores, engines):
+    def answer(h, name, cores):
         def H(tile):
             return at(tile, 32, h)
-        ts(sixth("d1", h, 0), R("cI", span(h, 0)), "+", 4096.0 * me)
+        if h == far:
+            ts(sixth("d1", 2, 0), R("cI", span(2, 0)), "+", 4096.0 * me)
         for i in range(1, TRY):
             tt(sixth("d1", h, i), R("cI", span(h, i)), "-", R("cI", span(h, i - 1)))
         scan(at("res", 192, h), at("d0", 192, h), at("d1", 192, h))
         ts(H("f16"), sixth("res", h, 0), "-", 4096.0 * me)
         cp(H("iH"), sixth("res", h, 0))
         tt(H("iL"), sixth("res", h, 0), "-", H("iH"))
-        mms("p7:0:32", [("wU", H("iH")), ("wI0", H("iL"))])
-        mms("p7:32:64", [("wD", H("iH")), ("wI1", H("iL"))])
-        for j in range(2):
-            cp((T["rsp"][:, 4 * h:4 * h + 4, 128 + 8 * j:136 + 8 * j], parts("rsp", 128 + 8 * j, 136 + 8 * j)[1][4 * h:4 * h + 4]),
-               at("p7", 32, j))
-        for c, q in zip(cores, engines):
-            (act if q == "S" else cp)(block("rsp", T.rank_of(c), 0, 128), "vecB@" + at("f16", 8, T.rank_of(c)))
-        send(name, lambda q: block("rsp", q), lambda r: at("rspR", RW, r), cores)
+        mms("p7:0:64:2", [("wU", H("iH")), ("wI0", H("iL"))])
+        mms("p7:1:64:2", [("wD", H("iH")), ("wI1", H("iL"))])
+        move((T["rsp"][:, 4 * h:4 * h + 4, 128:RW], parts("rsp", 128, RW)[1][4 * h:4 * h + 4]), "p7:0:64")
+        for c in cores:
+            move(block("rsp", T.rank_of(c), 0, 128), "vecB@" + at("f16", 8, T.rank_of(c)))
+        send(name, lambda q: block("rsp", q), lambda r: at("rspR", RW, r))
 
+    if HERE < TRY:
+        ts("xq", parts("rq", 0, 8), "&", 8191)
+        for i in range(HERE, TRY):
+            hashes(i)
+        send("ah", lambda q: block("ah", q), lambda r: block("ar", r))
+        cp(block("ar", me), block("ah", me))
+    dma("Y", "vecB", ext(T.vec), "d_vec", 1.0, after=[named["ah" if HERE < TRY else "rq"]])
     ts("xl", parts("rr", 0, 8), "&", 8191)
-    for i in range(TRY):
+    for i in range(HERE):
         hashes(i)
     iota("iotaS", [[1, 128]], 0, 0)
-    ts("nm0", "beR:1:32:4", "*", 0.5, "+", 0.5)
-    ts("ha2", "beR:1:32:4", "*", -0.5, "+", -0.25)
-    tt("nm", "nm0", "+", "beR:0:32:4")
+    mms("p3:0:8", [("lt", "beR:7:64:8")])
+    ts("nm0", "beR:7:64:8", "*", 0.5, "+", 0.5)
+    ts("ha2", "beR:7:64:8", "*", -0.5, "+", -0.25)
+    tt("nm", "p3:0:8", "+", "nm0")
     masks(order[:4])
     banks = {"T": ["p2", "p5", "p6"], "S": ["p3", "p4", "p1"]}
     for s in PLAN.split():
-        h, i, n = {"f": far, "n": near, "b": 0}[s[1]], int(s[2]), int(s[3])
+        h, i, n = {"f": far, "n": near, "b": 2}[s[1]], int(s[2]), int(s[3])
         if s[0] == "T":
-            candidates((TRY - 1, 2) if s[1] == "b" else span(h, i, n), banks["T"][0])
+            candidates(h, i, n, banks["T"][0])
             banks["T"].append(banks["T"].pop(0))
         elif s[0] == "S":
-            unseen(h, i, n, banks["S"][0], [int(j) for j in s[4:]])
+            unseen(h, i, n, banks["S"][0])
             banks["S"].append(banks["S"].pop(0))
         elif s[0] == "A":
-            answer(h, "far" if h == far else "near", off if h == far else on, s[4:])
+            answer(h, "far" if h == far else "near", off if h == far else on)
         else:
             masks(order[4:])
             shifts()
-    act("rspR:%d:%d" % (RW * me, RW * me + 128), "vecB@" + at("f16", 8, me))
-    cp("rspR:%d:%d" % (RW * me + 128, RW * me + RW), block("rsp", me, 128, RW))
+    move("rspR:%d:%d" % (RW * me, RW * me + 128), "vecB@" + at("f16", 8, me))
+    move("rspR:%d:%d" % (RW * me + 128, RW * me + RW), block("rsp", me, 128, RW))
 
     fill("selC", 0.0)
-    act("selC:3:35:4", "g9:0:8")
+    move("selC:3:35:4", "g9:0:8")
     tt("oh8:0:8", "oh:0:8", "+", "oh:8:16")
     cp("v", "a16")
-    ts("q1", "v", ">>", 7)
-    ts("mm", "v", ">>", 4, "&", 7)
-    ts("bl", "v", "&", 7)
-    ts("b8I", "v", "&", 8)
-    ts("q16", "q1", "*", float(RW - 128))
-    ts("cq", "q1", "*", float(RW), "+", 128.0)
-    tt("mb", "mm", "+", "b8I")
-    tt("ps", "v", "+", "q16")
-    cp("l16:64:96", "bl")
-    tt("cl", "cq", "+", "mb")
-    cp("l16:0:32", "ps")
-    cp("l16:32:64", "cl")
-    cp("m2", "oh8:0:8@l16:64:96")
+    ts("lI:64:96", "v", "&", 7)
+    ts("mm", "v", ">>", 3, "&", 15)
+    ts("q16", "own", "*", float(RW - 128))
+    ts("cq", "own", "*", float(RW), "+", 128.0)
+    tt("lI:0:32", "v", "+", "q16")
+    tt("lI:32:64", "cq", "+", "mm")
+    cp("l16", "lI")
+    move("m2", "oh8:0:8@l16:64:96")
 
     act("ysb", "rspR@l16:0:32")
     dma("Y", ext(T.y), "ysb", "d_y", 0.1)
@@ -586,16 +697,19 @@ def rank_program(g, core, T, topo):
     dma("S", ext(T.chosen), "32|ch1", "d_ch", 0.0)
 
     count, waited = {}, {q: {} for q in queues}
-    for c in arrange(calls):
-        if c["q"] is not None:
+    for c, way in arrange(calls):
+        q, emit = c["ways"][way][:2]
+        if q is not None:
+            c["sem"] = c["sem"] or queues[q][1]
             need = {}
             for a in c["after"]:
-                need[a["sem"]] = max(need.get(a["sem"], 0), a["count"])
+                if a["sem"]:
+                    need[a["sem"]] = max(need.get(a["sem"], 0), a["count"])
             for s in sorted(need):
-                if waited[c["q"]].get(s, 0) < need[s]:
-                    queues[c["q"]][0].wait_ge(T.sem[s], need[s])
-                    waited[c["q"]][s] = need[s]
-            done = c["emit"]()
+                if waited[q].get(s, 0) < need[s]:
+                    queues[q][0].wait_ge(T.sem[s], need[s])
+                    waited[q][s] = need[s]
+            done = emit()
             if done is not None:
                 done.then_inc(T.sem[c["sem"]], c["inc"])
         c["count"] = count[c["sem"]] = count.get(c["sem"], 0) + c["inc"]

@@ -3,27 +3,27 @@ from concourse.mybir import AluOpType as A_, ActivationFunctionType as AF
 
 N = 8
 TRY = 6
-RW = 144
+RW = 128
 BIG = float(1 << 23)
 OPS = {"+": A_.add, "-": A_.subtract, "*": A_.mult, "min": A_.min, "max": A_.max, ">=": A_.is_ge, ">": A_.is_gt, "<": A_.is_lt,
        "==": A_.is_equal, ">>": A_.arith_shift_right, "&": A_.bitwise_and}
 
-PLAN = "Tb01 Tf12 Tf31 Tf41 Tf51 Mf00 Sf03 Sf31 Sf41 Af00 Tn41 Tn12 Tn31 Tn51 Sn41 Sn02 Sn22 An00"
-RELAYED = ("ah", "far")
-APART = 4
+PLAN = "Tb01 Tf12 Tf41v Tf31 Tn12 Mf00 Sf01 Sf12 Tf51 Sf323 Tn41 Sn01 Tn31 Af00 Tn51 Sn1212 Sn323 An00"
+RELAYED = ("ah5", "far")
+APART = 6
 HERE = 4
 
 SMALL = {
     "bufI": ("int32", 8, "pI 8 p16I 8 sdI 128 hI 8 h64 32 lh 8 ckp 8 ckA 8 rkI 16 oT 32 oB0 64 oA0 64 oA 32 "
-             "oW 32 oB16 32 own 32 yI 256 v 32 thrI 256 aliI 256 xl 64 xq 64 hT 384 hb 768 ha 768 oz 128 oy 128 lz 384 ly 384 bz 384 by 768 "
-             "xI 384 cI 384 wI 384 d0 384 d1 384 res 384 q16 32 mm 32 cq 32 lI 96"),
-    "bufF": ("float32", 8, "ones 128 p16F 8 n16 8 e8a 128 e8 128 g9a 16 g9 16 w2 8 w5 8 w6 8 wcol 8 c3 8 wS 8 lhF 8 ckF 8 "
-             "ya 8 yc 16 dy 8 dyS 8 st 256 top 256 ha2 8 nm 8 nm0 8 ch1 128"),
+             "oW 32 oB16 32 own 64 yI 288 v 32 thrI 256 aliI 256 xl 64 xq 64 hT 384 hb 768 ha 768 oz 128 oy 128 lz 384 ly 384 bz 384 by 768 "
+             "xI 384 cI 384 wI 384 d0 384 d1 384 res 384 lI 64"),
+    "bufF": ("float32", 8, "ones 128 p16F 8 n16 8 e8a 128 e8 128 g9a 16 g9 16 w2 8 wcol 8 c3 8 wS 8 lhF 8 ckF 8 "
+             "ya 8 yc 16 dy 8 dyS 8 st 288 top 288 mine 256 sb 256 least 256 ha2 8 nm 8 nm0 8 item 64 itemR 64 ch1 128"),
     "bufB": ("bfloat16", 16, "onesB 128 ones5 512 lta 128 lt 128 selB 144 selT 144 selP 144 selX 128 ckL 128 "
-             "idn 128 up8 128 dn8 128 wI0 128 wI1 128 wU 128 wD 128 iH 64 iL 64 oh8 16 o128 32 beR 64 "
-             "iotaS 128 ohI 512 ohA 512 oh 512 kE 512 inX 512 rs 256 mq 256 sc 256 mine 256 sb 256 "
-             "alH 256 alL 256 thH 256 thL 256 win 1024 mT 1024 mask 1024 m2 512 cm 512 ysb 512 selC 48"),
-    "bufU": ("uint16", 16, "a16 32 e16 384 c16 384 f16 64 l16 96"),
+             "idn 128 q8 16 beR 64 q4k 32 iotaS 128 ohI 512 ohA 512 oh 512 kE 512 inX 512 rs 256 mq 256 sc 256 rs8 256 "
+             "alH 256 alL 256 thH 256 thL 256 win 1024 mT 1024 mask 1024 m2 512 ysb 512"),
+    "bufH": ("float16", 16, "cm 512 selC 48"),
+    "bufU": ("uint16", 16, "a16 32 e16 384 c16 384 f16 64 l16 64"),
 }
 SCRATCH = {}
 TILES = {}
@@ -40,18 +40,18 @@ for _n, _c, _type in (("seenB", 4096, "bfloat16"), ("vecB", 4096, "bfloat16"), (
 for _j in range(8):
     SCRATCH["p%d" % _j] = ("psum", [128, 512], "float32")
     TILES["p%d" % _j] = ("p%d" % _j, 0, 512)
-BLOCKS = {"rsp": RW, "rq": 8, "rr": 8, "ah": 16 * (TRY - HERE) or 8, "ar": 16 * (TRY - HERE) or 8}
+BLOCKS = {"rsp": RW, "rq": 8, "rr": 8, "ah4": 16, "ar4": 16, "ah5": 16, "ar5": 16}
 for _n, _c in BLOCKS.items():
     SCRATCH[_n] = ("sbuf", [128, N, _c], "bfloat16" if _n == "rsp" else "int32")
 for _n in ("hA", "kp"):
     SCRATCH[_n] = ("sbuf", [128, 2 * TRY, 32], "int32")
-SEMAPHORES = ("sv ss sp sg d_sd d_rk d_thr d_ali d_seen0 d_seen1 d_pad1 d_pad2 d_pad3 d_vec d_tab0 d_tab1 d_tab2 d_tab3 d_y d_ch "
-              "l_be l_rq l_ah l_far l_near r_be r_rq r_ah r_far r_near").split()
+SEMAPHORES = ("sv ss sp sg d_sd d_rk d_thr d_ali d_seen0 d_vec d_tab0 d_tab1 d_tab2 d_tab3 d_y0 d_ch "
+              "l_be l_rq l_ah4 l_ah5 l_far l_fari l_neari l_near r_be r_rq r_ah4 r_ah5 r_far r_fari r_neari r_near").split()
 
-COSTS = [dict(zip("cycle pe gather scatter pick act pool wait dma MB issue first be rq ah far near".split(), _row)) for _row in (
-    (0.00083, 0.00042, 0.00125, 0.0025, 0.06, 0.25, 0.15, 0.20, 1.3, 3.6, 0.4, 1.0, 4.0, 2.0, 5.2, 4.5, 1.8),
-    (0.00105, 0.00053, 0.00190, 0.0047, 0.06, 0.31, 0.15, 0.25, 1.6, 5.0, 0.6, 2.5, 6.0, 3.5, 7.5, 6.5, 3.0))]
-ROUNDS, REACH, SHARE, TURN, GAIN, BAR, BACK, SEED = 20000, 8, 5, 4, 0.2, 50, 2500, 2
+COSTS = [dict(zip("cycle pe gather scatter pick act pool own other dma MB issue first be rq ah4 ah5 far near fari neari".split(), _row)) for _row in (
+    (0.00083, 0.00042, 0.00125, 0.0025, 0.06, 0.22, 0.15, 0.18, 0.27, 1.4, 3.6, 0.5, 1.0, 3.6, 1.8, 2.8, 6.2, 4.7, 1.5, 1.9, 1.2),
+    (0.00105, 0.00053, 0.00180, 0.0042, 0.06, 0.31, 0.15, 0.23, 0.32, 1.7, 5.0, 1.0, 2.5, 5.6, 2.7, 4.0, 8.2, 6.4, 2.3, 2.8, 1.8))]
+ROUNDS, REACH, SHARE, TURN, GAIN, BAR, BACK, SEED = 20000, 8, 5, 4, 0.2, 50, 2500, 4
 KNOWN = []
 
 
@@ -59,8 +59,10 @@ def routes(core, name, T, topo):
     here = [c for c in T.cores if topo.chip(c) == topo.chip(core)]
     off, on = [c for c in T.cores if c not in here], [c for c in here if c != core]
     pool = topo.engines(core, off[0])
-    rest = [e for e in topo.engines(core, on[0]) if name == "near" or e not in pool]
-    off, on, via = ([] if name == "near" else off), ([] if name == "far" else on), {}
+    rest = [e for e in topo.engines(core, on[0]) if e not in pool]
+    if name[:4] == "near":
+        rest = rest + pool[:len(pool) // 2]
+    off, on, via = ([] if name[:4] == "near" else off), ([] if name[:3] == "far" else on), {}
     if name in RELAYED:
         idle = [c for c in topo.cores_of(core) if topo.die(c) != topo.die(core) and c not in T.cores]
         via[off[here.index(core)]] = idle[here.index(core)]
@@ -91,7 +93,7 @@ def relay_program(g, core, T, topo):
             for to, (via, engines, n) in routes(c, name, T, topo).items():
                 if via == core:
                     r = T.rank_of(c)
-                    piece = T.ar[:, r, :] if name == "ah" else T.rspR[:, RW * r:RW * r + RW]
+                    piece = T.ar5[:, r, :] if name == "ah5" else T.rspR[:, RW * r:RW * r + RW]
                     g.wait_ge(T.sem["r_" + name], len(engines))
                     g.remote_dma_fused([transfer(to, topo.engines(core, to), name, piece, piece, T, topo)], local_sem=T.sem["l_" + name])
                     g.wait_ge(T.sem["l_" + name], n)
@@ -114,17 +116,22 @@ def arrange(calls):
         if len(order) == n and all(at[a] < at[i] for i in range(n) for a in near[i]):
             return [(calls[i], way[i]) for i in order]
     edges = [[n + a["n"] for a in c["after"] if a["n"] in near[c["n"]]] + [a["n"] for a in c["behind"]] for c in calls]
-    way, sets = [0] * n, [([0.0] * n, [0.0] * n) for _ in COSTS]
+    way, sets = [0] * n, [([0.0] * n, [0.0] * (3 * n)) for _ in COSTS]
     users = [[] for _ in calls]
     for i in range(n):
         for a in edges[i]:
-            users[a % n].append((i, a >= n))
+            users[a % n].append((i, a))
 
     def take(i, w):
         way[i], qs[i] = w, calls[i]["ways"][w][0]
         for cost, (time, full) in zip(COSTS, sets):
             time[i] = sum(cost[k] * v for k, v in calls[i]["ways"][w][2].items()) + 1e-6
-            full[i] = time[i] + (sum(cost[k] * v for k, v in calls[i]["late"].items()) or (cost["wait"] if qs[i] else 0.0))
+            late = sum(cost[k] * v for k, v in calls[i]["late"].items())
+            full[n + i] = time[i] + (late or (cost["other"] if qs[i] else 0.0))
+            full[2 * n + i] = time[i] + (late or (cost["own"] if qs[i] else 0.0))
+        for j in [i] + [a % n for a in edges[i]] + [u for u, _a in users[i]]:
+            edges[j] = [a if a < n else a % n + (2 * n if qs[a % n] == qs[j] else n) for a in edges[j]]
+            users[j] = [(u, a if a < n else j + (2 * n if qs[u] == qs[j] else n)) for u, a in users[j]]
 
     def turn(i):
         for c in calls[i:i + 2]:
@@ -132,7 +139,7 @@ def arrange(calls):
                 take(c["n"], 1 - way[c["n"]])
 
     def heads(order, time, full):
-        free, at, can = dict.fromkeys("VSPGY", 0.0), [0.0] * (2 * n), [0.0] * n
+        free, at, can = dict.fromkeys("VSPGY", 0.0), [0.0] * (3 * n), [0.0] * n
         for i in order:
             t = 0.0
             for a in edges[i]:
@@ -145,17 +152,17 @@ def arrange(calls):
                     t = free[q]
                 free[q] = t + time[i]
             at[i] = t
-            at[n + i] = t + full[i]
+            at[n + i] = t + full[n + i]
+            at[2 * n + i] = t + full[2 * n + i]
         return at, can
 
     def tails(order, time, full):
         rest, left, own = dict.fromkeys("VSPGY", 0.0), [0.0] * n, [0.0] * n
         for i in reversed(order):
-            f = t = full[i]
-            for u, after in users[i]:
-                d = left[u] + f if after else left[u]
-                if d > t:
-                    t = d
+            t = full[n + i]
+            for u, a in users[i]:
+                if left[u] + full[a] > t:
+                    t = left[u] + full[a]
             own[i] = t
             q = qs[i]
             if q:
@@ -186,11 +193,11 @@ def arrange(calls):
         return total
 
     for i in range(n):
-        take(i, 0)
+        take(i, calls[i].get("first", 0))
     time, full = sets[0]
     busy, start = {}, [0.0] * n
     for i in range(n):
-        t = max([start[a % n] + (full[a % n] if a >= n else 1e-6) for a in edges[i]] + [0.0])
+        t = max([start[a % n] + (full[a] or 1e-6) for a in edges[i]] + [0.0])
         if qs[i]:
             for a, b in busy.setdefault(qs[i], []):
                 if t + time[i] <= a:
@@ -416,7 +423,8 @@ def rank_program(g, core, T, topo):
         def emit():
             g.remote_dma_fused(tr, local_sem=T.sem["l_" + name])
         named[name] = add("G", emit, [p for c in plan for p in X(src(T.rank_of(c)))[1]], [], {"issue": 1, "first": name == "be"},
-                          {name: 1}, "l_" + name, sum(len(engines) for _via, engines, _n in plan.values()))
+                          {name: 1}, "l_" + name, sum(len(engines) for _via, engines, _n in plan.values()),
+                          behind=[named[name + "i"]] if name + "i" in named else [])
         add(None, None, [], [p for c in plan for p in X(dst(T.rank_of(c)))[1]], {}, {"issue": 1, name: 1},
             "r_" + name, sum(routes(c, name, T, topo)[core][2] for c in plan), behind=[named[name]])
 
@@ -443,7 +451,7 @@ def rank_program(g, core, T, topo):
 
     step = 1597 * (TRY + 1)
     for name, c in (("ones", 1.0), ("sdI:4:128", step), ("h64", 0), ("oz:0:128:2", 0), ("win", 0.0), ("onesB", 1.0),
-                    ("ones5", 1.0), ("yc", 0.0), ("top", BIG), ("st:0:256:8", BIG)):
+                    ("ones5", 1.0), ("yc", 0.0), ("top", BIG), ("st:0:288:9", BIG), ("st:8:288:9", 4.0)):
         fill(name, c)
     for name, n in (("lz:0:384:2", 192), ("bz:0:384:2", 192), ("d0:0:384:6", 64)):
         either((iota, name, [[0, n]], 0, 0, True), (fill, name, 0))
@@ -464,36 +472,40 @@ def rank_program(g, core, T, topo):
     square(("oB0", 64, 0), ("oz", 64, 0), ("oy", 64, 0), "oT", "&", 4095)
     ts("oy:65:128:2", "oy:0:64:2", "*", 64.0)
     square(("oA0", 64, 0), ("oz", 64, 1), ("oy", 64, 1), "oB0:1:64:2", ">>", 6, "&", 4095)
-    ts("oA", "oA0:1:64:2", ">>", 6, "&", 4095)
+    ts("oW", "oA0:1:64:2", ">>", 15, "&", 7)
     ts("8|ya", "8|rkI:0:8", "*", 16.0)
     tt("8|yc:1:9", "8|ya", "+", "8|rkI:8:16")
     tt("8|dy", "8|yc:1:9", "-", "8|yc:0:8")
     mms("p3:0:8", [("8|e8", "8|dy")], True)
     move("dyS", "p3:0:8")
-    scaled("top:0:256:8", "ones:0:32", "dyS:0:1")
+    scaled("top:0:288:9", "ones:0:32", "dyS:0:1")
     for w in range(1, N):
-        ts("st:%d:256:8" % w, "oA", ">=", 512.0 * w, "*", at("dyS", 1, w))
-    ts("oW", "oA", ">>", 9)
+        ts("st:%d:288:9" % w, "oW", ">=", float(w), "*", at("dyS", 1, w))
     ts("oB16", "oy:64:128:2", "*", 16.0, "+", 8.0)
-    tt("top:7:256:8", "oB16", "+", "oW")
+    tt("top:7:288:9", "oB16", "+", "oW")
     scan("yI", "st", "top", A_.add, A_.min)
-    ts("own", "yI:7:256:8", "&", 7)
+    ts("own:0:32", "yI:7:288:9", "&", 7)
+    ts("own:32:64", "yI:8:288:9", "&", 7)
 
-    for q in range(N):
-        ts(at("mq", 32, q), "own", "==", float(q), "*", -1.0)
-    ts("o128", "own", "*", 128.0)
+    for q in range(N // 2):
+        ts(at("mq", 64, q), "own", "==", float(q), "*", -1.0)
+    for q in range(N // 2):
+        ts(at("p0", 64, q), "own", "==", float(q), "*", -4096.0)
     fill("rs", 1.0)
     fill("rs:0:256:32", 0.0)
     scan("sc", "rs", "mq")
-    send("be", lambda q: "sc:%d:%d" % (32 * q + 24, 32 * q + 32), lambda r: at("beR", 8, r))
-    mms("p2:0:8", [("lt", "sc:31:256:32")])
-    scan("mine", "sc", "mq", A_.min, A_.mult)
-    keep("idn", "onesB", [[-1, 128]], "==", 0, 1)
-    begun = mms("p1:0:32", [("idn", "o128")] + [("idn", at("mine", 32, q)) for q in range(N)], stop=False)
+    def counts(q):
+        return "sc:%d:%d" % (64 * (q % 4) + 32 * (q // 4) + 24, 64 * (q % 4) + 32 * (q // 4) + 32)
+    send("be", counts, lambda r: at("beR", 8, r))
+    iota("q8:0:8", [[-1, 4], [-4, 2]], 0, 0)
+    mms("p2:0:8", [("onesB", "q8:0:8"), ("lt", "sc:31:256:32")])
+    tt("mine", "p0:0:256", "+", "sc")
     for q in range(N):
-        ts(at("sb", 32, q), at("mq", 32, q), "*", at("p2", 1, q))
-    mms("p1:0:32", [("idn", at("sb", 32, q)) for q in range(N)], begun=begun)
-    ts("a16", "p1:0:32", "-", 1.0)
+        ts("sb:%d:256:8" % q, at("mine", 32, q), "+", at("p2", 1, q))
+    fill("rs8", 1.0)
+    fill("rs8:0:256:8", 0.0)
+    scan("least", "rs8", "sb", A_.mult, A_.min)
+    ts("a16", "least:7:256:8", "*", -1.0, "-", 4097.0)
 
     ts("p16I:0:1", "pI:0:1", "&", 15)
     cp("p16F:0:1", "p16I:0:1")
@@ -528,7 +540,7 @@ def rank_program(g, core, T, topo):
     cp(parts("rq", 0, 8), "p4:0:64")
     send("rq", lambda q: block("rq", q), lambda r: block("rr", r))
     cp(block("rr", me), block("rq", me))
-    move(at("beR", 8, me), "sc:%d:%d" % (32 * me + 24, 32 * me + 32))
+    move(at("beR", 8, me), counts(me))
 
     cp("p5:0:256", "aliI")
     either((act, "alH", "p5:0:256", -8.0, 1.0, AF.Relu), (ts, "alH", "p5:0:256", "-", 8.0, "max", 0.0))
@@ -555,17 +567,9 @@ def rank_program(g, core, T, topo):
             away(at("mT", 128, r), "iotaS", at("nm", 1, r))
             ts(at("mask", 128, r), at("mT", 128, r), "<", at("ha2", 1, r), "*", -float(2 ** (15 - r)))
 
-    def shifts():
-        ts("w6:0:1", "p16F:0:1", "<", 8.0)
-        ts("w5:0:1", "p16F:0:1", ">=", 8.0)
-        keep("up8", "onesB", [[-1, 128]], "==", 8, 1)
-        keep("dn8", "onesB", [[-1, 128]], "==", -8, 1)
-        for out, a, c in (("wI0", "idn", "w6"), ("wU", "up8", "w6"), ("wI1", "idn", "w5"), ("wD", "dn8", "w5")):
-            scaled(out, a, c + ":0:1")
-
     def span(h, i, n=1):
         if i >= APART:
-            return (2 * i, 2 * n) if h == 2 else (2 * i + h, 1)
+            return 2 * APART + (TRY - APART) * h + i - APART, n
         return (APART - 1, 2) if h == 2 else (APART - i - n if h == 0 else APART + i, n)
 
     def R(name, s, w=32):
@@ -578,8 +582,8 @@ def rank_program(g, core, T, topo):
         return units(name, APART - 1 - i, APART + 1 + i, 2 * i + 1) if i < APART else units(name, 2 * i, 2 * i + 2)
 
     def ahead(name, i, j, h=2):
-        a, lo, hi = 16 * (i - HERE) + 8 * j, 4 * (h % 2), 4 * min(h, 1) + 4
-        return T[name][:, lo:hi, a:a + 8], parts(name, a, a + 8)[1][lo:hi]
+        name, lo, hi = name + str(i), 4 * (h % 2), 4 * min(h, 1) + 4
+        return T[name][:, lo:hi, 8 * j:8 * j + 8], parts(name, 8 * j, 8 * j + 8)[1][lo:hi]
 
     def hashes(i):
         x, low = (parts("rr", 0, 8), "xl") if i < HERE else (parts("rq", 0, 8), "xq")
@@ -628,27 +632,23 @@ def rank_program(g, core, T, topo):
         def H(tile):
             return at(tile, 32, h)
         if h == far:
-            ts(sixth("d1", 2, 0), R("cI", span(2, 0)), "+", 4096.0 * me)
+            cp(sixth("d1", 2, 0), R("cI", span(2, 0)))
         for i in range(1, TRY):
             tt(sixth("d1", h, i), R("cI", span(h, i)), "-", R("cI", span(h, i - 1)))
         scan(at("res", 192, h), at("d0", 192, h), at("d1", 192, h))
-        ts(H("f16"), sixth("res", h, 0), "-", 4096.0 * me)
-        cp(H("iH"), sixth("res", h, 0))
-        tt(H("iL"), sixth("res", h, 0), "-", H("iH"))
-        mms("p7:0:64:2", [("wU", H("iH")), ("wI0", H("iL"))])
-        mms("p7:1:64:2", [("wD", H("iH")), ("wI1", H("iL"))])
-        move((T["rsp"][:, 4 * h:4 * h + 4, 128:RW], parts("rsp", 128, RW)[1][4 * h:4 * h + 4]), "p7:0:64")
+        cp(H("f16"), sixth("res", h, 0))
+        ts(H("item"), sixth("res", h, 0), "-", 2048.0)
         for c in cores:
-            move(block("rsp", T.rank_of(c), 0, 128), "vecB@" + at("f16", 8, T.rank_of(c)))
+            move(block("rsp", T.rank_of(c)), "vecB@" + at("f16", 8, T.rank_of(c)))
+        send(name + "i", lambda q: at("item", 8, q), lambda r: at("itemR", 8, r))
         send(name, lambda q: block("rsp", q), lambda r: at("rspR", RW, r))
 
-    if HERE < TRY:
-        ts("xq", parts("rq", 0, 8), "&", 8191)
-        for i in range(HERE, TRY):
-            hashes(i)
-        send("ah", lambda q: block("ah", q), lambda r: block("ar", r))
-        cp(block("ar", me), block("ah", me))
-    dma("Y", "vecB", ext(T.vec), "d_vec", 1.0, after=[named["ah" if HERE < TRY else "rq"]])
+    ts("xq", parts("rq", 0, 8), "&", 8191)
+    for i in range(HERE, TRY):
+        hashes(i)
+        send("ah%d" % i, lambda q: block("ah%d" % i, q), lambda r: block("ar%d" % i, r))
+        cp(block("ar%d" % i, me), block("ah%d" % i, me))
+    dma("Y", "vecB", ext(T.vec), "d_vec", 1.0, after=[named["ah4"], named["ah5"]])
     ts("xl", parts("rr", 0, 8), "&", 8191)
     for i in range(HERE):
         hashes(i)
@@ -663,36 +663,37 @@ def rank_program(g, core, T, topo):
         h, i, n = {"f": far, "n": near, "b": 2}[s[1]], int(s[2]), int(s[3])
         if s[0] == "T":
             candidates(h, i, n, banks["T"][0])
+            [c for c in calls if len(c["ways"]) > 1][-1]["first"] = len(s) - 4
             banks["T"].append(banks["T"].pop(0))
         elif s[0] == "S":
             unseen(h, i, n, banks["S"][0])
+            for j, c in enumerate([c for c in calls if len(c["ways"]) > 1][-2 * n:]):
+                c["first"] = int(str(i + j // 2) in s[4:])
             banks["S"].append(banks["S"].pop(0))
         elif s[0] == "A":
             answer(h, "far" if h == far else "near", off if h == far else on)
         else:
             masks(order[4:])
-            shifts()
-    move("rspR:%d:%d" % (RW * me, RW * me + 128), "vecB@" + at("f16", 8, me))
-    move("rspR:%d:%d" % (RW * me + 128, RW * me + RW), block("rsp", me, 128, RW))
+    move(at("rspR", RW, me), "vecB@" + at("f16", 8, me))
+    move(at("itemR", 8, me), at("item", 8, me))
 
     fill("selC", 0.0)
     move("selC:3:35:4", "g9:0:8")
-    tt("oh8:0:8", "oh:0:8", "+", "oh:8:16")
+    keep("idn", "onesB", [[-1, 128]], "==", 0, 1)
+    ts("q4k", "own:0:32", "*", 4096.0, "+", 2048.0)
     cp("v", "a16")
-    ts("lI:64:96", "v", "&", 7)
-    ts("mm", "v", ">>", 3, "&", 15)
-    ts("q16", "own", "*", float(RW - 128))
-    ts("cq", "own", "*", float(RW), "+", 128.0)
-    tt("lI:0:32", "v", "+", "q16")
-    tt("lI:32:64", "cq", "+", "mm")
+    ts("lI:0:32", "v", ">>", 4)
+    ts("lI:32:64", "v", "&", 15)
     cp("l16", "lI")
-    move("m2", "oh8:0:8@l16:64:96")
+    move("m2", "oh:0:16@l16:32:64")
 
-    act("ysb", "rspR@l16:0:32")
-    dma("Y", ext(T.y), "ysb", "d_y", 0.1)
-    tt("cm", "rspR@l16:32:64", "*", "m2")
+    for j, way in enumerate((act, cp)):
+        way(at("ysb", 256, j), "rspR@" + at("a16", 16, j))
+    dma("Y", ext(T.y), "ysb", "d_y0", 0.12)
+    tt("cm", "itemR@l16:0:32", "*", "m2")
     for c in range(4):
-        mms("32|" + at("p7", 32, c), [("selC:%d:%d" % (3 - a, 35 - a), "cm:%d:512:16" % (4 * a + c)) for a in range(4)])
+        mms("32|" + at("p7", 32, c), [("idn:%d:128:4" % c, "q4k")] +
+            [("selC:%d:%d" % (3 - a, 35 - a), "cm:%d:512:16" % (4 * a + c)) for a in range(4)])
     cp("32|ch1", "32|p7:0:128")
     dma("S", ext(T.chosen), "32|ch1", "d_ch", 0.0)
 

from concourse.bass import DstId, RemoteDMATransfer
from concourse.mybir import AluOpType as A_, ActivationFunctionType as AF

N = 8
TRY = 6
RW = 128
BIG = float(1 << 23)
OPS = {"+": A_.add, "-": A_.subtract, "*": A_.mult, "min": A_.min, "max": A_.max, ">=": A_.is_ge, ">": A_.is_gt, "<": A_.is_lt,
       "==": A_.is_equal, ">>": A_.arith_shift_right, "&": A_.bitwise_and}

PLAN = "Tb01 Tf12 Tf41v Tf31 Tn12 Mf00 Sf01 Sf12 Tf51 Sf323 Tn41 Sn01 Tn31 Af00 Tn51 Sn1212 Sn323 An00"
RELAYED = ("ah5", "far")
APART = 6
HERE = 4

SMALL = {
    "bufI": ("int32", 8, "pI 8 p16I 8 sdI 128 hI 8 h64 32 lh 8 ckp 8 ckA 8 rkI 16 oT 32 oB0 64 oA0 64 oA 32 "
             "oW 32 oB16 32 own 64 yI 288 v 32 thrI 256 aliI 256 xl 64 xq 64 hT 384 hb 768 ha 768 oz 128 oy 128 lz 384 ly 384 bz 384 by 768 "
             "xI 384 cI 384 wI 384 d0 384 d1 384 res 384 lI 64"),
    "bufF": ("float32", 8, "ones 128 p16F 8 n16 8 e8a 128 e8 128 g9a 16 g9 16 w2 8 wcol 8 c3 8 wS 8 lhF 8 ckF 8 "
             "ya 8 yc 16 dy 8 dyS 8 st 288 top 288 mine 256 sb 256 least 256 ha2 8 nm 8 nm0 8 item 64 itemR 64 ch1 128"),
    "bufB": ("bfloat16", 16, "onesB 128 ones5 512 lta 128 lt 128 selB 144 selT 144 selP 144 selX 128 ckL 128 "
             "idn 128 q8 16 beR 64 q4k 32 iotaS 128 ohI 512 ohA 512 oh 512 kE 512 inX 512 rs 256 mq 256 sc 256 rs8 256 "
             "alH 256 alL 256 thH 256 thL 256 win 1024 mT 1024 mask 1024 m2 512 ysb 512"),
    "bufH": ("float16", 16, "cm 512 selC 48"),
    "bufU": ("uint16", 16, "a16 32 e16 384 c16 384 f16 64 l16 64"),
}
SCRATCH = {}
TILES = {}
for _buf, (_type, _step, _list) in SMALL.items():
    _at, _w = 0, _list.split()
    for _n, _c in zip(_w[0::2], _w[1::2]):
        TILES[_n] = (_buf, _at, int(_c))
        _at += -(-int(_c) // _step) * _step
    SCRATCH[_buf] = ("sbuf", [128, _at], _type)
for _n, _c, _type in (("seenB", 4096, "bfloat16"), ("vecB", 4096, "bfloat16"), ("tabs", 4096, "bfloat16"),
                      ("tg", 6144, "bfloat16"), ("sg", 6144, "bfloat16"), ("su", 6144, "bfloat16"), ("rspR", N * RW, "bfloat16")):
    SCRATCH[_n] = ("sbuf", [128, _c], _type)
    TILES[_n] = (_n, 0, _c)
for _j in range(8):
    SCRATCH["p%d" % _j] = ("psum", [128, 512], "float32")
    TILES["p%d" % _j] = ("p%d" % _j, 0, 512)
BLOCKS = {"rsp": RW, "rq": 8, "rr": 8, "ah4": 16, "ar4": 16, "ah5": 16, "ar5": 16}
for _n, _c in BLOCKS.items():
    SCRATCH[_n] = ("sbuf", [128, N, _c], "bfloat16" if _n == "rsp" else "int32")
for _n in ("hA", "kp"):
    SCRATCH[_n] = ("sbuf", [128, 2 * TRY, 32], "int32")
SEMAPHORES = ("sv ss sp sg d_sd d_rk d_thr d_ali d_seen0 d_vec d_tab0 d_tab1 d_tab2 d_tab3 d_y0 d_ch "
              "l_be l_rq l_ah4 l_ah5 l_far l_fari l_neari l_near r_be r_rq r_ah4 r_ah5 r_far r_fari r_neari r_near").split()

COSTS = [dict(zip("cycle pe gather scatter pick act pool own other dma MB issue first be rq ah4 ah5 far near fari neari".split(), _row)) for _row in (
    (0.00083, 0.00042, 0.00125, 0.0025, 0.06, 0.22, 0.15, 0.18, 0.27, 1.4, 3.6, 0.5, 1.0, 3.6, 1.8, 2.8, 6.2, 4.7, 1.5, 1.9, 1.2),
    (0.00105, 0.00053, 0.00180, 0.0042, 0.06, 0.31, 0.15, 0.23, 0.32, 1.7, 5.0, 1.0, 2.5, 5.6, 2.7, 4.0, 8.2, 6.4, 2.3, 2.8, 1.8))]
ROUNDS, REACH, SHARE, TURN, GAIN, BAR, BACK, SEED = 20000, 8, 5, 4, 0.2, 50, 2500, 4
KNOWN = []


def routes(core, name, T, topo):
    here = [c for c in T.cores if topo.chip(c) == topo.chip(core)]
    off, on = [c for c in T.cores if c not in here], [c for c in here if c != core]
    pool = topo.engines(core, off[0])
    rest = [e for e in topo.engines(core, on[0]) if e not in pool]
    if name[:4] == "near":
        rest = rest + pool[:len(pool) // 2]
    off, on, via = ([] if name[:4] == "near" else off), ([] if name[:3] == "far" else on), {}
    if name in RELAYED:
        idle = [c for c in topo.cores_of(core) if topo.die(c) != topo.die(core) and c not in T.cores]
        via[off[here.index(core)]] = idle[here.index(core)]
    plan = {}
    for cores, engines in (([c for c in off if c not in via], pool), (on + list(via), rest)):
        n = 1
        while 2 * n * len(cores) <= len(engines) and cores:
            n *= 2
        at = 0
        for j, c in enumerate(cores):
            m = n
            if len(engines) - at - 2 * n >= n * (len(cores) - j - 1):
                m = 2 * n
            plan[c] = via.get(c, c), engines[at:at + m], len(topo.engines(via[c], c)) if c in via else m
            at += m
    return {c: plan[c] for c in off + on}


def transfer(to, engines, name, src, dst, T, topo):
    rid, pnc, _s = topo.addr(to)
    return RemoteDMATransfer(dst_ids=[DstId(rid=rid, pnc=pnc)], dma_engine_mask=sum(1 << e for e in engines),
                             remote_sem=T.sem["r_" + name], srcs=[src], dsts=[dst], alu_op=0)


def relay_program(g, core, T, topo):
    for name in RELAYED:
        for c in T.cores:
            for to, (via, engines, n) in routes(c, name, T, topo).items():
                if via == core:
                    r = T.rank_of(c)
                    piece = T.ar5[:, r, :] if name == "ah5" else T.rspR[:, RW * r:RW * r + RW]
                    g.wait_ge(T.sem["r_" + name], len(engines))
                    g.remote_dma_fused([transfer(to, topo.engines(core, to), name, piece, piece, T, topo)], local_sem=T.sem["l_" + name])
                    g.wait_ge(T.sem["l_" + name], n)


def arrange(calls):
    n = len(calls)
    qs = [None] * n
    above, near = [], []
    for c in calls:
        bits, keep = 0, set()
        for a in sorted({a["n"] for a in c["after"] + c["behind"]}, reverse=True):
            if not bits >> a & 1 or calls[a]["late"]:
                keep.add(a)
            bits |= above[a] | 1 << a
        above.append(bits)
        near.append(keep)
    for order, way, _end in KNOWN:
        at = {i: j for j, i in enumerate(order)}
        if len(order) == n and all(at[a] < at[i] for i in range(n) for a in near[i]):
            return [(calls[i], way[i]) for i in order]
    edges = [[n + a["n"] for a in c["after"] if a["n"] in near[c["n"]]] + [a["n"] for a in c["behind"]] for c in calls]
    way, sets = [0] * n, [([0.0] * n, [0.0] * (3 * n)) for _ in COSTS]
    users = [[] for _ in calls]
    for i in range(n):
        for a in edges[i]:
            users[a % n].append((i, a))

    def take(i, w):
        way[i], qs[i] = w, calls[i]["ways"][w][0]
        for cost, (time, full) in zip(COSTS, sets):
            time[i] = sum(cost[k] * v for k, v in calls[i]["ways"][w][2].items()) + 1e-6
            late = sum(cost[k] * v for k, v in calls[i]["late"].items())
            full[n + i] = time[i] + (late or (cost["other"] if qs[i] else 0.0))
            full[2 * n + i] = time[i] + (late or (cost["own"] if qs[i] else 0.0))
        for j in [i] + [a % n for a in edges[i]] + [u for u, _a in users[i]]:
            edges[j] = [a if a < n else a % n + (2 * n if qs[a % n] == qs[j] else n) for a in edges[j]]
            users[j] = [(u, a if a < n else j + (2 * n if qs[u] == qs[j] else n)) for u, a in users[j]]

    def turn(i):
        for c in calls[i:i + 2]:
            if c["n"] == i or c["lead"] is calls[i]:
                take(c["n"], 1 - way[c["n"]])

    def heads(order, time, full):
        free, at, can = dict.fromkeys("VSPGY", 0.0), [0.0] * (3 * n), [0.0] * n
        for i in order:
            t = 0.0
            for a in edges[i]:
                if at[a] > t:
                    t = at[a]
            can[i] = t
            q = qs[i]
            if q:
                if free[q] > t:
                    t = free[q]
                free[q] = t + time[i]
            at[i] = t
            at[n + i] = t + full[n + i]
            at[2 * n + i] = t + full[2 * n + i]
        return at, can

    def tails(order, time, full):
        rest, left, own = dict.fromkeys("VSPGY", 0.0), [0.0] * n, [0.0] * n
        for i in reversed(order):
            t = full[n + i]
            for u, a in users[i]:
                if left[u] + full[a] > t:
                    t = left[u] + full[a]
            own[i] = t
            q = qs[i]
            if q:
                if rest[q] + time[i] > t:
                    t = rest[q] + time[i]
                rest[q] = t
            left[i] = t
        return left, own

    def guess(row, a, b, seq):
        total = 0.0
        for (at, can, left, own, time, full), end in zip(state, ends):
            t = at[row[a - 1]] + time[row[a - 1]] if a else 0.0
            new = []
            for i in seq:
                if can[i] > t:
                    t = can[i]
                new.append(t)
                t += time[i]
            t, worst = left[row[b]] if b < len(row) else 0.0, end - GAIN
            for i, h in zip(reversed(seq), reversed(new)):
                t += time[i]
                if own[i] > t:
                    t = own[i]
                if h + t > worst:
                    worst = h + t
            total += worst
        return total

    for i in range(n):
        take(i, calls[i].get("first", 0))
    time, full = sets[0]
    busy, start = {}, [0.0] * n
    for i in range(n):
        t = max([start[a % n] + (full[a] or 1e-6) for a in edges[i]] + [0.0])
        if qs[i]:
            for a, b in busy.setdefault(qs[i], []):
                if t + time[i] <= a:
                    break
                t = max(t, b)
            busy[qs[i]] = sorted(busy[qs[i]] + [(t, t + time[i])])
        start[i] = t
    order = sorted(range(n), key=lambda i: (start[i], i))
    best, x, barred, since = None, SEED, {}, 0
    for r in range(ROUNDS):
        state = [heads(order, *s) for s in sets]
        at0 = state[0][0]
        order.sort(key=lambda i: at0[i])
        ends = [max(at) for at, _can in state]
        if best is None or sum(ends) < best[2] * len(sets) - 1e-9:
            best, since = (list(order), list(way), sum(ends) / len(sets)), r
        elif r - since > BACK:
            order, since, barred = list(best[0]), r, {}
            for i in range(n):
                take(i, best[1][i])
            continue
        state = [h + tails(order, *s) + s for h, s in zip(state, sets)]
        rows = {q: [i for i in order if qs[i] == q] for q in "VSPG"}
        x = (x * 6364136223846793005 + 1442695040888963407) % (1 << 64)
        at, can, left = state[(x >> 40) % len(sets)][:3]
        end, moves = ends[(x >> 40) % len(sets)], []
        for row in rows.values():
            for j, i in enumerate(row):
                if j and at[i] + left[i] > end - 1e-6 and can[i] < at[i] - 1e-6:
                    x = (x * 6364136223846793005 + 1442695040888963407) % (1 << 64)
                    if (x >> 40) % 100 >= SHARE:
                        continue
                    first = max([at0[a % n] for a in edges[i]] + [-1.0])
                    for k in range(j - 1, max(-1, j - 1 - REACH), -1):
                        if at0[row[k]] <= first:
                            break
                        moves.append((guess(row, k, j + 1, [i] + row[k:j]) + (barred.get((i, row[k]), 0) > r) * 99 +
                                      (x >> k % 30 & 255) * 1e-6, i, row[k], 0))
                    u = row[j - 1]
                    last = min([at0[o] for o, _after in users[u]] + [1e9])
                    for k in range(j, min(len(row), j + REACH)):
                        if at0[row[k]] >= last:
                            break
                        moves.append((guess(row, j - 1, k + 1, row[j:k + 1] + [u]) + (barred.get((row[k], u), 0) > r) * 99 +
                                      (x >> k % 30 & 255) * 1e-6, u, row[k], 1))
                    for o in (i, u):
                        o = calls[o]["lead"]["n"] if calls[o]["lead"] else o
                        if len(calls[o]["ways"]) > 1 and barred.get(o, 0) <= r and not (x >> 20) % TURN:
                            turn(o)
                            moves.append((sum(max(heads(order, *s)[0]) for s in sets), o, o, 2))
                            turn(o)
        if moves:
            _end, i, o, kind = min(moves)
            if kind == 2:
                turn(i)
                barred[i] = r + 3 * BAR
                continue
            row = rows[qs[i]]
            for p in (row[row.index(o):row.index(i)] if kind == 0 else row[row.index(i) + 1:row.index(o) + 1]):
                barred[(p, i) if kind == 0 else (i, p)] = r + BAR + (x >> 30) % BAR
            order.remove(i)
            order.insert(order.index(o) + kind, i)
    KNOWN.append(best)
    return [(calls[i], best[1][i]) for i in best[0]]


def rank_program(g, core, T, topo):
    me = T.rank_of(core)
    if me is None:
        relay_program(g, core, T, topo)
        return
    queues = {"V": (g.vector, "sv"), "S": (g.scalar, "ss"), "P": (g.tensor, "sp"), "G": (g, "sg"), "Y": (g.sync, None)}
    V, S, P = g.vector, g.scalar, g.tensor
    calls, past, named = [], {}, {}

    def X(spec):
        if not isinstance(spec, str):
            return spec
        if "@" in spec:
            w, o = spec.split("@")
            (wa, wr), (oa, orr) = X(w), X(o)
            return wa.indirect(oa), wr + orr
        rows, name = (int(spec.split("|")[0]), spec.split("|")[1]) if "|" in spec else (128, spec)
        f = name.split(":")
        buf, at, n = TILES[f[0]]
        a, b, st = (int(f[1]), int(f[2]), int(f[3]) if len(f) > 3 else 1) if len(f) > 1 else (0, n, 1)
        return T[buf][0:rows, at + a:at + b:st], [(buf, at + a, at + b, st)]

    def width(places):
        return sum(len(range(*p[1:])) for p in places)

    def meet(p, o, own):
        if p[0][0] == "p" and not own:
            return True
        if p[1] >= o[2] or o[1] >= p[2]:
            return False
        return (p[3] == 1 and o[3] == 1) or bool(set(range(p[1], p[2], p[3])) & set(range(o[1], o[2], o[3])))

    def add(q, emit, reads, writes, time, late=None, sem=None, inc=1, part=None, after=(), behind=(), ways=None, lead=None):
        c = {"n": len(calls), "q": q, "ways": ways or [(q, emit, time)], "late": late or {}, "sem": sem, "inc": inc,
             "behind": list(behind), "lead": lead}
        dep = {a["n"]: a for a in after}
        for places, wr in ((reads, False), (writes, True)):
            for p in places:
                for o, a, is_w, pt in past.get(p[0], []):
                    if (is_w or wr or (p[0][0] == "p" and a["q"] != q)) and a["n"] not in dep \
                            and meet(p, o, a["q"] == q) and (pt is None or part is None or pt == part):
                        dep[a["n"]] = a
        c["after"] = list(dep.values())
        for places, w in ((reads, False), (writes, True)):
            for p in places:
                past.setdefault(p[0], []).append((p, c, w, part))
        calls.append(c)
        return c

    def run(q, call, out, ins, *more, rate=1.0, time=None):
        oa, ow = X(out)
        reads, args, n = [], [], width(ow)
        for i in ins:
            if isinstance(i, (str, tuple)):
                a, r = X(i)
                args.append(a)
                reads = reads + r
            else:
                args.append(i)
        if isinstance(out, str) and "@" in out:
            n, rate, reads, ow = 16 * width(ow[1:]), "scatter", reads + ow[1:], ow[:1]
        elif ins and isinstance(ins[0], str) and "@" in ins[0]:
            rate = "gather"
        elif rate == 0.5 and not all(SCRATCH[p[0]][2] in ("bfloat16", "uint16") for p in ow + X(ins[0] if ins else out)[1]):
            rate = 1.0
        if time is None:
            time = {rate: n, "pick": 1} if isinstance(rate, str) else \
                {"V": {"cycle": max(64, n * rate)}, "S": {"cycle": n, "act": 1}, "G": {"cycle": 2 * n, "pool": 1}}[q]
        if offers:
            offers.append((q, lambda: call(oa, *args, *more), time, reads, ow))
            return None
        return add(q, lambda: call(oa, *args, *more), reads, ow, time)

    offers = []

    def either(*two, lead=None):
        offers.append(None)
        for c in two:
            if c:
                c[0](*c[1:])
            else:
                offers.append((None, None, {}, [], []))
        ways = offers[1:]
        del offers[:]
        return add("?%d" % len(calls), None, sum((w[3] for w in ways), []), sum((w[4] for w in ways), []), None,
                   ways=[w[:3] for w in ways], lead=lead)

    def ts(out, a, op, s1, op2=None, s2=None):
        run("V", V.tensor_scalar, out, [a, s1, s2], *([OPS[op]] if op2 is None else [OPS[op], OPS[op2]]), rate=0.5)

    def tt(out, a, op, b):
        run("V", V.tensor_tensor, out, [a, b], OPS[op], rate=1.0 if "p" in (X(a)[1][0][0][0], X(b)[1][0][0][0]) else 2.0)

    def cp(out, a):
        run("V", V.tensor_copy, out, [a], rate=0.5)

    def fill(out, c):
        run("V", V.memset, out, [], c, rate=0.5)

    def scan(out, a, b, op0=A_.mult, op1=A_.add, first=0.0):
        run("V", V.tensor_tensor_scan, out, [a, b], first, op0, op1, rate=0.5)

    def half(name, w, i, j):
        return "%s:%d:%d:2" % (name, w * i + j, w * i + w)

    def square(out, z, y, a, *ops):
        ts(half(*z, 1), a, *ops)
        ts(half(*y, 0), a, *ops)
        scan(at(*out), at(*z), at(*y))

    def act(out, a, bias=0.0, scale=1.0, func=AF.Copy):
        run("S", lambda o, i: S.activation(o, i, func, bias=bias, scale=scale), out, [a])

    def times(out, a, by):
        run("S", lambda o, i, c: S.activation(o, i, AF.Copy, scale=c), out, [a, by])

    def scaled(out, a, by):
        either((times, out, a, by), (ts, out, a, "*", by))

    def move(out, a):
        either((act, out, a), (cp, out, a))

    def away(out, a, by):
        run("S", lambda o, i, b: S.activation(o, i, AF.Abs, bias=b), out, [a, by])

    def iota(out, pattern, base, cm, exact=False):
        run("G", lambda o: g.iota(o, pattern, base, cm) if exact else
            g.iota(o, pattern, base, cm, allow_small_or_imprecise_dtypes=True), out, [])

    def keep(out, a, pattern, op, base, cm):
        run("G", lambda o, i: g.affine_select(o, i, pattern, OPS[op], 0.0, base, cm), out, [a])

    def mms(out, pairs, four=False, stop=True, begun=None):
        def call(o, *args):
            for j in range(0, len(args), 2):
                last = P.matmul(o, args[j], args[j + 1], j == 0 and not begun, j == len(args) - 2 and stop)
            return last
        n = sum(max(min(64, width(X(a)[1])), width(X(b)[1])) for a, b in pairs)
        c = run("P", call, out, [x for p in pairs for x in p], time={"pe": n * (4 if four else 1), "pick": 1})
        if begun:
            c["after"].remove(begun)
            c["behind"].append(begun)
        return c

    def dma(q, out, in_, sem, mb, part=None, after=()):
        (oa, ow), (ia, ir) = X(out), X(in_)
        last = named.get(q)
        named[q] = add(q, lambda: queues[q][0].dma_start(oa, ia), ir, ow, {"pick": 1}, {"dma": 1, "MB": mb}, sem, 16, part, after,
                       [last] if last else [])

    off, on = list(routes(core, "far", T, topo)), list(routes(core, "near", T, topo))

    def send(name, src, dst):
        plan = routes(core, name, T, topo)
        tr = [transfer(via, engines, name, X(src(T.rank_of(c)))[0], X(dst(me))[0], T, topo) for c, (via, engines, _n) in plan.items()]

        def emit():
            g.remote_dma_fused(tr, local_sem=T.sem["l_" + name])
        named[name] = add("G", emit, [p for c in plan for p in X(src(T.rank_of(c)))[1]], [], {"issue": 1, "first": name == "be"},
                          {name: 1}, "l_" + name, sum(len(engines) for _via, engines, _n in plan.values()),
                          behind=[named[name + "i"]] if name + "i" in named else [])
        add(None, None, [], [p for c in plan for p in X(dst(T.rank_of(c)))[1]], {}, {"issue": 1, name: 1},
            "r_" + name, sum(routes(c, name, T, topo)[core][2] for c in plan), behind=[named[name]])

    def block(name, r, a=0, b=None):
        w = BLOCKS[name]
        b = w if b is None else b
        return T[name][:, r, a:b], [(name, w * r + a, w * r + b, 1)]

    def parts(name, a, b):
        w = BLOCKS[name]
        return T[name][:, :, a:b], [(name, w * r + a, w * r + b, 1) for r in range(N)]

    def ext(t):
        return (t[:], [])

    def at(name, w, i):
        return "%s:%d:%d" % (name, w * i, w * i + w)

    dma("Y", "sdI:0:1", ext(T.sd), "d_sd", 0.03)
    dma("S", "8|rkI", ext(T.rk), "d_rk", 0.0)
    dma("Y", "thrI", ext(T.thr), "d_thr", 0.15)
    dma("Y", "aliI", ext(T.ali), "d_ali", 0.3)
    dma("Y", "seenB", ext(T.seen), "d_seen0", 1.3)

    step = 1597 * (TRY + 1)
    for name, c in (("ones", 1.0), ("sdI:4:128", step), ("h64", 0), ("oz:0:128:2", 0), ("win", 0.0), ("onesB", 1.0),
                    ("ones5", 1.0), ("yc", 0.0), ("top", BIG), ("st:0:288:9", BIG), ("st:8:288:9", 4.0)):
        fill(name, c)
    for name, n in (("lz:0:384:2", 192), ("bz:0:384:2", 192), ("d0:0:384:6", 64)):
        either((iota, name, [[0, n]], 0, 0, True), (fill, name, 0))
    iota("pI:0:1", [[0, 1]], 0, 1, True)
    keep("8|e8a", "8|ones", [[1, 128]], ">=", 0, -16)
    keep("8|e8", "8|e8a", [[-1, 128]], ">=", 15, 16)
    keep("g9a:0:9", "ones:0:9", [[-16, 9]], ">=", 0, 1)
    keep("g9:0:9", "g9a:0:9", [[16, 9]], ">=", 15, -1)
    iota("ohI", [[0, 32], [1, 16]], 0, 0)
    iota("ckp:0:1", [[0, 1]], 1597, step, True)
    keep("lta", "onesB", [[16, 8], [1, 16]], ">", 0, -1)
    keep("lt", "lta", [[-16, 8], [0, 16]], ">=", 0, 1)
    keep("kE", "ones5", [[1, 32], [0, 16]], "==", 0, -1)

    scan("oT", "ones:0:32", "sdI:0:128:4", first=-BIG)
    ts("h64:0:1", "sdI:0:1", ">>", 6, "&", 4095 << 6)
    scan("oy:1:64:2", "ones:0:32", "h64")
    square(("oB0", 64, 0), ("oz", 64, 0), ("oy", 64, 0), "oT", "&", 4095)
    ts("oy:65:128:2", "oy:0:64:2", "*", 64.0)
    square(("oA0", 64, 0), ("oz", 64, 1), ("oy", 64, 1), "oB0:1:64:2", ">>", 6, "&", 4095)
    ts("oW", "oA0:1:64:2", ">>", 15, "&", 7)
    ts("8|ya", "8|rkI:0:8", "*", 16.0)
    tt("8|yc:1:9", "8|ya", "+", "8|rkI:8:16")
    tt("8|dy", "8|yc:1:9", "-", "8|yc:0:8")
    mms("p3:0:8", [("8|e8", "8|dy")], True)
    move("dyS", "p3:0:8")
    scaled("top:0:288:9", "ones:0:32", "dyS:0:1")
    for w in range(1, N):
        ts("st:%d:288:9" % w, "oW", ">=", float(w), "*", at("dyS", 1, w))
    ts("oB16", "oy:64:128:2", "*", 16.0, "+", 8.0)
    tt("top:7:288:9", "oB16", "+", "oW")
    scan("yI", "st", "top", A_.add, A_.min)
    ts("own:0:32", "yI:7:288:9", "&", 7)
    ts("own:32:64", "yI:8:288:9", "&", 7)

    for q in range(N // 2):
        ts(at("mq", 64, q), "own", "==", float(q), "*", -1.0)
    for q in range(N // 2):
        ts(at("p0", 64, q), "own", "==", float(q), "*", -4096.0)
    fill("rs", 1.0)
    fill("rs:0:256:32", 0.0)
    scan("sc", "rs", "mq")
    def counts(q):
        return "sc:%d:%d" % (64 * (q % 4) + 32 * (q // 4) + 24, 64 * (q % 4) + 32 * (q // 4) + 32)
    send("be", counts, lambda r: at("beR", 8, r))
    iota("q8:0:8", [[-1, 4], [-4, 2]], 0, 0)
    mms("p2:0:8", [("onesB", "q8:0:8"), ("lt", "sc:31:256:32")])
    tt("mine", "p0:0:256", "+", "sc")
    for q in range(N):
        ts("sb:%d:256:8" % q, at("mine", 32, q), "+", at("p2", 1, q))
    fill("rs8", 1.0)
    fill("rs8:0:256:8", 0.0)
    scan("least", "rs8", "sb", A_.mult, A_.min)
    ts("a16", "least:7:256:8", "*", -1.0, "-", 4097.0)

    ts("p16I:0:1", "pI:0:1", "&", 15)
    cp("p16F:0:1", "p16I:0:1")
    ts("n16:0:1", "p16F:0:1", "*", -1.0)
    either((act, "oh", "ohA", 1.0, -1.0, AF.Relu), None,
           lead=either((away, "ohA", "ohI", "n16:0:1"), (ts, "oh", "ohI", "==", "p16F:0:1")))
    for name in ("selX", "ckL", "selB"):
        fill(name, 0.0)
    ts("lh:0:1", "sdI:0:1", "&", 3840)
    ts("lh:1:2", "sdI:0:1", "&", 255)
    ts("lh:2:3", "sdI:0:1", ">>", 12, "&", 255)
    ts("hI:0:1", "sdI:0:1", ">>", 12)
    ts("hI:1:2", "hI:0:1", "+", 2048.0)
    ts("lh:3:4", "hI:1:2", "&", 3840)
    cp("lhF:0:3", "lh:0:3")
    ts("lhF:3:4", "lh:3:4", "+", -2048.0)
    for j, c in ((0, "lhF:0:1"), (1, "lhF:1:2"), (4, "lhF:3:4"), (5, "lhF:2:3")):
        scaled("selX:%d:128:16" % j, "g9:0:8", c)
    ts("ckA:0:1", "ckp:0:1", "&", 3840)
    ts("ckA:1:2", "ckp:0:1", "&", 255)
    cp("ckF:0:2", "ckA:0:2")
    ts("ckL:2:128:16", "onesB:0:8", "*", "ckF:0:1")
    ts("ckL:3:128:16", "onesB:0:8", "*", "ckF:1:2")
    mms("p7", [("selX", "oh"), ("ckL", "kE")])
    move("inX", "p7")
    cp("win@a16", "inX")
    move("selB:15:144:16", "g9:0:9")
    ts("c3:0:1", "p16F:0:1", ">=", 4.0, "*", 8192.0)
    ts("wS:0:1", "c3:0:1", "max", 1.0)
    scaled("selP", "selB", "wS:0:1")
    mms("p4:0:64", [("selP:%d:%d" % (15 - b, 143 - b), "win:%d:1024:16" % b) for b in range(16)])
    cp(parts("rq", 0, 8), "p4:0:64")
    send("rq", lambda q: block("rq", q), lambda r: block("rr", r))
    cp(block("rr", me), block("rq", me))
    move(at("beR", 8, me), counts(me))

    cp("p5:0:256", "aliI")
    either((act, "alH", "p5:0:256", -8.0, 1.0, AF.Relu), (ts, "alH", "p5:0:256", "-", 8.0, "max", 0.0))
    ts("p6:0:256", "thrI", "+", -2048.0)
    either((act, "thH", "p6:0:256", -4.0), (ts, "thH", "p6:0:256", "-", 4.0))
    tt("alL", "p5:0:256", "-", "alH")
    tt("thL", "p6:0:256", "-", "thH")
    for j in range(8):
        either((act, at("tabs", 512, j), "ones5"), (fill, at("tabs", 512, j), 0.0) if j % 2 else (iota, at("tabs", 512, j), [[0, 512]], 0, 0))
    for j, name in ((1, "alH"), (3, "thH"), (0, "alL"), (2, "thL")):
        dma("Y", (T.tabs[4 * j:128:16, :], X("tabs")[1]), name, "d_tab%d" % j, 0.3, j)
    ts("p16I:1:2", "pI:0:1", "&", 3)
    ts("w2:0:1", "p16F:0:1", ">=", 8.0, "*", 8191.0)
    ts("w2:1:2", "w2:0:1", "+", 1.0)
    ts("wcol:0:1", "p16I:1:2", "==", 0.0, "*", "w2:1:2")
    scaled("selT", "selB", "wcol:0:1")

    near = me // 4
    far = 1 - near
    order = [T.rank_of(c) for c in off + on] + [me]

    def masks(ranks):
        for r in ranks:
            away(at("mT", 128, r), "iotaS", at("nm", 1, r))
            ts(at("mask", 128, r), at("mT", 128, r), "<", at("ha2", 1, r), "*", -float(2 ** (15 - r)))

    def span(h, i, n=1):
        if i >= APART:
            return 2 * APART + (TRY - APART) * h + i - APART, n
        return (APART - 1, 2) if h == 2 else (APART - i - n if h == 0 else APART + i, n)

    def R(name, s, w=32):
        return "%s:%d:%d" % (name, w * s[0], w * (s[0] + s[1]))

    def units(name, a, b, step=1):
        return T[name][:, a:b:step, :], [(name, 32 * j, 32 * j + 32, 1) for j in range(a, b, step)]

    def both(name, i):
        return units(name, APART - 1 - i, APART + 1 + i, 2 * i + 1) if i < APART else units(name, 2 * i, 2 * i + 2)

    def ahead(name, i, j, h=2):
        name, lo, hi = name + str(i), 4 * (h % 2), 4 * min(h, 1) + 4
        return T[name][:, lo:hi, 8 * j:8 * j + 8], parts(name, 8 * j, 8 * j + 8)[1][lo:hi]

    def hashes(i):
        x, low = (parts("rr", 0, 8), "xl") if i < HERE else (parts("rq", 0, 8), "xq")
        a, k = (both("hA", i), both("kp", i)) if i < HERE else (ahead("ah", i, 0), ahead("ah", i, 1))
        if i:
            ts(at("hT", 64, i), low, "+", float(1597 * i % 4096))
        if i < 3 or i >= HERE:
            ts(half("ly", 128, i % 3, 1), x, ">>", 7, "&", 4095 << 6)
        square(("hb", 128, i), ("lz", 128, i % 3), ("ly", 128, i % 3), at("hT", 64, i) if i else x, "&", 4095)
        ts(half("by", 128, i, 1), at("hT", 64, i) if i else half("ly", 128, 0, 0), "*", 64.0)
        square(("ha", 128, i), ("bz", 128, i % 3), ("by", 128, i), half("hb", 128, i, 1), ">>", 6, "&", 4095)
        ts(a, half("ha", 128, i, 1), ">>", 6, "&", 4095)
        ts(at("p0", 64, i), half("by", 128, i, 0), "*", 8192.0, "+", 4096.0 - 16777216.0)
        tt(k, at("p0", 64, i), "+", a)

    def wrap(bank, sel, src, s):
        a, b = 512 * s[0], 512 * (s[0] + s[1])
        mms(R(bank, (0, s[1])), [("%s:%d:%d" % (sel, 15 - j, 143 - j), "%s:%d:%d:16" % (src, a + j, b)) for j in range(16)])

    def candidates(h, i, n, bank):
        s = span(h, i, n)
        cp(R("e16", s), units("hA", s[0], s[0] + s[1]) if i < HERE else ahead("ar", i, 0, h))
        move(R("tg", s, 512), "tabs@" + R("e16", s))
        wrap(bank, "selT", "tg", s)
        tt(R("xI", s), R(bank, (0, s[1])), "min", units("kp", s[0], s[0] + s[1]) if i < HERE else ahead("ar", i, 1, h))
        ts(R("cI", s), R("xI", s), "&", 4095)
        if i < TRY - 1:
            cp(R("c16", s), R("cI", s))

    def sixth(name, h, i):
        return "%s:%d:%d:6" % (name, 192 * (h % 2) + TRY - 1 - i, 192 * min(h, 1) + 192)

    def unseen(h, i, n, bank):
        for j, k in [(j, h) for j in range(i, i + n)] if h < 2 else [(i, far), (i, near)]:
            s = span(k, j)
            either(None, (scan, R("sg", s, 512), R("su", s, 512), at("mask", 512, k), A_.max, A_.mult),
                   lead=either((tt, R("sg", s, 512), "seenB@" + R("c16", s), "*", at("mask", 512, k)),
                               (act, R("su", s, 512), "seenB@" + R("c16", s))))
        s = span(h, i, n)
        wrap(bank, "selB", "sg", s)
        ts(R("wI", s), R(bank, (0, s[1])), "*", -1.0)
        for j in range(i, i + n):
            ts(sixth("d0", h, j), R("wI", span(h, j)), ">>", 15, "&", 1)

    def answer(h, name, cores):
        def H(tile):
            return at(tile, 32, h)
        if h == far:
            cp(sixth("d1", 2, 0), R("cI", span(2, 0)))
        for i in range(1, TRY):
            tt(sixth("d1", h, i), R("cI", span(h, i)), "-", R("cI", span(h, i - 1)))
        scan(at("res", 192, h), at("d0", 192, h), at("d1", 192, h))
        cp(H("f16"), sixth("res", h, 0))
        ts(H("item"), sixth("res", h, 0), "-", 2048.0)
        for c in cores:
            move(block("rsp", T.rank_of(c)), "vecB@" + at("f16", 8, T.rank_of(c)))
        send(name + "i", lambda q: at("item", 8, q), lambda r: at("itemR", 8, r))
        send(name, lambda q: block("rsp", q), lambda r: at("rspR", RW, r))

    ts("xq", parts("rq", 0, 8), "&", 8191)
    for i in range(HERE, TRY):
        hashes(i)
        send("ah%d" % i, lambda q: block("ah%d" % i, q), lambda r: block("ar%d" % i, r))
        cp(block("ar%d" % i, me), block("ah%d" % i, me))
    dma("Y", "vecB", ext(T.vec), "d_vec", 1.0, after=[named["ah4"], named["ah5"]])
    ts("xl", parts("rr", 0, 8), "&", 8191)
    for i in range(HERE):
        hashes(i)
    iota("iotaS", [[1, 128]], 0, 0)
    mms("p3:0:8", [("lt", "beR:7:64:8")])
    ts("nm0", "beR:7:64:8", "*", 0.5, "+", 0.5)
    ts("ha2", "beR:7:64:8", "*", -0.5, "+", -0.25)
    tt("nm", "p3:0:8", "+", "nm0")
    masks(order[:4])
    banks = {"T": ["p2", "p5", "p6"], "S": ["p3", "p4", "p1"]}
    for s in PLAN.split():
        h, i, n = {"f": far, "n": near, "b": 2}[s[1]], int(s[2]), int(s[3])
        if s[0] == "T":
            candidates(h, i, n, banks["T"][0])
            [c for c in calls if len(c["ways"]) > 1][-1]["first"] = len(s) - 4
            banks["T"].append(banks["T"].pop(0))
        elif s[0] == "S":
            unseen(h, i, n, banks["S"][0])
            for j, c in enumerate([c for c in calls if len(c["ways"]) > 1][-2 * n:]):
                c["first"] = int(str(i + j // 2) in s[4:])
            banks["S"].append(banks["S"].pop(0))
        elif s[0] == "A":
            answer(h, "far" if h == far else "near", off if h == far else on)
        else:
            masks(order[4:])
    move(at("rspR", RW, me), "vecB@" + at("f16", 8, me))
    move(at("itemR", 8, me), at("item", 8, me))

    fill("selC", 0.0)
    move("selC:3:35:4", "g9:0:8")
    keep("idn", "onesB", [[-1, 128]], "==", 0, 1)
    ts("q4k", "own:0:32", "*", 4096.0, "+", 2048.0)
    cp("v", "a16")
    ts("lI:0:32", "v", ">>", 4)
    ts("lI:32:64", "v", "&", 15)
    cp("l16", "lI")
    move("m2", "oh:0:16@l16:32:64")

    for j, way in enumerate((act, cp)):
        way(at("ysb", 256, j), "rspR@" + at("a16", 16, j))
    dma("Y", ext(T.y), "ysb", "d_y0", 0.12)
    tt("cm", "itemR@l16:0:32", "*", "m2")
    for c in range(4):
        mms("32|" + at("p7", 32, c), [("idn:%d:128:4" % c, "q4k")] +
            [("selC:%d:%d" % (3 - a, 35 - a), "cm:%d:512:16" % (4 * a + c)) for a in range(4)])
    cp("32|ch1", "32|p7:0:128")
    dma("S", ext(T.chosen), "32|ch1", "d_ch", 0.0)

    count, waited = {}, {q: {} for q in queues}
    for c, way in arrange(calls):
        q, emit = c["ways"][way][:2]
        if q is not None:
            c["sem"] = c["sem"] or queues[q][1]
            need = {}
            for a in c["after"]:
                if a["sem"]:
                    need[a["sem"]] = max(need.get(a["sem"], 0), a["count"])
            for s in sorted(need):
                if waited[q].get(s, 0) < need[s]:
                    queues[q][0].wait_ge(T.sem[s], need[s])
                    waited[q][s] = need[s]
            done = emit()
            if done is not None:
                done.then_inc(T.sem[c["sem"]], c["inc"])
        c["count"] = count[c["sem"]] = count.get(c["sem"], 0) + c["inc"]
    for s in SEMAPHORES:
        if count.get(s, 0) > waited["G"].get(s, 0):
            g.wait_ge(T.sem[s], count[s])
